import numpy as np
import ml_dtypes


def mxq(x, axis, fmt="e4m3"):
    dtype, down = {"e4m3": (ml_dtypes.float8_e4m3fn, 7), "e5m2": (ml_dtypes.float8_e5m2, 14)}[fmt]
    v = np.moveaxis(np.asarray(x, np.float32).astype(ml_dtypes.bfloat16).astype(np.float64), axis, -1)
    blocks = v.reshape(v.shape[:-1] + (-1, 32))
    amax = np.abs(blocks).max(-1, keepdims=True)
    byte = np.maximum(np.where(amax > 0, np.frexp(amax)[1] - 1 + 127, 0) - down, 1)
    scale = np.exp2(byte - 127.0)
    codes = (blocks / scale).astype(np.float32).astype(dtype).astype(np.float64)
    return np.moveaxis((codes * scale).reshape(v.shape), -1, axis)


WIDE = False


def mx_kscale(k):
    if not WIDE:
        return np.ones(k)
    levels = np.array([10, -10, 5, -5, 0])
    if k % 512:
        return np.exp2(np.random.permutation(np.resize(levels, k // 32))).repeat(32)
    a = np.empty((k // 512, 16))
    for p in range(k // 512):
        a[p, :8] = np.random.permutation(np.resize(levels, 8))
        for g in range(8):
            far = levels[np.abs(levels - a[p, g]) >= 10]
            a[p, g + 8] = far[np.random.randint(len(far))]
    return np.exp2(a.ravel()).repeat(32)


BF16 = ml_dtypes.bfloat16


def bf(x):
    return np.asarray(x, np.float32).astype(BF16)


def f64(x):
    return np.asarray(x).astype(np.float64)


E2M1 = np.array([0.0, 0.5, 1.0, 1.5, 2.0, 3.0, 4.0, 6.0, -0.0, -0.5, -1.0, -1.5, -2.0, -3.0, -4.0, -6.0])


def pack_weight(w, fmt):
    k, n = w.shape
    w = f64(bf(w)).reshape(k // 32, 32, n)
    amax = np.abs(w).max(1)
    if fmt == "e4m3":
        byte = np.frexp(amax)[1] - 1 + 127 - 7
    else:
        mant, ex = np.frexp(amax / 6.0)
        byte = np.where(mant > 0.5, ex, ex - 1) + 127
    byte = np.clip(np.where(amax > 0, byte, 1), 1, 254)
    scaled = (w * np.exp2(127.0 - byte)[:, None, :]).reshape(k, n).astype(np.float32)
    by_word = np.ascontiguousarray(scaled.reshape(k // 512, 128, 4, n).transpose(0, 1, 3, 2))
    if fmt == "e4m3":
        words = by_word.astype(ml_dtypes.float8_e4m3fn).view(np.uint8)
    else:
        c = by_word.astype(ml_dtypes.float4_e2m1fn).view(np.uint8) & 0xF
        words = c[..., 0::2] | (c[..., 1::2] << 4)
    return np.ascontiguousarray(words), np.ascontiguousarray(byte.astype(np.uint8).reshape(k // 512, 16, n))


def unpack_weight(words, scales, fmt):
    g, p, n, _ = words.shape
    if fmt == "e4m3":
        vals = np.ascontiguousarray(words).view(ml_dtypes.float8_e4m3fn).astype(np.float64)
    else:
        nib = np.empty((g, p, n, 4), np.uint8)
        nib[..., 0::2] = words & 0xF
        nib[..., 1::2] = words >> 4
        vals = E2M1[nib]
    vals = vals * np.repeat(np.exp2(scales.astype(np.float64) - 127.0), 8, axis=1)[..., None]
    return vals.transpose(0, 1, 3, 2).reshape(g * 512, n)
def pack4(w):
    words, scales = pack_weight(w, "e2m1")
    return words.reshape(words.shape[0], 128, -1), scales


def unpack4(words, scales):
    return unpack_weight(words.reshape(words.shape[0], 128, -1, 2), scales, "e2m1")


E4M3FN = np.array([(-1.0 if i & 128 else 1.0) * ((1.0 + (i & 7) / 8.0) * 2.0 ** (((i >> 3) & 15) - 7) if i & 120 else (i & 7) * 2.0 ** -9) for i in range(256)])


def e4m3fn_bytes(y):
    return np.clip(np.asarray(y, np.float64), -448.0, 448.0).astype(np.float32).astype(ml_dtypes.float8_e4m3fn).view(np.uint8)


def e4m3fn_values(b):
    return E4M3FN[b]


T, N, J, K, P = 1024, 1024, 1024, 128, 512


def soft_threshold(e, t):
    return np.sign(e) * np.maximum(np.abs(e) - t, 0.0)


def draw0():
    s = mx_kscale(T)
    u = mx_kscale(N)
    a = 0.88 * T**0.25
    inputs = {"x": bf(np.random.standard_normal((T, N)) * a * s[:, None]),
              "y": bf(np.random.standard_normal((T, J)) * a / s[:, None]),
              "l": bf(np.random.standard_normal((N, K))),
              "m": bf(np.random.standard_normal((K, J)) / np.sqrt(K)),
              "tau": bf(np.random.uniform(0.3, 0.9, N)),
              "g": bf((1.0 + 0.1 * np.random.standard_normal(N)) * u)}
    w = np.random.standard_normal((P, N)) / np.sqrt(N) / u[None, :]
    words, scales = pack4(w.T)
    inputs["w_words"] = words
    inputs["w_scales"] = scales
    return inputs


def core(x, y, l, m, tau, g, w_words, w_scales):
    xq = mxq(f64(x), 0, "e4m3")
    yq = mxq(f64(y), 0, "e4m3")
    c = (xq.T @ yq) / x.shape[0]
    f = f64(l) @ f64(m)
    e = c - f
    th = soft_threshold(e, f64(tau)[:, None])
    sig = f64(g)[:, None] * (f + th)
    return unpack4(w_words, w_scales).T @ mxq(sig, 0, "e4m3")


def setup_inputs():
    drawn = draw0()
    full = np.asarray(drawn['y']).astype(np.float64)
    scale = (np.abs(full).reshape(8, 128, 8, 128).max(axis=(1, 3)) / 448.0).astype(np.float32)
    given = {}
    for key, value in drawn.items():
        if key == 'y':
            given['y_bytes'] = e4m3fn_bytes(full / np.repeat(np.repeat(scale.astype(np.float64), 128, axis=0), 128, axis=1))
            given['y_scale'] = scale
        else:
            given[key] = value
    return given


def reference(x, y_bytes, y_scale, l, m, tau, g, w_words, w_scales):
    return core(x, e4m3fn_values(y_bytes) * np.repeat(np.repeat(y_scale.astype(np.float64), 128, axis=0), 128, axis=1), l, m, tau, g, w_words, w_scales)

@@ -1,0 +1,375 @@
+from contextlib import ExitStack
+
+import concourse.mybir as mybir
+from concourse.masks import make_identity
+
+F32 = mybir.dt.float32
+BF16 = mybir.dt.bfloat16
+U8 = mybir.dt.uint8
+U32 = mybir.dt.uint32
+I32 = mybir.dt.int32
+FP8 = mybir.dt.float8_e4m3fn
+FP8X4 = mybir.dt.float8_e4m3fn_x4
+FP4X4 = mybir.dt.float4_e2m1fn_x4
+ALU = mybir.AluOpType
+COPY = mybir.ActivationFunctionType.Copy
+
+T, N, J, K, P = 1024, 1024, 1024, 128, 512
+FLOPS = 2 * T * N * J + 2 * N * K * J + 2 * P * N * J
+H = 512
+
+
+def tile_lowrankplussoftthresholdedcrosscovarianc_d2p_kernel(
+    tc, x, y_bytes, y_scale, l, m, tau, g, w_words, w_scales, out
+):
+    nc = tc.nc
+    with ExitStack() as ctx:
+        keep = ctx.enter_context(tc.tile_pool(name="keep", bufs=1))
+        work = ctx.enter_context(tc.tile_pool(name="work", bufs=2))
+        deep = ctx.enter_context(tc.tile_pool(name="deep", bufs=8))
+        psum = ctx.enter_context(tc.psum_pool(name="psum", bufs=8))
+        ctx.enter_context(tc.manual_schedule())
+
+        x_v = x.rearrange("(q p j) n -> q p j n", q=2, p=128, j=4)
+        y_v = y_bytes.rearrange("(q p j) n -> q p j n", q=2, p=128, j=4)
+
+        x_raw = {(q, s): keep.tile([128, 4, H], BF16, name=f"x_raw_{q}{s}", align_bytes=64) for q in range(2) for s in range(2)}
+        y_raw = {(q, h): keep.tile([128, 4, H], U8, name=f"y_raw_{q}{h}", align_bytes=64) for q in range(2) for h in range(2)}
+        x_code = {(q, s): keep.tile([128, H], U32, name=f"x_code_{q}{s}", align_bytes=64) for q in range(2) for s in range(2)}
+        x_sc = {(q, s): keep.tile([128, H], U8, name=f"x_sc_{q}{s}", align_bytes=64) for q in range(2) for s in range(2)}
+        y_code = {(q, h): keep.tile([128, H], U32, name=f"y_code_{q}{h}", align_bytes=64) for q in range(2) for h in range(2)}
+        y_sc = {(q, h): keep.tile([128, H], U8, name=f"y_sc_{q}{h}", align_bytes=64) for q in range(2) for h in range(2)}
+        s_code = {(s, h): keep.tile([128, H], U32, name=f"s_code_{s}{h}", align_bytes=64) for s in range(2) for h in range(2)}
+        s_sc = {(s, h): keep.tile([128, H], U8, name=f"s_sc_{s}{h}", align_bytes=64) for s in range(2) for h in range(2)}
+        l_sb = keep.tile([128, 2, 4, K], BF16, name="l_sb")
+        m_sb = keep.tile([K, J], BF16, name="m_sb")
+        lT = keep.tile([K, 8, 128], BF16, name="lT")
+        ident = keep.tile([128, 128], BF16, name="ident")
+        ysc = keep.tile([128, 2, 8], F32, name="ysc")
+        g_b = keep.tile([128, 8], BF16, name="g_b")
+        t_b = keep.tile([128, 8], BF16, name="t_b")
+        gf = keep.tile([128, 8], F32, name="gf")
+        gs = keep.tile([128, 8], F32, name="gs")
+        ga = keep.tile([128, 8], F32, name="ga")
+        hi = keep.tile([128, 8], F32, name="hi")
+        hi2 = keep.tile([128, 8], F32, name="hi2")
+        ww = keep.tile([128, 2, 2 * P], U8, name="ww", align_bytes=64)
+        wsc = keep.tile([128, 2, P], U8, name="wsc", align_bytes=64)
+
+        def load_x(q, s, parts=1):
+            w = H // parts
+            for c in range(parts):
+                nc.sync.dma_start(
+                    out=x_raw[q, s][:, :, c * w : (c + 1) * w], in_=x_v[q][:, :, s * H + c * w : s * H + (c + 1) * w]
+                )
+
+        def load_y(q, h):
+            nc.sync.dma_start(out=y_raw[q, h][:], in_=y_v[q][:, :, h * H : (h + 1) * H])
+
+        load_x(0, 0, 2)
+        load_y(0, 0)
+        load_x(1, 0, 2)
+        load_y(1, 0)
+        nc.sync.dma_start(out=l_sb[:], in_=l.rearrange("(s p t) k -> p s t k", s=2, p=128, t=4))
+        nc.sync.dma_start(out=m_sb[:], in_=m)
+        nc.sync.dma_start(out=g_b[:].rearrange("p (s t) -> p s t", s=2), in_=g.rearrange("(s p t) -> p s t", s=2, p=128, t=4))
+        nc.sync.dma_start(out=t_b[:].rearrange("p (s t) -> p s t", s=2), in_=tau.rearrange("(s p t) -> p s t", s=2, p=128, t=4))
+        load_x(0, 1)
+        load_x(1, 1)
+        load_y(0, 1)
+        load_y(1, 1)
+        nc.sync.dma_start(out=ww[:].bitcast(I32), in_=w_words.bitcast(I32).rearrange("s p n -> p s n"))
+        nc.gpsimd.memset(wsc[:].bitcast(I32), 0)
+        for i in range(4):
+            nc.sync.dma_start(
+                out=wsc[32 * i : 32 * i + 4].bitcast(I32),
+                in_=w_scales[:, 4 * i : 4 * i + 4, :].bitcast(I32).rearrange("s r n -> r s n"),
+            )
+
+        for i in range(4):
+            nc.scalar.dma_start(
+                out=ysc[32 * i : 32 * i + 32], in_=y_scale.rearrange("(q i) b -> i q b", i=4)[i].partition_broadcast(32)
+            )
+
+        make_identity(nc, ident[:])
+
+        xi = {}
+        yw = {}
+        yi = {}
+        bank = {}
+        f_bank = {}
+        c_sb = {}
+        a_sb = {}
+        sg = {}
+        si = {}
+
+        def x_lay(q, s, engine_copy=nc.vector.tensor_copy, parts=1):
+            xi[q, s] = work.tile([128, 4 * H], BF16, name="xi", bufs=4, align_bytes=64)
+            dst = xi[q, s][:].rearrange("p (t m j) -> p t m j", t=4, j=4)
+            src = x_raw[q, s][:].rearrange("p j (m t) -> p t m j", t=4)
+            w = 128 // parts
+            for c in range(parts):
+                engine_copy(out=dst[:, :, c * w : (c + 1) * w, :], in_=src[:, :, c * w : (c + 1) * w, :])
+
+        def x_quant(q, s):
+            nc.vector.quantize_mx(out=x_code[q, s][:].bitcast(FP8X4), scales=x_sc[q, s][:], in_=xi[q, s][:])
+
+        def y_widen(q, h):
+            yw[q, h] = work.tile([128, 4, H], BF16, name="yw", bufs=4, align_bytes=64)
+            nc.scalar.copy(
+                out=yw[q, h][:].rearrange("p j n -> p (j n)"), in_=y_raw[q, h][:].rearrange("p j n -> p (j n)").bitcast(FP8)
+            )
+
+        def y_lay_scalar(q, h, blocks=range(4)):
+            if (q, h) not in yi:
+                yi[q, h] = work.tile([128, H, 4], BF16, name="yi", bufs=4, align_bytes=64)
+            for b in blocks:
+                cols = slice(128 * b, 128 * b + 128)
+                nc.scalar.activation(
+                    out=yi[q, h][:, cols, :].rearrange("p (c i) j -> p c j i", i=4),
+                    in_=yw[q, h][:, :, cols].rearrange("p j (c i) -> p c j i", i=4),
+                    func=COPY,
+                    scale=ysc[:, q, 4 * h + b : 4 * h + b + 1],
+                )
+
+        def y_lay(q, h, blocks=range(4)):
+            if (q, h) not in yi:
+                yi[q, h] = work.tile([128, H, 4], BF16, name="yi", bufs=4, align_bytes=64)
+            for b in blocks:
+                cols = slice(128 * b, 128 * b + 128)
+                nc.vector.tensor_scalar(
+                    out=yi[q, h][:, cols, :].rearrange("p (c i) j -> p c j i", i=4),
+                    in0=yw[q, h][:, :, cols].rearrange("p j (c i) -> p c j i", i=4),
+                    scalar1=ysc[:, q, 4 * h + b : 4 * h + b + 1],
+                    scalar2=None,
+                    op0=ALU.mult,
+                )
+
+        def y_quant(q, h):
+            nc.vector.quantize_mx(
+                out=y_code[q, h][:].bitcast(FP8X4), scales=y_sc[q, h][:], in_=yi[q, h][:].rearrange("p n j -> p (n j)")
+            )
+
+        def low_rank_weights():
+            for s in range(2):
+                ps = psum.tile([128, 512], BF16, name="ps_l", tag="ps")
+                for t in range(4):
+                    nc.tensor.transpose(ps[:, 128 * t : 128 * t + 128], l_sb[:, s, t, :], ident[:])
+                nc.scalar.copy(out=lT[:, 4 * s : 4 * s + 4, :].rearrange("p t n -> p (t n)"), in_=ps[:])
+
+        def low_rank(s, h):
+            for t in range(4):
+                ps = psum.tile([128, H], F32, name="ps_f", tag="ps")
+                nc.tensor.matmul(ps[:], lT[:, 4 * s + t, :], m_sb[:, h * H : (h + 1) * H], start=True, stop=True)
+                f_bank[s, t, h] = ps
+
+        def cross(s, h):
+            for t in range(4):
+                ps = psum.tile([128, H], F32, name="ps_c", tag="ps")
+                bank[s, t, h] = ps
+                for q in range(2):
+                    nc.tensor.matmul_mx(
+                        out=ps[:],
+                        lhsT=x_code[q, s][:, 128 * t : 128 * t + 128].bitcast(FP8X4),
+                        lhsT_scale=x_sc[q, s][:, 128 * t : 128 * t + 128],
+                        rhs=y_code[q, h][:].bitcast(FP8X4),
+                        rhs_scale=y_sc[q, h][:],
+                        start=(q == 0),
+                        stop=(q == 1),
+                    )
+
+        def evac(s, h):
+            for t in range(4):
+                col = slice(4 * s + t, 4 * s + t + 1)
+                c_up = deep.tile([128, H], F32, name="c_up")
+                c_sb[s, t, h] = c_up
+                nc.scalar.activation(
+                    out=c_up[:], in_=bank[s, t, h][:], func=mybir.ActivationFunctionType.Identity, scale=gs[:, col], bias=hi[:, col]
+                )
+
+        def cap(s, h, t):
+            a = deep.tile([128, H], F32, name="a_sb", bufs=4)
+            a_sb[s, t, h] = a
+            nc.vector.scalar_tensor_tensor(
+                out=a[:], in0=f_bank[s, t, h][:], scalar=gf[:, 4 * s + t : 4 * s + t + 1], in1=c_sb[s, t, h][:], op0=ALU.mult, op1=ALU.min
+            )
+
+        def floor(s, h, t, lo_c=0, hi_c=H):
+            if (s, h) not in sg:
+                sg[s, h] = work.tile([128, 4, H], BF16, name="sg", bufs=3, align_bytes=64)
+            cols = slice(lo_c, hi_c)
+            nc.vector.scalar_tensor_tensor(
+                out=sg[s, h][:, t, cols],
+                in0=c_sb[s, t, h][:, cols],
+                scalar=hi2[:, 4 * s + t : 4 * s + t + 1],
+                in1=a_sb[s, t, h][:, cols],
+                op0=ALU.subtract,
+                op1=ALU.max,
+            )
+
+        def clip(s, h, lag=1):
+            for t in range(4 + lag):
+                if t < 4:
+                    cap(s, h, t)
+                if t >= lag:
+                    floor(s, h, t - lag)
+
+        def s_lay(s, h, lo_c, hi_c, engine_copy):
+            if (s, h) not in si:
+                si[s, h] = work.tile([128, H, 4], BF16, name="si", bufs=3, align_bytes=64)
+            engine_copy(
+                out=si[s, h][:, lo_c:hi_c, :].rearrange("p (c i) t -> p c t i", i=4),
+                in_=sg[s, h][:, :, lo_c:hi_c].rearrange("p t (c i) -> p c t i", i=4),
+            )
+
+        def s_quant(s, h, lo_c, hi_c):
+            nc.vector.quantize_mx(
+                out=s_code[s, h][:, lo_c:hi_c].bitcast(FP8X4),
+                scales=s_sc[s, h][:, lo_c:hi_c],
+                in_=si[s, h][:, lo_c:hi_c, :].rearrange("p n t -> p (n t)"),
+            )
+
+        acc = {}
+
+        def exposure(s, h):
+            for b in range(4):
+                if s == 0:
+                    acc[b, h] = psum.tile([128, H], F32, name="ps_o", tag="ps")
+                nc.tensor.matmul_mx(
+                    out=acc[b, h][:],
+                    lhsT=ww[:, s, 256 * b : 256 * b + 256].bitcast(FP4X4),
+                    lhsT_scale=wsc[:, s, 128 * b : 128 * b + 128],
+                    rhs=s_code[s, h][:].bitcast(FP8X4),
+                    rhs_scale=s_sc[s, h][:],
+                    start=(s == 0),
+                    stop=(s == 1),
+                )
+
+        def store(h, vector_too):
+            for b in range(4):
+                o = deep.tile([128, H], F32, name="o_sb")
+                if vector_too and b % 2 == 1:
+                    nc.vector.tensor_copy(out=o[:], in_=acc[b, h][:])
+                else:
+                    nc.scalar.copy(out=o[:], in_=acc[b, h][:])
+                nc.sync.dma_start(out=out[128 * b : 128 * b + 128, h * H : (h + 1) * H], in_=o[:])
+
+        def exposure_cols(bank_of, h, lo_c, hi_c):
+            for c in range(lo_c, hi_c, 128):
+                for b in range(4):
+                    for s in range(2):
+                        nc.tensor.matmul_mx(
+                            out=bank_of(b, c),
+                            lhsT=ww[:, s, 256 * b : 256 * b + 256].bitcast(FP4X4),
+                            lhsT_scale=wsc[:, s, 128 * b : 128 * b + 128],
+                            rhs=s_code[s, h][:, c : c + 128].bitcast(FP8X4),
+                            rhs_scale=s_sc[s, h][:, c : c + 128],
+                            start=(s == 0),
+                            stop=(s == 1),
+                        )
+
+        tail = {}
+
+        def exposure_main(h, lo_c, hi_c):
+            if lo_c == 0:
+                for b in range(4):
+                    tail[b] = psum.tile([128, H], F32, name="ps_m", tag="ps")
+            exposure_cols(lambda b, c: tail[b][:, c : c + 128], h, lo_c, hi_c)
+
+        def exposure_last(h):
+            for b in range(2):
+                tail[4 + b] = psum.tile([128, H], F32, name="ps_t", tag="ps")
+            exposure_cols(lambda b, c: tail[4 + b // 2][:, 128 * (b % 2) : 128 * (b % 2) + 128], h, H - 128, H)
+
+        def store_main(h, b, engine_copy):
+            o = deep.tile([128, H - 128], F32, name="o_main", bufs=4)
+            engine_copy(out=o[:], in_=tail[b][:, : H - 128])
+            nc.sync.dma_start(out=out[128 * b : 128 * b + 128, h * H : h * H + H - 128], in_=o[:])
+
+        def store_last(h):
+            for b, engine_copy in ((0, vcopy), (1, scopy)):
+                o = deep.tile([128, 2, 128], F32, name="o_last", bufs=2)
+                engine_copy(out=o[:].rearrange("p b n -> p (b n)"), in_=tail[4 + b][:, :256])
+                nc.sync.dma_start(
+                    out=out[256 * b : 256 * b + 256, h * H + H - 128 : h * H + H].rearrange("(b p) n -> p b n", b=2), in_=o[:]
+                )
+
+        def row_factors():
+            nc.scalar.activation(out=gf[:], in_=g_b[:], func=COPY)
+            nc.scalar.activation(out=gs[:], in_=g_b[:], func=COPY, scale=1.0 / T)
+            nc.scalar.activation(out=ga[:], in_=g_b[:], func=mybir.ActivationFunctionType.Abs)
+
+        def thresholds():
+            nc.vector.tensor_tensor(out=hi[:], in0=ga[:], in1=t_b[:], op=ALU.mult)
+            nc.vector.scalar_tensor_tensor(out=hi2[:], in0=t_b[:], scalar=2.0, in1=ga[:], op0=ALU.mult, op1=ALU.mult)
+
+        def warm(s, h, t, lo_c, hi_c):
+            if t == 0 and lo_c == 0:
+                bank["warm"] = psum.tile([128, H], F32, name="ps_w", tag="ps")
+            nc.tensor.matmul(bank["warm"][:, lo_c:hi_c], ident[:], sg[s, h][:, t, lo_c:hi_c], start=True, stop=True)
+
+        vcopy = nc.vector.tensor_copy
+        scopy = nc.scalar.copy
+
+        x_lay(0, 0, vcopy, 2)
+        y_widen(0, 0)
+        x_lay(1, 0, vcopy, 2)
+        y_widen(1, 0)
+        x_quant(0, 0)
+        x_quant(1, 0)
+        low_rank_weights()
+        row_factors()
+        y_lay(0, 0)
+        y_lay(1, 0)
+        y_widen(0, 1)
+        thresholds()
+        y_quant(0, 0)
+        y_quant(1, 0)
+        cross(0, 0)
+        low_rank(0, 0)
+        x_lay(0, 1)
+        x_lay(1, 1)
+        evac(0, 0)
+        x_quant(0, 1)
+        x_quant(1, 1)
+        y_widen(1, 1)
+        cross(1, 0)
+        clip(0, 0)
+        low_rank(1, 0)
+        y_lay_scalar(1, 1)
+        y_lay_scalar(0, 1, range(2))
+        y_lay(0, 1, range(2, 4))
+        y_quant(1, 1)
+        y_quant(0, 1)
+        evac(1, 0)
+        cross(0, 1)
+        s_lay(0, 0, 0, H, scopy)
+        clip(1, 0)
+        evac(0, 1)
+        low_rank(0, 1)
+        cross(1, 1)
+        s_quant(0, 0, 0, H)
+        exposure(0, 0)
+        clip(0, 1)
+        s_lay(1, 0, 0, H, scopy)
+        evac(1, 1)
+        low_rank(1, 1)
+        s_quant(1, 0, 0, H)
+        exposure(1, 0)
+        s_lay(0, 1, 0, H, scopy)
+        cap(1, 1, 0)
+        cap(1, 1, 1)
+        cap(1, 1, 2)
+        cap(1, 1, 3)
+        for t in range(4): floor(1, 1, t, 0, 256); warm(1, 1, t, 0, 256)
+        for t in range(4): floor(1, 1, t, 256, H); warm(1, 1, t, 256, H)
+        store(0, False)
+        s_lay(1, 1, 0, 256, scopy)
+        s_lay(1, 1, 256, 384, scopy)
+        s_quant(0, 1, 0, H)
+        exposure(0, 1)
+        s_lay(1, 1, 384, H, vcopy)
+        s_quant(1, 1, 0, 256)
+        s_quant(1, 1, 256, H)
+        exposure(1, 1)
+        store(1, True)

@@ -303,11 +303,6 @@ def tile_lowrankplussoftthresholdedcrosscovarianc_d2p_kernel(
             nc.vector.tensor_tensor(out=hi[:], in0=ga[:], in1=t_b[:], op=ALU.mult)
             nc.vector.scalar_tensor_tensor(out=hi2[:], in0=t_b[:], scalar=2.0, in1=ga[:], op0=ALU.mult, op1=ALU.mult)
 
-        def warm(s, h, t, lo_c, hi_c):
-            if t == 0 and lo_c == 0:
-                bank["warm"] = psum.tile([128, H], F32, name="ps_w", tag="ps")
-            nc.tensor.matmul(bank["warm"][:, lo_c:hi_c], ident[:], sg[s, h][:, t, lo_c:hi_c], start=True, stop=True)
-
         vcopy = nc.vector.tensor_copy
         scopy = nc.scalar.copy
 
@@ -361,8 +356,8 @@ def tile_lowrankplussoftthresholdedcrosscovarianc_d2p_kernel(
         cap(1, 1, 1)
         cap(1, 1, 2)
         cap(1, 1, 3)
-        for t in range(4): floor(1, 1, t, 0, 256); warm(1, 1, t, 0, 256)
-        for t in range(4): floor(1, 1, t, 256, H); warm(1, 1, t, 256, H)
+        for t in range(4): floor(1, 1, t, 0, 256)
+        for t in range(4): floor(1, 1, t, 256, H)
         store(0, False)
         s_lay(1, 1, 0, 256, scopy)
         s_lay(1, 1, 256, 384, scopy)

@@ -12,11 +12,13 @@ FP8 = mybir.dt.float8_e4m3fn
 FP8X4 = mybir.dt.float8_e4m3fn_x4
 FP4X4 = mybir.dt.float4_e2m1fn_x4
 ALU = mybir.AluOpType
-COPY = mybir.ActivationFunctionType.Copy
+ACT = mybir.ActivationFunctionType
 
 T, N, J, K, P = 1024, 1024, 1024, 128, 512
 FLOPS = 2 * T * N * J + 2 * N * K * J + 2 * P * N * J
-H = 512
+BANK = 512
+BLOCK = 128
+CHUNKS = ((0, 512), (512, 256), (768, 256))
 
 
 def tile_lowrankplussoftthresholdedcrosscovarianc_d2p_kernel(
@@ -26,345 +28,321 @@ def tile_lowrankplussoftthresholdedcrosscovarianc_d2p_kernel(
     with ExitStack() as ctx:
         keep = ctx.enter_context(tc.tile_pool(name="keep", bufs=1))
         work = ctx.enter_context(tc.tile_pool(name="work", bufs=2))
-        deep = ctx.enter_context(tc.tile_pool(name="deep", bufs=8))
-        psum = ctx.enter_context(tc.psum_pool(name="psum", bufs=8))
+        psum = ctx.enter_context(tc.psum_pool(name="psum", bufs=1))
         ctx.enter_context(tc.manual_schedule())
 
         x_v = x.rearrange("(q p j) n -> q p j n", q=2, p=128, j=4)
-        y_v = y_bytes.rearrange("(q p j) n -> q p j n", q=2, p=128, j=4)
+        y_v = y_bytes.rearrange("(q p j) n -> q p (j n)", q=2, p=128, j=4)
+        both = [(q, h) for q in range(2) for h in range(2)]
 
-        x_raw = {(q, s): keep.tile([128, 4, H], BF16, name=f"x_raw_{q}{s}", align_bytes=64) for q in range(2) for s in range(2)}
-        y_raw = {(q, h): keep.tile([128, 4, H], U8, name=f"y_raw_{q}{h}", align_bytes=64) for q in range(2) for h in range(2)}
-        x_code = {(q, s): keep.tile([128, H], U32, name=f"x_code_{q}{s}", align_bytes=64) for q in range(2) for s in range(2)}
-        x_sc = {(q, s): keep.tile([128, H], U8, name=f"x_sc_{q}{s}", align_bytes=64) for q in range(2) for s in range(2)}
-        y_code = {(q, h): keep.tile([128, H], U32, name=f"y_code_{q}{h}", align_bytes=64) for q in range(2) for h in range(2)}
-        y_sc = {(q, h): keep.tile([128, H], U8, name=f"y_sc_{q}{h}", align_bytes=64) for q in range(2) for h in range(2)}
-        s_code = {(s, h): keep.tile([128, H], U32, name=f"s_code_{s}{h}", align_bytes=64) for s in range(2) for h in range(2)}
-        s_sc = {(s, h): keep.tile([128, H], U8, name=f"s_sc_{s}{h}", align_bytes=64) for s in range(2) for h in range(2)}
+        x_raw = [keep.tile([128, 4, N], BF16, name=f"x_raw_{q}", align_bytes=64) for q in range(2)]
+        y_raw = {(q, h): keep.tile([128, 2 * J], U8, name=f"y_raw_{q}{h}", align_bytes=64) for q, h in both}
+        y_wide = [keep.tile([128, 4, J], BF16, name=f"y_wide_{q}", align_bytes=64) for q in range(2)]
+        x_laid = {(q, s): keep.tile([128, 4 * BANK], BF16, name=f"x_laid_{q}{s}", align_bytes=64) for q, s in both}
+        y_laid = {(q, h): keep.tile([128, BANK, 4], BF16, name=f"y_laid_{q}{h}", align_bytes=64) for q, h in both}
+        x_code = {(q, s): keep.tile([128, BANK], U32, name=f"x_code_{q}{s}", align_bytes=64) for q, s in both}
+        x_sc = {(q, s): keep.tile([128, BANK], U8, name=f"x_sc_{q}{s}", align_bytes=64) for q, s in both}
+        y_code = [keep.tile([128, J], U32, name=f"y_code_{q}", align_bytes=64) for q in range(2)]
+        y_sc = [keep.tile([128, J], U8, name=f"y_sc_{q}", align_bytes=64) for q in range(2)]
+        s_code = [keep.tile([128, J], U32, name=f"s_code_{s}", align_bytes=64) for s in range(2)]
+        s_sc = [keep.tile([128, J], U8, name=f"s_sc_{s}", align_bytes=64) for s in range(2)]
         l_sb = keep.tile([128, 2, 4, K], BF16, name="l_sb")
         m_sb = keep.tile([K, J], BF16, name="m_sb")
-        lT = keep.tile([K, 8, 128], BF16, name="lT")
+        l_t = keep.tile([K, 8, 128], BF16, name="l_t")
         ident = keep.tile([128, 128], BF16, name="ident")
-        ysc = keep.tile([128, 2, 8], F32, name="ysc")
+        y_fac = keep.tile([128, 2, 8], F32, name="y_fac")
         g_b = keep.tile([128, 8], BF16, name="g_b")
         t_b = keep.tile([128, 8], BF16, name="t_b")
-        gf = keep.tile([128, 8], F32, name="gf")
-        gs = keep.tile([128, 8], F32, name="gs")
-        ga = keep.tile([128, 8], F32, name="ga")
-        hi = keep.tile([128, 8], F32, name="hi")
-        hi2 = keep.tile([128, 8], F32, name="hi2")
-        ww = keep.tile([128, 2, 2 * P], U8, name="ww", align_bytes=64)
-        wsc = keep.tile([128, 2, P], U8, name="wsc", align_bytes=64)
+        g_f = keep.tile([128, 8], F32, name="g_f")
+        g_c = keep.tile([128, 8], F32, name="g_c")
+        g_abs = keep.tile([128, 8], F32, name="g_abs")
+        width = keep.tile([128, 8], F32, name="width")
+        width2 = keep.tile([128, 8], F32, name="width2")
+        w_code = keep.tile([128, 2, 2 * P], U8, name="w_code", align_bytes=64)
+        w_sc = keep.tile([128, 2, P], U8, name="w_sc", align_bytes=64)
 
-        def load_x(q, s, parts=1):
-            w = H // parts
-            for c in range(parts):
-                nc.sync.dma_start(
-                    out=x_raw[q, s][:, :, c * w : (c + 1) * w], in_=x_v[q][:, :, s * H + c * w : s * H + (c + 1) * w]
-                )
-
-        def load_y(q, h):
-            nc.sync.dma_start(out=y_raw[q, h][:], in_=y_v[q][:, :, h * H : (h + 1) * H])
-
-        load_x(0, 0, 2)
-        load_y(0, 0)
-        load_x(1, 0, 2)
-        load_y(1, 0)
+        for q, h in both:
+            nc.sync.dma_start(out=y_raw[q, h][:], in_=y_v[q][:, 2 * J * h : 2 * J * (h + 1)])
+        for q in range(2):
+            nc.sync.dma_start(out=x_raw[q][:], in_=x_v[q])
         nc.sync.dma_start(out=l_sb[:], in_=l.rearrange("(s p t) k -> p s t k", s=2, p=128, t=4))
         nc.sync.dma_start(out=m_sb[:], in_=m)
         nc.sync.dma_start(out=g_b[:].rearrange("p (s t) -> p s t", s=2), in_=g.rearrange("(s p t) -> p s t", s=2, p=128, t=4))
         nc.sync.dma_start(out=t_b[:].rearrange("p (s t) -> p s t", s=2), in_=tau.rearrange("(s p t) -> p s t", s=2, p=128, t=4))
-        load_x(0, 1)
-        load_x(1, 1)
-        load_y(0, 1)
-        load_y(1, 1)
-        nc.sync.dma_start(out=ww[:].bitcast(I32), in_=w_words.bitcast(I32).rearrange("s p n -> p s n"))
-        nc.gpsimd.memset(wsc[:].bitcast(I32), 0)
+        nc.sync.dma_start(out=w_code[:].bitcast(I32), in_=w_words.bitcast(I32).rearrange("s p n -> p s n"))
+        nc.gpsimd.memset(w_sc[:].bitcast(I32), 0)
         for i in range(4):
             nc.sync.dma_start(
-                out=wsc[32 * i : 32 * i + 4].bitcast(I32),
+                out=w_sc[32 * i : 32 * i + 4].bitcast(I32),
                 in_=w_scales[:, 4 * i : 4 * i + 4, :].bitcast(I32).rearrange("s r n -> r s n"),
             )
-
         for i in range(4):
             nc.scalar.dma_start(
-                out=ysc[32 * i : 32 * i + 32], in_=y_scale.rearrange("(q i) b -> i q b", i=4)[i].partition_broadcast(32)
+                out=y_fac[32 * i : 32 * i + 32], in_=y_scale.rearrange("(q i) b -> i q b", i=4)[i].partition_broadcast(32)
             )
-
         make_identity(nc, ident[:])
-
-        xi = {}
-        yw = {}
-        yi = {}
-        bank = {}
-        f_bank = {}
-        c_sb = {}
-        a_sb = {}
-        sg = {}
-        si = {}
-
-        def x_lay(q, s, engine_copy=nc.vector.tensor_copy, parts=1):
-            xi[q, s] = work.tile([128, 4 * H], BF16, name="xi", bufs=4, align_bytes=64)
-            dst = xi[q, s][:].rearrange("p (t m j) -> p t m j", t=4, j=4)
-            src = x_raw[q, s][:].rearrange("p j (m t) -> p t m j", t=4)
-            w = 128 // parts
-            for c in range(parts):
-                engine_copy(out=dst[:, :, c * w : (c + 1) * w, :], in_=src[:, :, c * w : (c + 1) * w, :])
-
-        def x_quant(q, s):
-            nc.vector.quantize_mx(out=x_code[q, s][:].bitcast(FP8X4), scales=x_sc[q, s][:], in_=xi[q, s][:])
-
-        def y_widen(q, h):
-            yw[q, h] = work.tile([128, 4, H], BF16, name="yw", bufs=4, align_bytes=64)
-            nc.scalar.copy(
-                out=yw[q, h][:].rearrange("p j n -> p (j n)"), in_=y_raw[q, h][:].rearrange("p j n -> p (j n)").bitcast(FP8)
-            )
-
-        def y_lay_scalar(q, h, blocks=range(4)):
-            if (q, h) not in yi:
-                yi[q, h] = work.tile([128, H, 4], BF16, name="yi", bufs=4, align_bytes=64)
-            for b in blocks:
-                cols = slice(128 * b, 128 * b + 128)
-                nc.scalar.activation(
-                    out=yi[q, h][:, cols, :].rearrange("p (c i) j -> p c j i", i=4),
-                    in_=yw[q, h][:, :, cols].rearrange("p j (c i) -> p c j i", i=4),
-                    func=COPY,
-                    scale=ysc[:, q, 4 * h + b : 4 * h + b + 1],
-                )
-
-        def y_lay(q, h, blocks=range(4)):
-            if (q, h) not in yi:
-                yi[q, h] = work.tile([128, H, 4], BF16, name="yi", bufs=4, align_bytes=64)
-            for b in blocks:
-                cols = slice(128 * b, 128 * b + 128)
-                nc.vector.tensor_scalar(
-                    out=yi[q, h][:, cols, :].rearrange("p (c i) j -> p c j i", i=4),
-                    in0=yw[q, h][:, :, cols].rearrange("p j (c i) -> p c j i", i=4),
-                    scalar1=ysc[:, q, 4 * h + b : 4 * h + b + 1],
-                    scalar2=None,
-                    op0=ALU.mult,
-                )
-
-        def y_quant(q, h):
-            nc.vector.quantize_mx(
-                out=y_code[q, h][:].bitcast(FP8X4), scales=y_sc[q, h][:], in_=yi[q, h][:].rearrange("p n j -> p (n j)")
-            )
-
-        def low_rank_weights():
-            for s in range(2):
-                ps = psum.tile([128, 512], BF16, name="ps_l", tag="ps")
-                for t in range(4):
-                    nc.tensor.transpose(ps[:, 128 * t : 128 * t + 128], l_sb[:, s, t, :], ident[:])
-                nc.scalar.copy(out=lT[:, 4 * s : 4 * s + 4, :].rearrange("p t n -> p (t n)"), in_=ps[:])
-
-        def low_rank(s, h):
-            for t in range(4):
-                ps = psum.tile([128, H], F32, name="ps_f", tag="ps")
-                nc.tensor.matmul(ps[:], lT[:, 4 * s + t, :], m_sb[:, h * H : (h + 1) * H], start=True, stop=True)
-                f_bank[s, t, h] = ps
-
-        def cross(s, h):
-            for t in range(4):
-                ps = psum.tile([128, H], F32, name="ps_c", tag="ps")
-                bank[s, t, h] = ps
-                for q in range(2):
-                    nc.tensor.matmul_mx(
-                        out=ps[:],
-                        lhsT=x_code[q, s][:, 128 * t : 128 * t + 128].bitcast(FP8X4),
-                        lhsT_scale=x_sc[q, s][:, 128 * t : 128 * t + 128],
-                        rhs=y_code[q, h][:].bitcast(FP8X4),
-                        rhs_scale=y_sc[q, h][:],
-                        start=(q == 0),
-                        stop=(q == 1),
-                    )
-
-        def evac(s, h):
-            for t in range(4):
-                col = slice(4 * s + t, 4 * s + t + 1)
-                c_up = deep.tile([128, H], F32, name="c_up")
-                c_sb[s, t, h] = c_up
-                nc.scalar.activation(
-                    out=c_up[:], in_=bank[s, t, h][:], func=mybir.ActivationFunctionType.Identity, scale=gs[:, col], bias=hi[:, col]
-                )
-
-        def cap(s, h, t):
-            a = deep.tile([128, H], F32, name="a_sb", bufs=4)
-            a_sb[s, t, h] = a
-            nc.vector.scalar_tensor_tensor(
-                out=a[:], in0=f_bank[s, t, h][:], scalar=gf[:, 4 * s + t : 4 * s + t + 1], in1=c_sb[s, t, h][:], op0=ALU.mult, op1=ALU.min
-            )
-
-        def floor(s, h, t, lo_c=0, hi_c=H):
-            if (s, h) not in sg:
-                sg[s, h] = work.tile([128, 4, H], BF16, name="sg", bufs=3, align_bytes=64)
-            cols = slice(lo_c, hi_c)
-            nc.vector.scalar_tensor_tensor(
-                out=sg[s, h][:, t, cols],
-                in0=c_sb[s, t, h][:, cols],
-                scalar=hi2[:, 4 * s + t : 4 * s + t + 1],
-                in1=a_sb[s, t, h][:, cols],
-                op0=ALU.subtract,
-                op1=ALU.max,
-            )
-
-        def clip(s, h, lag=1):
-            for t in range(4 + lag):
-                if t < 4:
-                    cap(s, h, t)
-                if t >= lag:
-                    floor(s, h, t - lag)
-
-        def s_lay(s, h, lo_c, hi_c, engine_copy):
-            if (s, h) not in si:
-                si[s, h] = work.tile([128, H, 4], BF16, name="si", bufs=3, align_bytes=64)
-            engine_copy(
-                out=si[s, h][:, lo_c:hi_c, :].rearrange("p (c i) t -> p c t i", i=4),
-                in_=sg[s, h][:, :, lo_c:hi_c].rearrange("p t (c i) -> p c t i", i=4),
-            )
-
-        def s_quant(s, h, lo_c, hi_c):
-            nc.vector.quantize_mx(
-                out=s_code[s, h][:, lo_c:hi_c].bitcast(FP8X4),
-                scales=s_sc[s, h][:, lo_c:hi_c],
-                in_=si[s, h][:, lo_c:hi_c, :].rearrange("p n t -> p (n t)"),
-            )
-
-        acc = {}
-
-        def exposure(s, h):
-            for b in range(4):
-                if s == 0:
-                    acc[b, h] = psum.tile([128, H], F32, name="ps_o", tag="ps")
-                nc.tensor.matmul_mx(
-                    out=acc[b, h][:],
-                    lhsT=ww[:, s, 256 * b : 256 * b + 256].bitcast(FP4X4),
-                    lhsT_scale=wsc[:, s, 128 * b : 128 * b + 128],
-                    rhs=s_code[s, h][:].bitcast(FP8X4),
-                    rhs_scale=s_sc[s, h][:],
-                    start=(s == 0),
-                    stop=(s == 1),
-                )
-
-        def store(h, vector_too):
-            for b in range(4):
-                o = deep.tile([128, H], F32, name="o_sb")
-                if vector_too and b % 2 == 1:
-                    nc.vector.tensor_copy(out=o[:], in_=acc[b, h][:])
-                else:
-                    nc.scalar.copy(out=o[:], in_=acc[b, h][:])
-                nc.sync.dma_start(out=out[128 * b : 128 * b + 128, h * H : (h + 1) * H], in_=o[:])
-
-        def exposure_cols(bank_of, h, lo_c, hi_c):
-            for c in range(lo_c, hi_c, 128):
-                for b in range(4):
-                    for s in range(2):
-                        nc.tensor.matmul_mx(
-                            out=bank_of(b, c),
-                            lhsT=ww[:, s, 256 * b : 256 * b + 256].bitcast(FP4X4),
-                            lhsT_scale=wsc[:, s, 128 * b : 128 * b + 128],
-                            rhs=s_code[s, h][:, c : c + 128].bitcast(FP8X4),
-                            rhs_scale=s_sc[s, h][:, c : c + 128],
-                            start=(s == 0),
-                            stop=(s == 1),
-                        )
-
-        tail = {}
-
-        def exposure_main(h, lo_c, hi_c):
-            if lo_c == 0:
-                for b in range(4):
-                    tail[b] = psum.tile([128, H], F32, name="ps_m", tag="ps")
-            exposure_cols(lambda b, c: tail[b][:, c : c + 128], h, lo_c, hi_c)
-
-        def exposure_last(h):
-            for b in range(2):
-                tail[4 + b] = psum.tile([128, H], F32, name="ps_t", tag="ps")
-            exposure_cols(lambda b, c: tail[4 + b // 2][:, 128 * (b % 2) : 128 * (b % 2) + 128], h, H - 128, H)
-
-        def store_main(h, b, engine_copy):
-            o = deep.tile([128, H - 128], F32, name="o_main", bufs=4)
-            engine_copy(out=o[:], in_=tail[b][:, : H - 128])
-            nc.sync.dma_start(out=out[128 * b : 128 * b + 128, h * H : h * H + H - 128], in_=o[:])
-
-        def store_last(h):
-            for b, engine_copy in ((0, vcopy), (1, scopy)):
-                o = deep.tile([128, 2, 128], F32, name="o_last", bufs=2)
-                engine_copy(out=o[:].rearrange("p b n -> p (b n)"), in_=tail[4 + b][:, :256])
-                nc.sync.dma_start(
-                    out=out[256 * b : 256 * b + 256, h * H + H - 128 : h * H + H].rearrange("(b p) n -> p b n", b=2), in_=o[:]
-                )
-
-        def row_factors():
-            nc.scalar.activation(out=gf[:], in_=g_b[:], func=COPY)
-            nc.scalar.activation(out=gs[:], in_=g_b[:], func=COPY, scale=1.0 / T)
-            nc.scalar.activation(out=ga[:], in_=g_b[:], func=mybir.ActivationFunctionType.Abs)
-
-        def thresholds():
-            nc.vector.tensor_tensor(out=hi[:], in0=ga[:], in1=t_b[:], op=ALU.mult)
-            nc.vector.scalar_tensor_tensor(out=hi2[:], in0=t_b[:], scalar=2.0, in1=ga[:], op0=ALU.mult, op1=ALU.mult)
 
         vcopy = nc.vector.tensor_copy
         scopy = nc.scalar.copy
 
-        x_lay(0, 0, vcopy, 2)
-        y_widen(0, 0)
-        x_lay(1, 0, vcopy, 2)
-        y_widen(1, 0)
+        def vscale(out, in_, scale):
+            nc.vector.tensor_scalar(out=out, in0=in_, scalar1=scale, scalar2=None, op0=ALU.mult)
+
+        def sscale(out, in_, scale):
+            nc.scalar.activation(out=out, in_=in_, func=ACT.Copy, scale=scale)
+
+        def y_widen(q, lo, hi, copy):
+            src = y_raw[q, lo // 2][:, (lo % 2) * J : (lo % 2 + hi - lo) * J]
+            copy(out=y_wide[q][:, lo:hi, :].rearrange("p j n -> p (j n)"), in_=src.bitcast(FP8))
+
+        def y_lay(q, h, scaled_copy, blocks=range(4)):
+            for b in blocks:
+                col = 4 * h + b
+                scaled_copy(
+                    y_laid[q, h][:, BLOCK * b : BLOCK * (b + 1), :].rearrange("p (c i) j -> p c j i", i=4),
+                    y_wide[q][:, :, BLOCK * col : BLOCK * (col + 1)].rearrange("p j (c i) -> p c j i", i=4),
+                    y_fac[:, q, col : col + 1],
+                )
+
+        def y_quant(q, h):
+            cols = slice(BANK * h, BANK * (h + 1))
+            nc.vector.quantize_mx(
+                out=y_code[q][:, cols].bitcast(FP8X4), scales=y_sc[q][:, cols], in_=y_laid[q, h][:].rearrange("p n j -> p (n j)")
+            )
+
+        def x_lay(q, s, copy, lo=0, hi=64):
+            dst = x_laid[q, s][:].rearrange("p (t r e j) -> p r t e j", t=4, e=2, j=4)
+            src = x_raw[q][:, :, BANK * s : BANK * (s + 1)].rearrange("p j (r e t) -> p r t e j", e=2, t=4)
+            copy(out=dst[:, lo:hi], in_=src[:, lo:hi])
+
+        def x_quant(q, s):
+            nc.vector.quantize_mx(out=x_code[q, s][:].bitcast(FP8X4), scales=x_sc[q, s][:], in_=x_laid[q, s][:])
+
+        def low_rank_weights():
+            for s in range(2):
+                ps = psum.tile([128, BANK], BF16, name="ps_l", tag="o", bufs=2)
+                for t in range(4):
+                    nc.tensor.transpose(ps[:, 128 * t : 128 * t + 128], l_sb[:, s, t, :], ident[:])
+                scopy(out=l_t[:, 4 * s : 4 * s + 4, :].rearrange("p t n -> p (t n)"), in_=ps[:])
+
+        def row_factors():
+            nc.scalar.activation(out=g_f[:], in_=g_b[:], func=ACT.Copy)
+            nc.scalar.activation(out=g_c[:], in_=g_b[:], func=ACT.Copy, scale=1.0 / T)
+            nc.scalar.activation(out=g_abs[:], in_=g_b[:], func=ACT.Abs)
+
+        def widths():
+            nc.vector.tensor_tensor(out=width[:], in0=g_abs[:], in1=t_b[:], op=ALU.mult)
+            nc.vector.scalar_tensor_tensor(out=width2[:], in0=t_b[:], scalar=2.0, in1=g_abs[:], op0=ALU.mult, op1=ALU.mult)
+
+        c_ps, f_ps, c_up, capped, sig, sig_laid, o_ps = {}, {}, {}, {}, {}, {}, {}
+
+        def slot(store, tag, bufs, k, s, t):
+            w = CHUNKS[k][1]
+            per = BANK // w
+            if t % per == 0:
+                store[k, s, t // per] = psum.tile([128, BANK], F32, name="ps_" + tag, tag=tag, bufs=bufs)
+            return store[k, s, t // per][:, w * (t % per) : w * (t % per + 1)]
+
+        def at(store, k, s, t):
+            w = CHUNKS[k][1]
+            per = BANK // w
+            return store[k, s, t // per][:, w * (t % per) : w * (t % per + 1)]
+
+        def cross(k, s, t):
+            lo, w = CHUNKS[k]
+            ps = slot(c_ps, "c", 3, k, s, t)
+            for q in range(2):
+                nc.tensor.matmul_mx(
+                    out=ps,
+                    lhsT=x_code[q, s][:, 128 * t : 128 * t + 128].bitcast(FP8X4),
+                    lhsT_scale=x_sc[q, s][:, 128 * t : 128 * t + 128],
+                    rhs=y_code[q][:, lo : lo + w].bitcast(FP8X4),
+                    rhs_scale=y_sc[q][:, lo : lo + w],
+                    start=(q == 0),
+                    stop=(q == 1),
+                )
+
+        def low_rank(k, s, t):
+            lo, w = CHUNKS[k]
+            nc.tensor.matmul(slot(f_ps, "f", 3, k, s, t), l_t[:, 4 * s + t, :], m_sb[:, lo : lo + w], start=True, stop=True)
+
+        def lift(k, s, t):
+            col = slice(4 * s + t, 4 * s + t + 1)
+            c_up[k, s, t] = work.tile([128, CHUNKS[k][1]], F32, name=f"c_up_{k}{s}{t}", bufs=1)
+            nc.scalar.activation(out=c_up[k, s, t][:], in_=at(c_ps, k, s, t), func=ACT.Identity, scale=g_c[:, col], bias=width[:, col])
+
+        def cap(k, s, t, lo, hi):
+            if lo == 0:
+                capped[k, s, t] = work.tile([128, CHUNKS[k][1]], F32, name="capped", bufs=4)
+            nc.vector.scalar_tensor_tensor(
+                out=capped[k, s, t][:, lo:hi],
+                in0=at(f_ps, k, s, t)[:, lo:hi],
+                scalar=g_f[:, 4 * s + t : 4 * s + t + 1],
+                in1=c_up[k, s, t][:, lo:hi],
+                op0=ALU.mult,
+                op1=ALU.min,
+            )
+
+        def floor(k, s, t, lo, hi):
+            if t == 0 and lo == 0:
+                sig[k, s] = work.tile([128, 4, CHUNKS[k][1]], BF16, name="sig", bufs=3, align_bytes=64)
+            nc.vector.scalar_tensor_tensor(
+                out=sig[k, s][:, t, lo:hi],
+                in0=c_up[k, s, t][:, lo:hi],
+                scalar=width2[:, 4 * s + t : 4 * s + t + 1],
+                in1=capped[k, s, t][:, lo:hi],
+                op0=ALU.subtract,
+                op1=ALU.max,
+            )
+
+        def s_lay(k, s, lo, hi, copy):
+            if lo == 0:
+                sig_laid[k, s] = work.tile([128, CHUNKS[k][1], 4], BF16, name="sig_laid", bufs=3, align_bytes=64)
+            copy(
+                out=sig_laid[k, s][:, lo:hi, :].rearrange("p (c i) t -> p c t i", i=4),
+                in_=sig[k, s][:, :, lo:hi].rearrange("p t (c i) -> p c t i", i=4),
+            )
+
+        def s_quant(k, s, lo, hi):
+            cols = slice(CHUNKS[k][0] + lo, CHUNKS[k][0] + hi)
+            nc.vector.quantize_mx(
+                out=s_code[s][:, cols].bitcast(FP8X4),
+                scales=s_sc[s][:, cols],
+                in_=sig_laid[k, s][:, lo:hi, :].rearrange("p n t -> p (n t)"),
+            )
+
+        def exposure_group(ps, b, lo, hi):
+            for s in range(2):
+                nc.tensor.matmul_mx(
+                    out=ps,
+                    lhsT=w_code[:, s, 256 * b : 256 * b + 256].bitcast(FP4X4),
+                    lhsT_scale=w_sc[:, s, 128 * b : 128 * b + 128],
+                    rhs=s_code[s][:, lo:hi].bitcast(FP8X4),
+                    rhs_scale=s_sc[s][:, lo:hi],
+                    start=(s == 0),
+                    stop=(s == 1),
+                )
+
+        def exposure_wide(b, lo):
+            o_ps[b, lo] = psum.tile([128, BANK], F32, name="ps_o", tag="o", bufs=2)
+            exposure_group(o_ps[b, lo][:], b, lo, lo + BANK)
+
+        def store_wide(b, lo, copy):
+            o_sb = work.tile([128, BANK], F32, name="o_sb", bufs=8)
+            copy(out=o_sb[:], in_=o_ps[b, lo][:])
+            nc.sync.dma_start(out=out[128 * b : 128 * b + 128, lo : lo + BANK], in_=o_sb[:])
+
+        def exposure_narrow(bs, lo, hi, tag="c", bufs=3):
+            ps = psum.tile([128, BANK], F32, name="ps_o", tag=tag, bufs=bufs)
+            o_ps[bs[0], lo] = ps
+            for i, b in enumerate(bs):
+                for c in range(lo, hi, BLOCK):
+                    at_col = i * (hi - lo) + c - lo
+                    exposure_group(ps[:, at_col : at_col + BLOCK], b, c, c + BLOCK)
+
+        def store_narrow(bs, lo, hi, copy):
+            n = len(bs) * (hi - lo)
+            o_sb = work.tile([128, BANK], F32, name="o_sb", bufs=8)
+            copy(out=o_sb[:, :n], in_=o_ps[bs[0], lo][:, :n])
+            nc.sync.dma_start(
+                out=out[128 * bs[0] : 128 * (bs[-1] + 1), lo:hi].rearrange("(b p) n -> p b n", p=128),
+                in_=o_sb[:, :n].rearrange("p (b n) -> p b n", b=len(bs)),
+            )
+
+
+        units = [(k, s) for k in range(len(CHUNKS)) for s in range(2)]
+        per_bank = [BANK // CHUNKS[k][1] for k, s in units]
+        f_banks = [[(k, s, t) for t in range(lo, lo + per)] for (k, s), per in zip(units, per_bank) for lo in range(0, 4, per)]
+
+        def low_rank_bank(i):
+            if i < len(f_banks):
+                for tile in f_banks[i]:
+                    low_rank(*tile)
+
+        def cross_and_lift(u, t):
+            cross(*units[u], t)
+            if (t + 1) % per_bank[u] == 0:
+                for a in range(t + 1 - per_bank[u], t + 1):
+                    lift(*units[u], a)
+
+        def clamp_unit(u, *beside):
+            k, s = units[u]
+            w = CHUNKS[k][1]
+            for t in range(4):
+                cap(k, s, t, 0, w)
+                if t > 0:
+                    floor(k, s, t - 1, 0, w)
+                for step, *args in beside[t]:
+                    step(*args)
+                if (t + 1) % per_bank[u] == 0:
+                    low_rank_bank(f_banks.index([(k, s, a) for a in range(t + 1 - per_bank[u], t + 1)]) + 3)
+            floor(k, s, 3, 0, w)
+
+        y_widen(0, 0, 2, vcopy)
+        y_widen(0, 2, 3, scopy)
+        y_widen(0, 3, 4, vcopy)
+        y_widen(1, 0, 2, scopy)
+        y_widen(1, 2, 3, scopy)
+        y_lay(0, 0, vscale)
+        y_widen(1, 3, 4, vcopy)
+        y_quant(0, 0)
+        x_lay(0, 0, vcopy)
+        y_lay(1, 0, vscale)
+        y_lay(0, 1, sscale)
+        x_lay(1, 0, vcopy)
         x_quant(0, 0)
+        y_quant(1, 0)
         x_quant(1, 0)
+        x_lay(1, 1, scopy)
         low_rank_weights()
         row_factors()
-        y_lay(0, 0)
-        y_lay(1, 0)
-        y_widen(0, 1)
-        thresholds()
-        y_quant(0, 0)
-        y_quant(1, 0)
-        cross(0, 0)
-        low_rank(0, 0)
-        x_lay(0, 1)
-        x_lay(1, 1)
-        evac(0, 0)
+        for i in range(3):
+            low_rank_bank(i)
+        x_lay(0, 1, vcopy)
+        widths()
+        y_lay(1, 1, sscale)
+        for t in range(4):
+            cross_and_lift(0, t)
+        y_quant(0, 1)
         x_quant(0, 1)
         x_quant(1, 1)
-        y_widen(1, 1)
-        cross(1, 0)
-        clip(0, 0)
-        low_rank(1, 0)
-        y_lay_scalar(1, 1)
-        y_lay_scalar(0, 1, range(2))
-        y_lay(0, 1, range(2, 4))
         y_quant(1, 1)
-        y_quant(0, 1)
-        evac(1, 0)
-        cross(0, 1)
-        s_lay(0, 0, 0, H, scopy)
-        clip(1, 0)
-        evac(0, 1)
-        low_rank(0, 1)
-        cross(1, 1)
-        s_quant(0, 0, 0, H)
-        exposure(0, 0)
-        clip(0, 1)
-        s_lay(1, 0, 0, H, scopy)
-        evac(1, 1)
-        low_rank(1, 1)
-        s_quant(1, 0, 0, H)
-        exposure(1, 0)
-        s_lay(0, 1, 0, H, scopy)
-        cap(1, 1, 0)
-        cap(1, 1, 1)
-        cap(1, 1, 2)
-        cap(1, 1, 3)
-        for t in range(4): floor(1, 1, t, 0, 256)
-        for t in range(4): floor(1, 1, t, 256, H)
-        store(0, False)
+
+        def lifts(u, ts=range(4)):
+            return [(cross_and_lift, u, t) for t in ts]
+
+        clamp_unit(0, lifts(1, [0, 1, 2]), lifts(1, [3]) + lifts(2, [0, 1]), lifts(2, [2, 3]), [])
+        s_lay(0, 0, 0, 512, scopy)
+        clamp_unit(1, lifts(3), lifts(4), [], [])
+        s_quant(0, 0, 0, 512)
+        s_lay(0, 1, 0, 512, scopy)
+        clamp_unit(2, lifts(5), [], [], [])
+        s_quant(0, 1, 0, 512)
+        s_lay(1, 0, 0, 256, scopy)
+        clamp_unit(3, [(exposure_wide, 0, 0), (exposure_wide, 1, 0)], [(exposure_wide, 2, 0), (store_wide, 0, 0, scopy)], [(store_wide, 1, 0, scopy), (exposure_wide, 3, 0)], [])
         s_lay(1, 1, 0, 256, scopy)
-        s_lay(1, 1, 256, 384, scopy)
-        s_quant(0, 1, 0, H)
-        exposure(0, 1)
-        s_lay(1, 1, 384, H, vcopy)
+        s_quant(1, 0, 0, 256)
+        clamp_unit(4, [(store_wide, 2, 0, scopy)], [(store_wide, 3, 0, scopy)], [], [])
+        s_lay(2, 0, 0, 256, scopy)
         s_quant(1, 1, 0, 256)
-        s_quant(1, 1, 256, H)
-        exposure(1, 1)
-        store(1, True)
+        exposure_narrow((0, 1), 512, 768)
+        exposure_narrow((2, 3), 512, 768)
+        for lo in (0, 128):
+            for t in range(4):
+                cap(2, 1, t, lo, lo + 128)
+            for t in range(4):
+                floor(2, 1, t, lo, lo + 128)
+            if lo == 0:
+                store_narrow((0, 1), 512, 768, scopy)
+                s_lay(2, 1, 0, 128, scopy)
+                store_narrow((2, 3), 512, 768, scopy)
+                s_quant(2, 0, 0, 256)
+        s_quant(2, 1, 0, 128)
+        s_lay(2, 1, 128, 256, vcopy)
+        exposure_narrow((0, 1, 2, 3), 768, 896)
+        s_quant(2, 1, 128, 256)
+        store_narrow((0, 1, 2, 3), 768, 896, scopy)
+        exposure_narrow((0, 1), 896, 1024, "o", 2)
+        exposure_narrow((2, 3), 896, 1024, "o", 2)
+        store_narrow((0, 1), 896, 1024, vcopy)
+        store_narrow((2, 3), 896, 1024, scopy)

@@ -18,7 +18,7 @@ T, N, J, K, P = 1024, 1024, 1024, 128, 512
 FLOPS = 2 * T * N * J + 2 * N * K * J + 2 * P * N * J
 BANK = 512
 BLOCK = 128
-CHUNKS = ((0, 512), (512, 256), (768, 256))
+CHUNKS = ((0, 512), (512, 256), (768, 128), (896, 128))
 
 
 def tile_lowrankplussoftthresholdedcrosscovarianc_d2p_kernel(
@@ -35,7 +35,7 @@ def tile_lowrankplussoftthresholdedcrosscovarianc_d2p_kernel(
         y_v = y_bytes.rearrange("(q p j) n -> q p (j n)", q=2, p=128, j=4)
         both = [(q, h) for q in range(2) for h in range(2)]
 
-        x_raw = [keep.tile([128, 4, N], BF16, name=f"x_raw_{q}", align_bytes=64) for q in range(2)]
+        x_raw = {(q, s): keep.tile([128, 4, BANK], BF16, name=f"x_raw_{q}{s}", align_bytes=64) for q, s in both}
         y_raw = {(q, h): keep.tile([128, 2 * J], U8, name=f"y_raw_{q}{h}", align_bytes=64) for q, h in both}
         y_wide = [keep.tile([128, 4, J], BF16, name=f"y_wide_{q}", align_bytes=64) for q in range(2)]
         x_laid = {(q, s): keep.tile([128, 4 * BANK], BF16, name=f"x_laid_{q}{s}", align_bytes=64) for q, s in both}
@@ -46,6 +46,7 @@ def tile_lowrankplussoftthresholdedcrosscovarianc_d2p_kernel(
         y_sc = [keep.tile([128, J], U8, name=f"y_sc_{q}", align_bytes=64) for q in range(2)]
         s_code = [keep.tile([128, J], U32, name=f"s_code_{s}", align_bytes=64) for s in range(2)]
         s_sc = [keep.tile([128, J], U8, name=f"s_sc_{s}", align_bytes=64) for s in range(2)]
+        c_up = {(h, s, t): keep.tile([128, BANK], F32, name=f"c_up_{h}{s}{t}") for h, s in both for t in range(4)}
         l_sb = keep.tile([128, 2, 4, K], BF16, name="l_sb")
         m_sb = keep.tile([K, J], BF16, name="m_sb")
         l_t = keep.tile([K, 8, 128], BF16, name="l_t")
@@ -61,14 +62,24 @@ def tile_lowrankplussoftthresholdedcrosscovarianc_d2p_kernel(
         w_code = keep.tile([128, 2, 2 * P], U8, name="w_code", align_bytes=64)
         w_sc = keep.tile([128, 2, P], U8, name="w_sc", align_bytes=64)
 
-        for q, h in both:
+        def load_y(q, h):
             nc.sync.dma_start(out=y_raw[q, h][:], in_=y_v[q][:, 2 * J * h : 2 * J * (h + 1)])
-        for q in range(2):
-            nc.sync.dma_start(out=x_raw[q][:], in_=x_v[q])
+
+        def load_x(q, s):
+            nc.sync.dma_start(out=x_raw[q, s][:], in_=x_v[q][:, :, BANK * s : BANK * (s + 1)])
+
+        load_y(0, 0)
+        load_y(0, 1)
+        load_x(0, 0)
+        load_y(1, 0)
+        load_y(1, 1)
+        load_x(1, 0)
         nc.sync.dma_start(out=l_sb[:], in_=l.rearrange("(s p t) k -> p s t k", s=2, p=128, t=4))
         nc.sync.dma_start(out=m_sb[:], in_=m)
         nc.sync.dma_start(out=g_b[:].rearrange("p (s t) -> p s t", s=2), in_=g.rearrange("(s p t) -> p s t", s=2, p=128, t=4))
         nc.sync.dma_start(out=t_b[:].rearrange("p (s t) -> p s t", s=2), in_=tau.rearrange("(s p t) -> p s t", s=2, p=128, t=4))
+        load_x(0, 1)
+        load_x(1, 1)
         nc.sync.dma_start(out=w_code[:].bitcast(I32), in_=w_words.bitcast(I32).rearrange("s p n -> p s n"))
         nc.gpsimd.memset(w_sc[:].bitcast(I32), 0)
         for i in range(4):
@@ -91,9 +102,10 @@ def tile_lowrankplussoftthresholdedcrosscovarianc_d2p_kernel(
         def sscale(out, in_, scale):
             nc.scalar.activation(out=out, in_=in_, func=ACT.Copy, scale=scale)
 
-        def y_widen(q, lo, hi, copy):
-            src = y_raw[q, lo // 2][:, (lo % 2) * J : (lo % 2 + hi - lo) * J]
-            copy(out=y_wide[q][:, lo:hi, :].rearrange("p j n -> p (j n)"), in_=src.bitcast(FP8))
+        def y_widen(q, rows, h, copy):
+            for j in rows:
+                lo = (j % 2) * J + BANK * h
+                copy(out=y_wide[q][:, j, BANK * h : BANK * (h + 1)], in_=y_raw[q, j // 2][:, lo : lo + BANK].bitcast(FP8))
 
         def y_lay(q, h, scaled_copy, blocks=range(4)):
             for b in blocks:
@@ -110,20 +122,39 @@ def tile_lowrankplussoftthresholdedcrosscovarianc_d2p_kernel(
                 out=y_code[q][:, cols].bitcast(FP8X4), scales=y_sc[q][:, cols], in_=y_laid[q, h][:].rearrange("p n j -> p (n j)")
             )
 
-        def x_lay(q, s, copy, lo=0, hi=64):
+        def x_lay(q, s, copy):
             dst = x_laid[q, s][:].rearrange("p (t r e j) -> p r t e j", t=4, e=2, j=4)
-            src = x_raw[q][:, :, BANK * s : BANK * (s + 1)].rearrange("p j (r e t) -> p r t e j", e=2, t=4)
-            copy(out=dst[:, lo:hi], in_=src[:, lo:hi])
+            src = x_raw[q, s][:].rearrange("p j (r e t) -> p r t e j", e=2, t=4)
+            copy(out=dst, in_=src)
+
+        def x_slot(q, s, t):
+            return x_raw[q, s][:].rearrange("p j (r t) -> p t r j", t=4)[:, t]
+
+        def x_lay_slot(q, s, t, copy):
+            copy(out=x_laid[q, s][:, BANK * t : BANK * (t + 1)].rearrange("p (r j) -> p r j", j=4), in_=x_slot(q, s, t))
+
+        x_ps = {}
+
+        def x_pass(q, s, ts):
+            ps = psum.tile([128, 2 * BANK], BF16, name="ps_x", tag="c", bufs=3)
+            x_ps[q, s, ts[0]] = ps
+            for i, t in enumerate(ts):
+                nc.tensor.matmul(
+                    ps[:, BANK * i : BANK * (i + 1)].rearrange("p (r j) -> p r j", j=4), ident[:], x_slot(q, s, t), start=True, stop=True
+                )
+
+        def x_fetch(q, s, ts, copy):
+            copy(out=x_laid[q, s][:, BANK * ts[0] : BANK * (ts[-1] + 1)], in_=x_ps[q, s, ts[0]][:, : BANK * len(ts)])
 
         def x_quant(q, s):
             nc.vector.quantize_mx(out=x_code[q, s][:].bitcast(FP8X4), scales=x_sc[q, s][:], in_=x_laid[q, s][:])
 
         def low_rank_weights():
+            ps = psum.tile([128, 2 * BANK], BF16, name="ps_l", tag="o", bufs=2)
             for s in range(2):
-                ps = psum.tile([128, BANK], BF16, name="ps_l", tag="o", bufs=2)
                 for t in range(4):
-                    nc.tensor.transpose(ps[:, 128 * t : 128 * t + 128], l_sb[:, s, t, :], ident[:])
-                scopy(out=l_t[:, 4 * s : 4 * s + 4, :].rearrange("p t n -> p (t n)"), in_=ps[:])
+                    nc.tensor.transpose(ps[:, 128 * (4 * s + t) : 128 * (4 * s + t + 1)], l_sb[:, s, t, :], ident[:])
+            scopy(out=l_t[:].rearrange("p t n -> p (t n)"), in_=ps[:])
 
         def row_factors():
             nc.scalar.activation(out=g_f[:], in_=g_b[:], func=ACT.Copy)
@@ -134,7 +165,7 @@ def tile_lowrankplussoftthresholdedcrosscovarianc_d2p_kernel(
             nc.vector.tensor_tensor(out=width[:], in0=g_abs[:], in1=t_b[:], op=ALU.mult)
             nc.vector.scalar_tensor_tensor(out=width2[:], in0=t_b[:], scalar=2.0, in1=g_abs[:], op0=ALU.mult, op1=ALU.mult)
 
-        c_ps, f_ps, c_up, capped, sig, sig_laid, o_ps = {}, {}, {}, {}, {}, {}, {}
+        f_ps, capped, sig, sig_laid, o_ps = {}, {}, {}, {}, {}
 
         def slot(store, tag, bufs, k, s, t):
             w = CHUNKS[k][1]
@@ -148,56 +179,56 @@ def tile_lowrankplussoftthresholdedcrosscovarianc_d2p_kernel(
             per = BANK // w
             return store[k, s, t // per][:, w * (t % per) : w * (t % per + 1)]
 
-        def cross(k, s, t):
-            lo, w = CHUNKS[k]
-            ps = slot(c_ps, "c", 3, k, s, t)
+        def cross_and_lift(h, s, t):
+            cols = slice(BANK * h, BANK * (h + 1))
+            ps = psum.tile([128, BANK], F32, name="ps_c", tag="c", bufs=3)
             for q in range(2):
                 nc.tensor.matmul_mx(
-                    out=ps,
+                    out=ps[:],
                     lhsT=x_code[q, s][:, 128 * t : 128 * t + 128].bitcast(FP8X4),
                     lhsT_scale=x_sc[q, s][:, 128 * t : 128 * t + 128],
-                    rhs=y_code[q][:, lo : lo + w].bitcast(FP8X4),
-                    rhs_scale=y_sc[q][:, lo : lo + w],
+                    rhs=y_code[q][:, cols].bitcast(FP8X4),
+                    rhs_scale=y_sc[q][:, cols],
                     start=(q == 0),
                     stop=(q == 1),
                 )
+            col = slice(4 * s + t, 4 * s + t + 1)
+            nc.scalar.activation(out=c_up[h, s, t][:], in_=ps[:], func=ACT.Identity, scale=g_c[:, col], bias=width[:, col])
+
+        def upper(k, s, t):
+            lo, w = CHUNKS[k]
+            return c_up[lo // BANK, s, t][:, lo % BANK : lo % BANK + w]
 
         def low_rank(k, s, t):
             lo, w = CHUNKS[k]
             nc.tensor.matmul(slot(f_ps, "f", 3, k, s, t), l_t[:, 4 * s + t, :], m_sb[:, lo : lo + w], start=True, stop=True)
 
-        def lift(k, s, t):
-            col = slice(4 * s + t, 4 * s + t + 1)
-            c_up[k, s, t] = work.tile([128, CHUNKS[k][1]], F32, name=f"c_up_{k}{s}{t}", bufs=1)
-            nc.scalar.activation(out=c_up[k, s, t][:], in_=at(c_ps, k, s, t), func=ACT.Identity, scale=g_c[:, col], bias=width[:, col])
-
-        def cap(k, s, t, lo, hi):
-            if lo == 0:
-                capped[k, s, t] = work.tile([128, CHUNKS[k][1]], F32, name="capped", bufs=4)
+        def cap(k, s, t):
+            capped[k, s, t] = work.tile([128, CHUNKS[k][1]], F32, name="capped", bufs=4)
             nc.vector.scalar_tensor_tensor(
-                out=capped[k, s, t][:, lo:hi],
-                in0=at(f_ps, k, s, t)[:, lo:hi],
+                out=capped[k, s, t][:],
+                in0=at(f_ps, k, s, t),
                 scalar=g_f[:, 4 * s + t : 4 * s + t + 1],
-                in1=c_up[k, s, t][:, lo:hi],
+                in1=upper(k, s, t),
                 op0=ALU.mult,
                 op1=ALU.min,
             )
 
-        def floor(k, s, t, lo, hi):
-            if t == 0 and lo == 0:
-                sig[k, s] = work.tile([128, 4, CHUNKS[k][1]], BF16, name="sig", bufs=3, align_bytes=64)
+        def floor(k, s, t):
+            if t == 0:
+                sig[k, s] = work.tile([128, 4, CHUNKS[k][1]], BF16, name="sig", bufs=4, align_bytes=64)
             nc.vector.scalar_tensor_tensor(
-                out=sig[k, s][:, t, lo:hi],
-                in0=c_up[k, s, t][:, lo:hi],
+                out=sig[k, s][:, t, :],
+                in0=upper(k, s, t),
                 scalar=width2[:, 4 * s + t : 4 * s + t + 1],
-                in1=capped[k, s, t][:, lo:hi],
+                in1=capped[k, s, t][:],
                 op0=ALU.subtract,
                 op1=ALU.max,
             )
 
         def s_lay(k, s, lo, hi, copy):
             if lo == 0:
-                sig_laid[k, s] = work.tile([128, CHUNKS[k][1], 4], BF16, name="sig_laid", bufs=3, align_bytes=64)
+                sig_laid[k, s] = work.tile([128, CHUNKS[k][1], 4], BF16, name="sig_laid", bufs=4, align_bytes=64)
             copy(
                 out=sig_laid[k, s][:, lo:hi, :].rearrange("p (c i) t -> p c t i", i=4),
                 in_=sig[k, s][:, :, lo:hi].rearrange("p t (c i) -> p c t i", i=4),
@@ -211,36 +242,23 @@ def tile_lowrankplussoftthresholdedcrosscovarianc_d2p_kernel(
                 in_=sig_laid[k, s][:, lo:hi, :].rearrange("p n t -> p (n t)"),
             )
 
-        def exposure_group(ps, b, lo, hi):
-            for s in range(2):
+        def exposure(s, bs, lo, hi, tag="c", bufs=3):
+            if s == 0:
+                o_ps[bs[0], lo] = psum.tile([128, BANK], F32, name="ps_o", tag=tag, bufs=bufs)
+            step = BANK if hi - lo == BANK else BLOCK
+            parts = [(b, c) for b in bs for c in range(lo, hi, step)]
+            for i, (b, c) in enumerate(parts):
                 nc.tensor.matmul_mx(
-                    out=ps,
+                    out=o_ps[bs[0], lo][:, step * i : step * (i + 1)],
                     lhsT=w_code[:, s, 256 * b : 256 * b + 256].bitcast(FP4X4),
                     lhsT_scale=w_sc[:, s, 128 * b : 128 * b + 128],
-                    rhs=s_code[s][:, lo:hi].bitcast(FP8X4),
-                    rhs_scale=s_sc[s][:, lo:hi],
-                    start=(s == 0),
-                    stop=(s == 1),
+                    rhs=s_code[s][:, c : c + step].bitcast(FP8X4),
+                    rhs_scale=s_sc[s][:, c : c + step],
+                    start=(s == 0 and i == 0),
+                    stop=(s == 1 and i == len(parts) - 1),
                 )
 
-        def exposure_wide(b, lo):
-            o_ps[b, lo] = psum.tile([128, BANK], F32, name="ps_o", tag="o", bufs=2)
-            exposure_group(o_ps[b, lo][:], b, lo, lo + BANK)
-
-        def store_wide(b, lo, copy):
-            o_sb = work.tile([128, BANK], F32, name="o_sb", bufs=8)
-            copy(out=o_sb[:], in_=o_ps[b, lo][:])
-            nc.sync.dma_start(out=out[128 * b : 128 * b + 128, lo : lo + BANK], in_=o_sb[:])
-
-        def exposure_narrow(bs, lo, hi, tag="c", bufs=3):
-            ps = psum.tile([128, BANK], F32, name="ps_o", tag=tag, bufs=bufs)
-            o_ps[bs[0], lo] = ps
-            for i, b in enumerate(bs):
-                for c in range(lo, hi, BLOCK):
-                    at_col = i * (hi - lo) + c - lo
-                    exposure_group(ps[:, at_col : at_col + BLOCK], b, c, c + BLOCK)
-
-        def store_narrow(bs, lo, hi, copy):
+        def store(bs, lo, hi, copy):
             n = len(bs) * (hi - lo)
             o_sb = work.tile([128, BANK], F32, name="o_sb", bufs=8)
             copy(out=o_sb[:, :n], in_=o_ps[bs[0], lo][:, :n])
@@ -259,90 +277,94 @@ def tile_lowrankplussoftthresholdedcrosscovarianc_d2p_kernel(
                 for tile in f_banks[i]:
                     low_rank(*tile)
 
-        def cross_and_lift(u, t):
-            cross(*units[u], t)
-            if (t + 1) % per_bank[u] == 0:
-                for a in range(t + 1 - per_bank[u], t + 1):
-                    lift(*units[u], a)
-
         def clamp_unit(u, *beside):
             k, s = units[u]
-            w = CHUNKS[k][1]
+            lag = per_bank[u]
             for t in range(4):
-                cap(k, s, t, 0, w)
-                if t > 0:
-                    floor(k, s, t - 1, 0, w)
+                if t % per_bank[u] == 0:
+                    low_rank_bank(f_banks.index([(k, s, a) for a in range(t, t + per_bank[u])]) + 2)
+                cap(k, s, t)
+                if t >= lag:
+                    floor(k, s, t - lag)
                 for step, *args in beside[t]:
                     step(*args)
-                if (t + 1) % per_bank[u] == 0:
-                    low_rank_bank(f_banks.index([(k, s, a) for a in range(t + 1 - per_bank[u], t + 1)]) + 3)
-            floor(k, s, 3, 0, w)
+            for t in range(4 - lag, 4):
+                floor(k, s, t)
 
-        y_widen(0, 0, 2, vcopy)
-        y_widen(0, 2, 3, scopy)
-        y_widen(0, 3, 4, vcopy)
-        y_widen(1, 0, 2, scopy)
-        y_widen(1, 2, 3, scopy)
+        def lifts(h, s, ts=range(4)):
+            return [(cross_and_lift, h, s, t) for t in ts]
+
+        y_widen(0, (0, 1, 2, 3), 0, vcopy)
+        y_widen(0, (0, 1, 2), 1, scopy)
+        y_widen(0, (3,), 1, vcopy)
         y_lay(0, 0, vscale)
-        y_widen(1, 3, 4, vcopy)
-        y_quant(0, 0)
+        y_lay(0, 1, sscale, (0, 1))
+        y_widen(1, (0, 1, 2, 3), 0, scopy)
         x_lay(0, 0, vcopy)
-        y_lay(1, 0, vscale)
-        y_lay(0, 1, sscale)
-        x_lay(1, 0, vcopy)
+        y_quant(0, 0)
         x_quant(0, 0)
-        y_quant(1, 0)
+        x_lay(1, 0, vcopy)
+        y_lay(0, 1, sscale, (2,))
+        y_lay(1, 0, sscale, (0, 1))
+        y_lay(1, 0, vscale, (2, 3))
         x_quant(1, 0)
-        x_lay(1, 1, scopy)
+        y_quant(1, 0)
         low_rank_weights()
         row_factors()
-        for i in range(3):
-            low_rank_bank(i)
+        low_rank_bank(0)
+        low_rank_bank(1)
+        y_lay(0, 1, sscale, (3,))
+        y_widen(1, (0, 1, 2, 3), 1, scopy)
         x_lay(0, 1, vcopy)
         widths()
-        y_lay(1, 1, sscale)
+        x_lay(1, 1, vcopy)
         for t in range(4):
-            cross_and_lift(0, t)
+            cross_and_lift(0, 0, t)
         y_quant(0, 1)
         x_quant(0, 1)
         x_quant(1, 1)
-        y_quant(1, 1)
+        y_lay(1, 1, sscale)
 
-        def lifts(u, ts=range(4)):
-            return [(cross_and_lift, u, t) for t in ts]
-
-        clamp_unit(0, lifts(1, [0, 1, 2]), lifts(1, [3]) + lifts(2, [0, 1]), lifts(2, [2, 3]), [])
-        s_lay(0, 0, 0, 512, scopy)
-        clamp_unit(1, lifts(3), lifts(4), [], [])
-        s_quant(0, 0, 0, 512)
+        every = (0, 1, 2, 3)
+        clamp_unit(0, lifts(0, 1, [0]), lifts(0, 1, [1]), lifts(0, 1, [2]) + [(y_quant, 1, 1)], lifts(0, 1, [3]) + lifts(1, 0, [0]))
+        clamp_unit(1, lifts(1, 0, [1, 2]), lifts(1, 0, [3]) + [(s_lay, 0, 0, 0, 512, scopy)], lifts(1, 1, [0, 1, 2]), lifts(1, 1, [3]))
         s_lay(0, 1, 0, 512, scopy)
-        clamp_unit(2, lifts(5), [], [], [])
-        s_quant(0, 1, 0, 512)
+        clamp_unit(2, [], [], [], [])
+        s_quant(0, 0, 0, 512)
         s_lay(1, 0, 0, 256, scopy)
-        clamp_unit(3, [(exposure_wide, 0, 0), (exposure_wide, 1, 0)], [(exposure_wide, 2, 0), (store_wide, 0, 0, scopy)], [(store_wide, 1, 0, scopy), (exposure_wide, 3, 0)], [])
+        for b in every:
+            exposure(0, (b,), 0, 512, *(("o", 2) if b < 2 else ("c", 3)))
+        clamp_unit(3, [], [], [], [])
+        s_quant(0, 1, 0, 512)
         s_lay(1, 1, 0, 256, scopy)
+        for b in every:
+            exposure(1, (b,), 0, 512)
+        clamp_unit(4, [], [], [], [])
+        for b in every:
+            store((b,), 0, 512, scopy)
         s_quant(1, 0, 0, 256)
-        clamp_unit(4, [(store_wide, 2, 0, scopy)], [(store_wide, 3, 0, scopy)], [], [])
-        s_lay(2, 0, 0, 256, scopy)
-        s_quant(1, 1, 0, 256)
-        exposure_narrow((0, 1), 512, 768)
-        exposure_narrow((2, 3), 512, 768)
-        for lo in (0, 128):
-            for t in range(4):
-                cap(2, 1, t, lo, lo + 128)
-            for t in range(4):
-                floor(2, 1, t, lo, lo + 128)
-            if lo == 0:
-                store_narrow((0, 1), 512, 768, scopy)
-                s_lay(2, 1, 0, 128, scopy)
-                store_narrow((2, 3), 512, 768, scopy)
-                s_quant(2, 0, 0, 256)
+        exposure(0, (0, 1), 512, 768)
+        exposure(0, (2, 3), 512, 768, "o", 2)
+        clamp_unit(5, [], [], [], [(s_quant, 1, 1, 0, 256)])
+        exposure(1, (0, 1), 512, 768)
+        exposure(1, (2, 3), 512, 768)
+        s_lay(2, 0, 0, 128, vcopy)
+        s_lay(2, 1, 0, 128, scopy)
+        store((0, 1), 512, 768, scopy)
+        store((2, 3), 512, 768, scopy)
+        clamp_unit(6, [], [], [], [(s_quant, 2, 0, 0, 128)])
         s_quant(2, 1, 0, 128)
-        s_lay(2, 1, 128, 256, vcopy)
-        exposure_narrow((0, 1, 2, 3), 768, 896)
-        s_quant(2, 1, 128, 256)
-        store_narrow((0, 1, 2, 3), 768, 896, scopy)
-        exposure_narrow((0, 1), 896, 1024, "o", 2)
-        exposure_narrow((2, 3), 896, 1024, "o", 2)
-        store_narrow((0, 1), 896, 1024, vcopy)
-        store_narrow((2, 3), 896, 1024, scopy)
+        exposure(0, every, 768, 896, "o", 2)
+        exposure(1, every, 768, 896)
+        s_lay(3, 0, 0, 128, scopy)
+        store(every, 768, 896, scopy)
+        clamp_unit(7, [], [], [], [])
+        s_quant(3, 0, 0, 128)
+        exposure(0, (0, 1), 896, 1024)
+        exposure(0, (2, 3), 896, 1024)
+        s_lay(3, 1, 0, 128, vcopy)
+        s_quant(3, 1, 0, 128)
+        exposure(1, (0, 1), 896, 1024)
+        exposure(1, (2, 3), 896, 1024)
+        store((0, 1), 896, 1024, vcopy)
+        store((2, 3), 896, 1024, scopy)

@@ -18,6 +18,7 @@ T, N, J, K, P = 1024, 1024, 1024, 128, 512
 FLOPS = 2 * T * N * J + 2 * N * K * J + 2 * P * N * J
 BANK = 512
 BLOCK = 128
+CAPS = ((0, 512), (512, 256), (768, 256))
 CHUNKS = ((0, 512), (512, 256), (768, 128), (896, 128))
 
 
@@ -47,6 +48,8 @@ def tile_lowrankplussoftthresholdedcrosscovarianc_d2p_kernel(
         s_code = [keep.tile([128, J], U32, name=f"s_code_{s}", align_bytes=64) for s in range(2)]
         s_sc = [keep.tile([128, J], U8, name=f"s_sc_{s}", align_bytes=64) for s in range(2)]
         c_up = {(h, s, t): keep.tile([128, BANK], F32, name=f"c_up_{h}{s}{t}") for h, s in both for t in range(4)}
+        capped_b = [keep.tile([128, 4, BANK], BF16, name=f"capped_b_{s}", align_bytes=64) for s in range(2)]
+        lower_b = [keep.tile([128, 4, BANK], BF16, name=f"lower_b_{s}", align_bytes=64) for s in range(2)]
         l_sb = keep.tile([128, 2, 4, K], BF16, name="l_sb")
         m_sb = keep.tile([K, J], BF16, name="m_sb")
         l_t = keep.tile([K, 8, 128], BF16, name="l_t")
@@ -101,6 +104,12 @@ def tile_lowrankplussoftthresholdedcrosscovarianc_d2p_kernel(
 
         def sscale(out, in_, scale):
             nc.scalar.activation(out=out, in_=in_, func=ACT.Copy, scale=scale)
+
+        def gscale(out, in_, scale):
+            nc.gpsimd.tensor_scalar(out=out, in0=in_, scalar1=scale, scalar2=0.0, op0=ALU.mult, op1=ALU.add)
+
+        def gcopy(out, in_):
+            gscale(out, in_, 1.0)
 
         def y_widen(q, rows, h, copy):
             for j in rows:
@@ -163,75 +172,120 @@ def tile_lowrankplussoftthresholdedcrosscovarianc_d2p_kernel(
 
         def widths():
             nc.vector.tensor_tensor(out=width[:], in0=g_abs[:], in1=t_b[:], op=ALU.mult)
-            nc.vector.scalar_tensor_tensor(out=width2[:], in0=t_b[:], scalar=2.0, in1=g_abs[:], op0=ALU.mult, op1=ALU.mult)
+            nc.vector.scalar_tensor_tensor(out=width2[:], in0=t_b[:], scalar=-2.0, in1=g_abs[:], op0=ALU.mult, op1=ALU.mult)
 
         f_ps, capped, sig, sig_laid, o_ps = {}, {}, {}, {}, {}
 
-        def slot(store, tag, bufs, k, s, t):
-            w = CHUNKS[k][1]
-            per = BANK // w
-            if t % per == 0:
-                store[k, s, t // per] = psum.tile([128, BANK], F32, name="ps_" + tag, tag=tag, bufs=bufs)
-            return store[k, s, t // per][:, w * (t % per) : w * (t % per + 1)]
+        c_ps = {}
 
-        def at(store, k, s, t):
-            w = CHUNKS[k][1]
-            per = BANK // w
-            return store[k, s, t // per][:, w * (t % per) : w * (t % per + 1)]
+        def cross_pass(h, s, t, q):
+            cols = slice(BANK * h, BANK * (h + 1))
+            if q == 0:
+                c_ps[h, s, t] = psum.tile([128, BANK], F32, name="ps_c", tag="c", bufs=3)
+            nc.tensor.matmul_mx(
+                out=c_ps[h, s, t][:],
+                lhsT=x_code[q, s][:, 128 * t : 128 * t + 128].bitcast(FP8X4),
+                lhsT_scale=x_sc[q, s][:, 128 * t : 128 * t + 128],
+                rhs=y_code[q][:, cols].bitcast(FP8X4),
+                rhs_scale=y_sc[q][:, cols],
+                start=(q == 0),
+                stop=(q == 1),
+            )
+
+        def lift(h, s, t):
+            col = slice(4 * s + t, 4 * s + t + 1)
+            nc.scalar.activation(out=c_up[h, s, t][:], in_=c_ps[h, s, t][:], func=ACT.Identity, scale=g_c[:, col], bias=width[:, col])
 
         def cross_and_lift(h, s, t):
-            cols = slice(BANK * h, BANK * (h + 1))
-            ps = psum.tile([128, BANK], F32, name="ps_c", tag="c", bufs=3)
-            for q in range(2):
-                nc.tensor.matmul_mx(
-                    out=ps[:],
-                    lhsT=x_code[q, s][:, 128 * t : 128 * t + 128].bitcast(FP8X4),
-                    lhsT_scale=x_sc[q, s][:, 128 * t : 128 * t + 128],
-                    rhs=y_code[q][:, cols].bitcast(FP8X4),
-                    rhs_scale=y_sc[q][:, cols],
-                    start=(q == 0),
-                    stop=(q == 1),
-                )
-            col = slice(4 * s + t, 4 * s + t + 1)
-            nc.scalar.activation(out=c_up[h, s, t][:], in_=ps[:], func=ACT.Identity, scale=g_c[:, col], bias=width[:, col])
+            cross_pass(h, s, t, 0)
+            cross_pass(h, s, t, 1)
+            lift(h, s, t)
 
-        def upper(k, s, t):
-            lo, w = CHUNKS[k]
-            return c_up[lo // BANK, s, t][:, lo % BANK : lo % BANK + w]
+        f_banks = [(k, s, range(lo, lo + BANK // w)) for k, (c0, w) in enumerate(CAPS) for s in range(2) for lo in range(0, 4, BANK // w)]
 
-        def low_rank(k, s, t):
-            lo, w = CHUNKS[k]
-            nc.tensor.matmul(slot(f_ps, "f", 3, k, s, t), l_t[:, 4 * s + t, :], m_sb[:, lo : lo + w], start=True, stop=True)
+        def low_rank(i):
+            if i < len(f_banks):
+                k, s, ts = f_banks[i]
+                lo, w = CAPS[k]
+                ps = psum.tile([128, BANK], F32, name="ps_f", tag="f", bufs=3)
+                for a, t in enumerate(ts):
+                    f_ps[k, s, t] = ps[:, w * a : w * (a + 1)]
+                    nc.tensor.matmul(f_ps[k, s, t], l_t[:, 4 * s + t, :], m_sb[:, lo : lo + w], start=True, stop=True)
 
         def cap(k, s, t):
-            capped[k, s, t] = work.tile([128, CHUNKS[k][1]], F32, name="capped", bufs=4)
+            lo, w = CAPS[k]
+            h, cols = lo // BANK, slice(lo % BANK, lo % BANK + w)
+            if t % (BANK // w) == 0:
+                low_rank(f_banks.index((k, s, range(t, t + BANK // w))) + 2)
+            if h == 0:
+                capped[s, t] = work.tile([128, BANK], F32, name="capped", bufs=4)
             nc.vector.scalar_tensor_tensor(
-                out=capped[k, s, t][:],
-                in0=at(f_ps, k, s, t),
+                out=capped[s, t][:] if h == 0 else capped_b[s][:, t, cols],
+                in0=f_ps[k, s, t],
                 scalar=g_f[:, 4 * s + t : 4 * s + t + 1],
-                in1=upper(k, s, t),
+                in1=c_up[h, s, t][:, cols],
                 op0=ALU.mult,
                 op1=ALU.min,
             )
 
-        def floor(k, s, t):
-            if t == 0:
-                sig[k, s] = work.tile([128, 4, CHUNKS[k][1]], BF16, name="sig", bufs=4, align_bytes=64)
-            nc.vector.scalar_tensor_tensor(
-                out=sig[k, s][:, t, :],
-                in0=upper(k, s, t),
-                scalar=width2[:, 4 * s + t : 4 * s + t + 1],
-                in1=capped[k, s, t][:],
-                op0=ALU.subtract,
-                op1=ALU.max,
+        def floors(k, s, *midway):
+            lo, w = CHUNKS[k]
+            h, cols = lo // BANK, slice(lo % BANK, lo % BANK + w)
+            sig[k, s] = work.tile([128, 4, w], BF16, name=f"sig_{k}{s}", bufs=1, align_bytes=64)
+            for t in range(4):
+                if t == 3:
+                    for step, *args in midway:
+                        step(*args)
+                nc.vector.scalar_tensor_tensor(
+                    out=sig[k, s][:, t, :],
+                    in0=c_up[h, s, t][:, cols],
+                    scalar=width2[:, 4 * s + t : 4 * s + t + 1],
+                    in1=capped[s, t][:],
+                    op0=ALU.add,
+                    op1=ALU.max,
+                )
+
+        def lower(k, s):
+            lo, w = CAPS[k]
+            cols = slice(lo % BANK, lo % BANK + w)
+            for t in range(4):
+                nc.scalar.activation(
+                    out=lower_b[s][:, t, cols], in_=c_up[1, s, t][:, cols], func=ACT.Identity, bias=width2[:, 4 * s + t : 4 * s + t + 1]
+                )
+
+        def floor_packed(k, s):
+            lo, w = CHUNKS[k]
+            cols = slice(lo % BANK, lo % BANK + w)
+            sig[k, s] = work.tile([128, 4, w], BF16, name=f"sig_{k}{s}", bufs=1, align_bytes=64)
+            nc.vector.tensor_tensor(out=sig[k, s][:], in0=capped_b[s][:, :, cols], in1=lower_b[s][:, :, cols], op=ALU.max)
+
+        def floor_laid(k, s):
+            lo, w = CHUNKS[k]
+            cols = slice(lo % BANK, lo % BANK + w)
+            sig_laid[k, s] = work.tile([128, w, 4], BF16, name=f"sig_laid_{k}{s}", bufs=1, align_bytes=64)
+            nc.vector.tensor_tensor(
+                out=sig_laid[k, s][:].rearrange("p (c i) t -> p c t i", i=4),
+                in0=capped_b[s][:, :, cols].rearrange("p t (c i) -> p c t i", i=4),
+                in1=lower_b[s][:, :, cols].rearrange("p t (c i) -> p c t i", i=4),
+                op=ALU.max,
             )
 
+        def caps(h, s, *beside):
+            for t in range(4):
+                cap(h, s, t)
+                for step, *args in beside[t] if beside else ():
+                    step(*args)
+
+        def lifts(h, s, ts=range(4)):
+            return [(cross_and_lift, h, s, t) for t in ts]
+
         def s_lay(k, s, lo, hi, copy):
-            if lo == 0:
-                sig_laid[k, s] = work.tile([128, CHUNKS[k][1], 4], BF16, name="sig_laid", bufs=4, align_bytes=64)
+            if (k, s) not in sig_laid:
+                sig_laid[k, s] = work.tile([128, CHUNKS[k][1], 4], BF16, name=f"sig_laid_{k}{s}", bufs=1, align_bytes=64)
+            run = 1 if copy is gcopy else 4
             copy(
-                out=sig_laid[k, s][:, lo:hi, :].rearrange("p (c i) t -> p c t i", i=4),
-                in_=sig[k, s][:, :, lo:hi].rearrange("p t (c i) -> p c t i", i=4),
+                out=sig_laid[k, s][:, lo:hi, :].rearrange("p (c i) t -> p c t i", i=run),
+                in_=sig[k, s][:, :, lo:hi].rearrange("p t (c i) -> p c t i", i=run),
             )
 
         def s_quant(k, s, lo, hi):
@@ -268,101 +322,96 @@ def tile_lowrankplussoftthresholdedcrosscovarianc_d2p_kernel(
             )
 
 
-        units = [(k, s) for k in range(len(CHUNKS)) for s in range(2)]
-        per_bank = [BANK // CHUNKS[k][1] for k, s in units]
-        f_banks = [[(k, s, t) for t in range(lo, lo + per)] for (k, s), per in zip(units, per_bank) for lo in range(0, 4, per)]
-
-        def low_rank_bank(i):
-            if i < len(f_banks):
-                for tile in f_banks[i]:
-                    low_rank(*tile)
-
-        def clamp_unit(u, *beside):
-            k, s = units[u]
-            lag = per_bank[u]
-            for t in range(4):
-                if t % per_bank[u] == 0:
-                    low_rank_bank(f_banks.index([(k, s, a) for a in range(t, t + per_bank[u])]) + 2)
-                cap(k, s, t)
-                if t >= lag:
-                    floor(k, s, t - lag)
-                for step, *args in beside[t]:
-                    step(*args)
-            for t in range(4 - lag, 4):
-                floor(k, s, t)
-
-        def lifts(h, s, ts=range(4)):
-            return [(cross_and_lift, h, s, t) for t in ts]
-
         y_widen(0, (0, 1, 2, 3), 0, vcopy)
-        y_widen(0, (0, 1, 2), 1, scopy)
-        y_widen(0, (3,), 1, vcopy)
+        y_widen(0, (0, 1, 2, 3), 1, scopy)
         y_lay(0, 0, vscale)
-        y_lay(0, 1, sscale, (0, 1))
+        y_lay(0, 1, sscale, (0,))
         y_widen(1, (0, 1, 2, 3), 0, scopy)
         x_lay(0, 0, vcopy)
         y_quant(0, 0)
-        x_quant(0, 0)
         x_lay(1, 0, vcopy)
-        y_lay(0, 1, sscale, (2,))
-        y_lay(1, 0, sscale, (0, 1))
-        y_lay(1, 0, vscale, (2, 3))
-        x_quant(1, 0)
-        y_quant(1, 0)
+        x_quant(0, 0)
+        y_lay(0, 1, sscale, (1,))
+        y_lay(1, 0, sscale, (0, 1, 2))
         low_rank_weights()
+        x_quant(1, 0)
+        y_lay(1, 0, vscale, (3,))
         row_factors()
-        low_rank_bank(0)
-        low_rank_bank(1)
-        y_lay(0, 1, sscale, (3,))
-        y_widen(1, (0, 1, 2, 3), 1, scopy)
         x_lay(0, 1, vcopy)
+        y_quant(1, 0)
+        for t in range(3):
+            cross_pass(0, 0, t, 0)
+        low_rank(0)
+        low_rank(1)
+        y_lay(0, 1, sscale, (2, 3))
+        y_widen(1, (0, 1), 1, scopy)
         widths()
         x_lay(1, 1, vcopy)
-        for t in range(4):
-            cross_and_lift(0, 0, t)
-        y_quant(0, 1)
+        for t in range(3):
+            cross_pass(0, 0, t, 1)
+            lift(0, 0, t)
+        cross_and_lift(0, 0, 3)
         x_quant(0, 1)
         x_quant(1, 1)
-        y_lay(1, 1, sscale)
+        y_widen(1, (2, 3), 1, scopy)
 
         every = (0, 1, 2, 3)
-        clamp_unit(0, lifts(0, 1, [0]), lifts(0, 1, [1]), lifts(0, 1, [2]) + [(y_quant, 1, 1)], lifts(0, 1, [3]) + lifts(1, 0, [0]))
-        clamp_unit(1, lifts(1, 0, [1, 2]), lifts(1, 0, [3]) + [(s_lay, 0, 0, 0, 512, scopy)], lifts(1, 1, [0, 1, 2]), lifts(1, 1, [3]))
-        s_lay(0, 1, 0, 512, scopy)
-        clamp_unit(2, [], [], [], [])
+        y_lay(1, 1, sscale)
+        caps(0, 0, [], lifts(0, 1, [0]), lifts(0, 1, [1]), lifts(0, 1, [2]))
+        y_quant(0, 1)
+        cross_and_lift(0, 1, 3)
+        floors(0, 0, (y_quant, 1, 1))
+        s_lay(0, 0, 0, 384, gcopy)
+        cross_and_lift(1, 0, 0)
+        s_lay(0, 0, 384, 512, scopy)
+        caps(0, 1, lifts(1, 0, [1]), lifts(1, 0, [2]), lifts(1, 0, [3]), lifts(1, 1, [0]))
+        for t in range(1, 4):
+            cross_and_lift(1, 1, t)
+        floors(0, 1)
+        s_lay(0, 1, 0, 416, gcopy)
+        caps(1, 0)
+        lower(1, 0)
+        s_lay(0, 1, 416, 512, scopy)
+        lower(1, 1)
+        caps(1, 1)
         s_quant(0, 0, 0, 512)
-        s_lay(1, 0, 0, 256, scopy)
         for b in every:
             exposure(0, (b,), 0, 512, *(("o", 2) if b < 2 else ("c", 3)))
-        clamp_unit(3, [], [], [], [])
+        floor_packed(1, 0)
         s_quant(0, 1, 0, 512)
-        s_lay(1, 1, 0, 256, scopy)
         for b in every:
             exposure(1, (b,), 0, 512)
-        clamp_unit(4, [], [], [], [])
-        for b in every:
-            store((b,), 0, 512, scopy)
+        floor_packed(1, 1)
+        s_lay(1, 1, 0, 256, gcopy)
+        s_lay(1, 0, 0, 256, scopy)
+        lower(2, 0)
+        store((0,), 0, 512, scopy)
+        store((1,), 0, 512, scopy)
+        lower(2, 1)
+        store((2,), 0, 512, scopy)
+        store((3,), 0, 512, scopy)
+        caps(2, 0)
+        caps(2, 1)
         s_quant(1, 0, 0, 256)
         exposure(0, (0, 1), 512, 768)
         exposure(0, (2, 3), 512, 768, "o", 2)
-        clamp_unit(5, [], [], [], [(s_quant, 1, 1, 0, 256)])
+        s_quant(1, 1, 0, 256)
         exposure(1, (0, 1), 512, 768)
         exposure(1, (2, 3), 512, 768)
-        s_lay(2, 0, 0, 128, vcopy)
-        s_lay(2, 1, 0, 128, scopy)
+        floor_laid(2, 0)
+        floor_laid(2, 1)
         store((0, 1), 512, 768, scopy)
         store((2, 3), 512, 768, scopy)
-        clamp_unit(6, [], [], [], [(s_quant, 2, 0, 0, 128)])
-        s_quant(2, 1, 0, 128)
+        s_quant(2, 0, 0, 128)
         exposure(0, every, 768, 896, "o", 2)
+        floor_laid(3, 0)
+        s_quant(2, 1, 0, 128)
         exposure(1, every, 768, 896)
-        s_lay(3, 0, 0, 128, scopy)
         store(every, 768, 896, scopy)
-        clamp_unit(7, [], [], [], [])
+        floor_laid(3, 1)
         s_quant(3, 0, 0, 128)
         exposure(0, (0, 1), 896, 1024)
         exposure(0, (2, 3), 896, 1024)
-        s_lay(3, 1, 0, 128, vcopy)
         s_quant(3, 1, 0, 128)
         exposure(1, (0, 1), 896, 1024)
         exposure(1, (2, 3), 896, 1024)

@@ -18,6 +18,7 @@ T, N, J, K, P = 1024, 1024, 1024, 128, 512
 FLOPS = 2 * T * N * J + 2 * N * K * J + 2 * P * N * J
 BANK = 512
 BLOCK = 128
+Y_LOADS = ((0, (0,)), (0, (1,)), (0, (2,)), (0, (3,)), (1, (0, 1)), (1, (2, 3)))
 CAPS = ((0, 512), (512, 256), (768, 256))
 CHUNKS = ((0, 512), (512, 256), (768, 128), (896, 128))
 
@@ -37,7 +38,7 @@ def tile_lowrankplussoftthresholdedcrosscovarianc_d2p_kernel(
         both = [(q, h) for q in range(2) for h in range(2)]
 
         x_raw = {(q, s): keep.tile([128, 4, BANK], BF16, name=f"x_raw_{q}{s}", align_bytes=64) for q, s in both}
-        y_raw = {(q, h): keep.tile([128, 2 * J], U8, name=f"y_raw_{q}{h}", align_bytes=64) for q, h in both}
+        y_raw = {(q, rows[0]): keep.tile([128, len(rows) * J], U8, name=f"y_raw_{q}{rows[0]}", align_bytes=64) for q, rows in Y_LOADS}
         y_wide = [keep.tile([128, 4, J], BF16, name=f"y_wide_{q}", align_bytes=64) for q in range(2)]
         x_laid = {(q, s): keep.tile([128, 4 * BANK], BF16, name=f"x_laid_{q}{s}", align_bytes=64) for q, s in both}
         y_laid = {(q, h): keep.tile([128, BANK, 4], BF16, name=f"y_laid_{q}{h}", align_bytes=64) for q, h in both}
@@ -65,23 +66,23 @@ def tile_lowrankplussoftthresholdedcrosscovarianc_d2p_kernel(
         w_code = keep.tile([128, 2, 2 * P], U8, name="w_code", align_bytes=64)
         w_sc = keep.tile([128, 2, P], U8, name="w_sc", align_bytes=64)
 
-        def load_y(q, h):
-            nc.sync.dma_start(out=y_raw[q, h][:], in_=y_v[q][:, 2 * J * h : 2 * J * (h + 1)])
+        def load_y(q):
+            for a, rows in Y_LOADS:
+                if a == q:
+                    nc.sync.dma_start(out=y_raw[q, rows[0]][:], in_=y_v[q][:, J * rows[0] : J * (rows[-1] + 1)])
 
         def load_x(q, s):
             nc.sync.dma_start(out=x_raw[q, s][:], in_=x_v[q][:, :, BANK * s : BANK * (s + 1)])
 
-        load_y(0, 0)
-        load_y(0, 1)
+        load_y(0)
         load_x(0, 0)
-        load_y(1, 0)
-        load_y(1, 1)
+        load_y(1)
         load_x(1, 0)
         nc.sync.dma_start(out=l_sb[:], in_=l.rearrange("(s p t) k -> p s t k", s=2, p=128, t=4))
+        load_x(0, 1)
         nc.sync.dma_start(out=m_sb[:], in_=m)
         nc.sync.dma_start(out=g_b[:].rearrange("p (s t) -> p s t", s=2), in_=g.rearrange("(s p t) -> p s t", s=2, p=128, t=4))
         nc.sync.dma_start(out=t_b[:].rearrange("p (s t) -> p s t", s=2), in_=tau.rearrange("(s p t) -> p s t", s=2, p=128, t=4))
-        load_x(0, 1)
         load_x(1, 1)
         nc.sync.dma_start(out=w_code[:].bitcast(I32), in_=w_words.bitcast(I32).rearrange("s p n -> p s n"))
         nc.gpsimd.memset(w_sc[:].bitcast(I32), 0)
@@ -90,10 +91,8 @@ def tile_lowrankplussoftthresholdedcrosscovarianc_d2p_kernel(
                 out=w_sc[32 * i : 32 * i + 4].bitcast(I32),
                 in_=w_scales[:, 4 * i : 4 * i + 4, :].bitcast(I32).rearrange("s r n -> r s n"),
             )
-        for i in range(4):
-            nc.scalar.dma_start(
-                out=y_fac[32 * i : 32 * i + 32], in_=y_scale.rearrange("(q i) b -> i q b", i=4)[i].partition_broadcast(32)
-            )
+        for q in range(2):
+            nc.scalar.dma_start(out=y_fac[:, q, :], in_=y_scale[4 * q : 4 * q + 4, :].unsqueeze(1).to_broadcast([4, 32, 8]))
         make_identity(nc, ident[:])
 
         vcopy = nc.vector.tensor_copy
@@ -113,8 +112,9 @@ def tile_lowrankplussoftthresholdedcrosscovarianc_d2p_kernel(
 
         def y_widen(q, rows, h, copy):
             for j in rows:
-                lo = (j % 2) * J + BANK * h
-                copy(out=y_wide[q][:, j, BANK * h : BANK * (h + 1)], in_=y_raw[q, j // 2][:, lo : lo + BANK].bitcast(FP8))
+                first = max(r[0] for a, r in Y_LOADS if a == q and r[0] <= j)
+                lo = (j - first) * J + BANK * h
+                copy(out=y_wide[q][:, j, BANK * h : BANK * (h + 1)], in_=y_raw[q, first][:, lo : lo + BANK].bitcast(FP8))
 
         def y_lay(q, h, scaled_copy, blocks=range(4)):
             for b in blocks:
@@ -178,10 +178,10 @@ def tile_lowrankplussoftthresholdedcrosscovarianc_d2p_kernel(
 
         c_ps = {}
 
-        def cross_pass(h, s, t, q):
+        def cross_pass(h, s, t, q, tag="c", bufs=3):
             cols = slice(BANK * h, BANK * (h + 1))
             if q == 0:
-                c_ps[h, s, t] = psum.tile([128, BANK], F32, name="ps_c", tag="c", bufs=3)
+                c_ps[h, s, t] = psum.tile([128, BANK], F32, name="ps_c", tag=tag, bufs=bufs)
             nc.tensor.matmul_mx(
                 out=c_ps[h, s, t][:],
                 lhsT=x_code[q, s][:, 128 * t : 128 * t + 128].bitcast(FP8X4),
@@ -196,18 +196,18 @@ def tile_lowrankplussoftthresholdedcrosscovarianc_d2p_kernel(
             col = slice(4 * s + t, 4 * s + t + 1)
             nc.scalar.activation(out=c_up[h, s, t][:], in_=c_ps[h, s, t][:], func=ACT.Identity, scale=g_c[:, col], bias=width[:, col])
 
-        def cross_and_lift(h, s, t):
-            cross_pass(h, s, t, 0)
+        def cross_and_lift(h, s, t, *bank):
+            cross_pass(h, s, t, 0, *bank)
             cross_pass(h, s, t, 1)
             lift(h, s, t)
 
         f_banks = [(k, s, range(lo, lo + BANK // w)) for k, (c0, w) in enumerate(CAPS) for s in range(2) for lo in range(0, 4, BANK // w)]
 
-        def low_rank(i):
-            if i < len(f_banks):
+        def low_rank(banks, tag="f", bufs=3):
+            for i in banks:
                 k, s, ts = f_banks[i]
                 lo, w = CAPS[k]
-                ps = psum.tile([128, BANK], F32, name="ps_f", tag="f", bufs=3)
+                ps = psum.tile([128, BANK], F32, name="ps_f", tag=tag, bufs=bufs)
                 for a, t in enumerate(ts):
                     f_ps[k, s, t] = ps[:, w * a : w * (a + 1)]
                     nc.tensor.matmul(f_ps[k, s, t], l_t[:, 4 * s + t, :], m_sb[:, lo : lo + w], start=True, stop=True)
@@ -215,8 +215,6 @@ def tile_lowrankplussoftthresholdedcrosscovarianc_d2p_kernel(
         def cap(k, s, t):
             lo, w = CAPS[k]
             h, cols = lo // BANK, slice(lo % BANK, lo % BANK + w)
-            if t % (BANK // w) == 0:
-                low_rank(f_banks.index((k, s, range(t, t + BANK // w))) + 2)
             if h == 0:
                 capped[s, t] = work.tile([128, BANK], F32, name="capped", bufs=4)
             nc.vector.scalar_tensor_tensor(
@@ -323,27 +321,26 @@ def tile_lowrankplussoftthresholdedcrosscovarianc_d2p_kernel(
 
 
         y_widen(0, (0, 1, 2, 3), 0, vcopy)
-        y_widen(0, (0, 1, 2, 3), 1, scopy)
+        y_widen(0, (3,), 1, vcopy)
+        y_widen(0, (0, 1, 2), 1, scopy)
         y_lay(0, 0, vscale)
-        y_lay(0, 1, sscale, (0,))
+        y_lay(0, 1, sscale, (0, 1))
         y_widen(1, (0, 1, 2, 3), 0, scopy)
         x_lay(0, 0, vcopy)
         y_quant(0, 0)
         x_lay(1, 0, vcopy)
         x_quant(0, 0)
-        y_lay(0, 1, sscale, (1,))
-        y_lay(1, 0, sscale, (0, 1, 2))
+        y_lay(0, 1, sscale, (2,))
+        y_lay(1, 0, sscale, (0, 1, 2, 3))
         low_rank_weights()
         x_quant(1, 0)
-        y_lay(1, 0, vscale, (3,))
         row_factors()
         x_lay(0, 1, vcopy)
         y_quant(1, 0)
         for t in range(3):
             cross_pass(0, 0, t, 0)
-        low_rank(0)
-        low_rank(1)
-        y_lay(0, 1, sscale, (2, 3))
+        low_rank((0, 1))
+        y_lay(0, 1, sscale, (3,))
         y_widen(1, (0, 1), 1, scopy)
         widths()
         x_lay(1, 1, vcopy)
@@ -351,6 +348,8 @@ def tile_lowrankplussoftthresholdedcrosscovarianc_d2p_kernel(
             cross_pass(0, 0, t, 1)
             lift(0, 0, t)
         cross_and_lift(0, 0, 3)
+        low_rank((2,))
+        low_rank((3, 4), "o", 2)
         x_quant(0, 1)
         x_quant(1, 1)
         y_widen(1, (2, 3), 1, scopy)
@@ -359,22 +358,25 @@ def tile_lowrankplussoftthresholdedcrosscovarianc_d2p_kernel(
         y_lay(1, 1, sscale)
         caps(0, 0, [], lifts(0, 1, [0]), lifts(0, 1, [1]), lifts(0, 1, [2]))
         y_quant(0, 1)
-        cross_and_lift(0, 1, 3)
+        cross_and_lift(0, 1, 3, "o", 2)
+        low_rank((5, 6, 7))
         floors(0, 0, (y_quant, 1, 1))
         s_lay(0, 0, 0, 384, gcopy)
         cross_and_lift(1, 0, 0)
         s_lay(0, 0, 384, 512, scopy)
-        caps(0, 1, lifts(1, 0, [1]), lifts(1, 0, [2]), lifts(1, 0, [3]), lifts(1, 1, [0]))
+        caps(0, 1, lifts(1, 0, [1]), lifts(1, 0, [2]) + [(low_rank, (8,), "o", 2)], lifts(1, 0, [3]) + [(low_rank, (9,), "o", 2)], lifts(1, 1, [0]))
         for t in range(1, 4):
             cross_and_lift(1, 1, t)
+            low_rank((9 + t,))
         floors(0, 1)
         s_lay(0, 1, 0, 416, gcopy)
         caps(1, 0)
         lower(1, 0)
-        s_lay(0, 1, 416, 512, scopy)
         lower(1, 1)
         caps(1, 1)
+        low_rank((13, 14))
         s_quant(0, 0, 0, 512)
+        s_lay(0, 1, 416, 512, vcopy)
         for b in every:
             exposure(0, (b,), 0, 512, *(("o", 2) if b < 2 else ("c", 3)))
         floor_packed(1, 0)
@@ -386,29 +388,31 @@ def tile_lowrankplussoftthresholdedcrosscovarianc_d2p_kernel(
         s_lay(1, 0, 0, 256, scopy)
         lower(2, 0)
         store((0,), 0, 512, scopy)
-        store((1,), 0, 512, scopy)
         lower(2, 1)
+        store((1,), 0, 512, scopy)
         store((2,), 0, 512, scopy)
         store((3,), 0, 512, scopy)
-        caps(2, 0)
-        caps(2, 1)
-        s_quant(1, 0, 0, 256)
+        caps(2, 0, [], [(low_rank, (15,))], [], [])
+        caps(2, 1, [], [(s_quant, 1, 0, 0, 256), (s_quant, 1, 1, 0, 256)], [], [])
         exposure(0, (0, 1), 512, 768)
-        exposure(0, (2, 3), 512, 768, "o", 2)
-        s_quant(1, 1, 0, 256)
         exposure(1, (0, 1), 512, 768)
+        exposure(0, (2, 3), 512, 768, "o", 2)
         exposure(1, (2, 3), 512, 768)
-        floor_laid(2, 0)
-        floor_laid(2, 1)
+        floor_packed(2, 0)
+        floor_packed(2, 1)
         store((0, 1), 512, 768, scopy)
         store((2, 3), 512, 768, scopy)
+        s_lay(2, 0, 0, 128, vcopy)
+        s_lay(2, 1, 0, 128, vcopy)
         s_quant(2, 0, 0, 128)
         exposure(0, every, 768, 896, "o", 2)
-        floor_laid(3, 0)
+        floor_packed(3, 0)
         s_quant(2, 1, 0, 128)
         exposure(1, every, 768, 896)
         store(every, 768, 896, scopy)
-        floor_laid(3, 1)
+        floor_packed(3, 1)
+        s_lay(3, 0, 0, 128, vcopy)
+        s_lay(3, 1, 0, 128, vcopy)
         s_quant(3, 0, 0, 128)
         exposure(0, (0, 1), 896, 1024)
         exposure(0, (2, 3), 896, 1024)

@@ -19,6 +19,7 @@ FLOPS = 2 * T * N * J + 2 * N * K * J + 2 * P * N * J
 BANK = 512
 BLOCK = 128
 Y_LOADS = ((0, (0,)), (0, (1,)), (0, (2,)), (0, (3,)), (1, (0, 1)), (1, (2, 3)))
+G00, G01 = 384, 464
 CAPS = ((0, 512), (512, 256), (768, 256))
 CHUNKS = ((0, 512), (512, 256), (768, 128), (896, 128))
 
@@ -215,10 +216,10 @@ def tile_lowrankplussoftthresholdedcrosscovarianc_d2p_kernel(
         def cap(k, s, t):
             lo, w = CAPS[k]
             h, cols = lo // BANK, slice(lo % BANK, lo % BANK + w)
-            if h == 0:
+            if (h, s) == (0, 1):
                 capped[s, t] = work.tile([128, BANK], F32, name="capped", bufs=4)
             nc.vector.scalar_tensor_tensor(
-                out=capped[s, t][:] if h == 0 else capped_b[s][:, t, cols],
+                out=capped[s, t][:] if (h, s) == (0, 1) else capped_b[s][:, t, cols],
                 in0=f_ps[k, s, t],
                 scalar=g_f[:, 4 * s + t : 4 * s + t + 1],
                 in1=c_up[h, s, t][:, cols],
@@ -243,13 +244,17 @@ def tile_lowrankplussoftthresholdedcrosscovarianc_d2p_kernel(
                     op1=ALU.max,
                 )
 
-        def lower(k, s):
+        def sshift(out, in_, bias):
+            nc.scalar.activation(out=out, in_=in_, func=ACT.Identity, bias=bias)
+
+        def gshift(out, in_, bias):
+            nc.gpsimd.tensor_scalar(out=out, in0=in_, scalar1=1.0, scalar2=bias, op0=ALU.mult, op1=ALU.add)
+
+        def lower(k, s, ts=range(4), shift=sshift):
             lo, w = CAPS[k]
             cols = slice(lo % BANK, lo % BANK + w)
-            for t in range(4):
-                nc.scalar.activation(
-                    out=lower_b[s][:, t, cols], in_=c_up[1, s, t][:, cols], func=ACT.Identity, bias=width2[:, 4 * s + t : 4 * s + t + 1]
-                )
+            for t in ts:
+                shift(lower_b[s][:, t, cols], c_up[lo // BANK, s, t][:, cols], width2[:, 4 * s + t : 4 * s + t + 1])
 
         def floor_packed(k, s):
             lo, w = CHUNKS[k]
@@ -328,6 +333,7 @@ def tile_lowrankplussoftthresholdedcrosscovarianc_d2p_kernel(
         y_widen(1, (0, 1, 2, 3), 0, scopy)
         x_lay(0, 0, vcopy)
         y_quant(0, 0)
+        y_lay(0, 1, vscale, (3,))
         x_lay(1, 0, vcopy)
         x_quant(0, 0)
         y_lay(0, 1, sscale, (2,))
@@ -340,8 +346,7 @@ def tile_lowrankplussoftthresholdedcrosscovarianc_d2p_kernel(
         for t in range(3):
             cross_pass(0, 0, t, 0)
         low_rank((0, 1))
-        y_lay(0, 1, sscale, (3,))
-        y_widen(1, (0, 1), 1, scopy)
+        y_widen(1, (0, 1, 2), 1, scopy)
         widths()
         x_lay(1, 1, vcopy)
         for t in range(3):
@@ -352,44 +357,48 @@ def tile_lowrankplussoftthresholdedcrosscovarianc_d2p_kernel(
         low_rank((3, 4), "o", 2)
         x_quant(0, 1)
         x_quant(1, 1)
-        y_widen(1, (2, 3), 1, scopy)
+        y_widen(1, (3,), 1, scopy)
+        lower(0, 0, (0,))
+        lower(0, 0, (1, 2, 3), gshift)
 
         every = (0, 1, 2, 3)
-        y_lay(1, 1, sscale)
+        y_lay(1, 1, sscale, (0, 1))
         caps(0, 0, [], lifts(0, 1, [0]), lifts(0, 1, [1]), lifts(0, 1, [2]))
+        y_lay(1, 1, vscale, (2, 3))
         y_quant(0, 1)
         cross_and_lift(0, 1, 3, "o", 2)
         low_rank((5, 6, 7))
-        floors(0, 0, (y_quant, 1, 1))
-        s_lay(0, 0, 0, 384, gcopy)
+        y_quant(1, 1)
+        floor_packed(0, 0)
+        s_lay(0, 0, 0, G00, gcopy)
         cross_and_lift(1, 0, 0)
-        s_lay(0, 0, 384, 512, scopy)
         caps(0, 1, lifts(1, 0, [1]), lifts(1, 0, [2]) + [(low_rank, (8,), "o", 2)], lifts(1, 0, [3]) + [(low_rank, (9,), "o", 2)], lifts(1, 1, [0]))
+        s_lay(0, 0, G00, 512, scopy)
         for t in range(1, 4):
             cross_and_lift(1, 1, t)
             low_rank((9 + t,))
         floors(0, 1)
-        s_lay(0, 1, 0, 416, gcopy)
+        s_quant(0, 0, 0, 512)
+        s_lay(0, 1, 0, G01, gcopy)
         caps(1, 0)
         lower(1, 0)
         lower(1, 1)
+        for b in (2, 3, 0, 1):
+            exposure(0, (b,), 0, 512, *(("o", 2) if b < 2 else ("c", 3)))
         caps(1, 1)
         low_rank((13, 14))
-        s_quant(0, 0, 0, 512)
-        s_lay(0, 1, 416, 512, vcopy)
-        for b in every:
-            exposure(0, (b,), 0, 512, *(("o", 2) if b < 2 else ("c", 3)))
+        s_lay(0, 1, G01, 512, vcopy)
         floor_packed(1, 0)
         s_quant(0, 1, 0, 512)
         for b in every:
             exposure(1, (b,), 0, 512)
         floor_packed(1, 1)
         s_lay(1, 1, 0, 256, gcopy)
-        s_lay(1, 0, 0, 256, scopy)
         lower(2, 0)
+        s_lay(1, 0, 0, 256, scopy)
         store((0,), 0, 512, scopy)
-        lower(2, 1)
         store((1,), 0, 512, scopy)
+        lower(2, 1)
         store((2,), 0, 512, scopy)
         store((3,), 0, 512, scopy)
         caps(2, 0, [], [(low_rank, (15,))], [], [])
@@ -398,21 +407,17 @@ def tile_lowrankplussoftthresholdedcrosscovarianc_d2p_kernel(
         exposure(1, (0, 1), 512, 768)
         exposure(0, (2, 3), 512, 768, "o", 2)
         exposure(1, (2, 3), 512, 768)
-        floor_packed(2, 0)
-        floor_packed(2, 1)
+        floor_laid(2, 0)
+        floor_laid(2, 1)
         store((0, 1), 512, 768, scopy)
         store((2, 3), 512, 768, scopy)
-        s_lay(2, 0, 0, 128, vcopy)
-        s_lay(2, 1, 0, 128, vcopy)
         s_quant(2, 0, 0, 128)
         exposure(0, every, 768, 896, "o", 2)
-        floor_packed(3, 0)
         s_quant(2, 1, 0, 128)
         exposure(1, every, 768, 896)
         store(every, 768, 896, scopy)
-        floor_packed(3, 1)
-        s_lay(3, 0, 0, 128, vcopy)
-        s_lay(3, 1, 0, 128, vcopy)
+        floor_laid(3, 0)
+        floor_laid(3, 1)
         s_quant(3, 0, 0, 128)
         exposure(0, (0, 1), 896, 1024)
         exposure(0, (2, 3), 896, 1024)

@@ -16,12 +16,16 @@ ACT = mybir.ActivationFunctionType
 
 T, N, J, K, P = 1024, 1024, 1024, 128, 512
 FLOPS = 2 * T * N * J + 2 * N * K * J + 2 * P * N * J
+
 BANK = 512
 BLOCK = 128
+SLOTS = range(4)
+ROW_BLOCKS = range(4)
+CROSS, LOW, OUT = ("cross", 3), ("low", 3), ("out", 2)
 Y_LOADS = ((0, (0,)), (0, (1,)), (0, (2,)), (0, (3,)), (1, (0, 1)), (1, (2, 3)))
-G00, G01 = 384, 464
-CAPS = ((0, 512), (512, 256), (768, 256))
+CAP_SPANS = ((0, 512), (512, 256), (768, 256))
 CHUNKS = ((0, 512), (512, 256), (768, 128), (896, 128))
+GPSIMD_COLUMNS = (384, 464)
 
 
 def tile_lowrankplussoftthresholdedcrosscovarianc_d2p_kernel(
@@ -30,50 +34,56 @@ def tile_lowrankplussoftthresholdedcrosscovarianc_d2p_kernel(
     nc = tc.nc
     with ExitStack() as ctx:
         keep = ctx.enter_context(tc.tile_pool(name="keep", bufs=1))
-        work = ctx.enter_context(tc.tile_pool(name="work", bufs=2))
+        work = ctx.enter_context(tc.tile_pool(name="work", bufs=1))
         psum = ctx.enter_context(tc.psum_pool(name="psum", bufs=1))
         ctx.enter_context(tc.manual_schedule())
 
-        x_v = x.rearrange("(q p j) n -> q p j n", q=2, p=128, j=4)
-        y_v = y_bytes.rearrange("(q p j) n -> q p (j n)", q=2, p=128, j=4)
-        both = [(q, h) for q in range(2) for h in range(2)]
+        pairs = [(a, b) for a in range(2) for b in range(2)]
 
-        x_raw = {(q, s): keep.tile([128, 4, BANK], BF16, name=f"x_raw_{q}{s}", align_bytes=64) for q, s in both}
+        def tiles(name, shape, dtype, keys):
+            return {key: keep.tile(shape, dtype, name=f"{name}_{i}", align_bytes=64) for i, key in enumerate(keys)}
+
+        x_raw = tiles("x_raw", [128, 4, BANK], BF16, pairs)
         y_raw = {(q, rows[0]): keep.tile([128, len(rows) * J], U8, name=f"y_raw_{q}{rows[0]}", align_bytes=64) for q, rows in Y_LOADS}
-        y_wide = [keep.tile([128, 4, J], BF16, name=f"y_wide_{q}", align_bytes=64) for q in range(2)]
-        x_laid = {(q, s): keep.tile([128, 4 * BANK], BF16, name=f"x_laid_{q}{s}", align_bytes=64) for q, s in both}
-        y_laid = {(q, h): keep.tile([128, BANK, 4], BF16, name=f"y_laid_{q}{h}", align_bytes=64) for q, h in both}
-        x_code = {(q, s): keep.tile([128, BANK], U32, name=f"x_code_{q}{s}", align_bytes=64) for q, s in both}
-        x_sc = {(q, s): keep.tile([128, BANK], U8, name=f"x_sc_{q}{s}", align_bytes=64) for q, s in both}
-        y_code = [keep.tile([128, J], U32, name=f"y_code_{q}", align_bytes=64) for q in range(2)]
-        y_sc = [keep.tile([128, J], U8, name=f"y_sc_{q}", align_bytes=64) for q in range(2)]
-        s_code = [keep.tile([128, J], U32, name=f"s_code_{s}", align_bytes=64) for s in range(2)]
-        s_sc = [keep.tile([128, J], U8, name=f"s_sc_{s}", align_bytes=64) for s in range(2)]
-        c_up = {(h, s, t): keep.tile([128, BANK], F32, name=f"c_up_{h}{s}{t}") for h, s in both for t in range(4)}
-        capped_b = [keep.tile([128, 4, BANK], BF16, name=f"capped_b_{s}", align_bytes=64) for s in range(2)]
-        lower_b = [keep.tile([128, 4, BANK], BF16, name=f"lower_b_{s}", align_bytes=64) for s in range(2)]
+        y_wide = tiles("y_wide", [128, 4, J], BF16, range(2))
+        x_laid = tiles("x_laid", [128, 4 * BANK], BF16, pairs)
+        y_laid = tiles("y_laid", [128, BANK, 4], BF16, pairs)
+        x_code = tiles("x_code", [128, BANK], U32, pairs)
+        x_sc = tiles("x_sc", [128, BANK], U8, pairs)
+        y_code = tiles("y_code", [128, J], U32, range(2))
+        y_sc = tiles("y_sc", [128, J], U8, range(2))
+        sig_code = tiles("sig_code", [128, J], U32, range(2))
+        sig_sc = tiles("sig_sc", [128, J], U8, range(2))
+        upper = {(h, s, t): keep.tile([128, BANK], F32, name=f"upper_{h}{s}{t}") for h, s in pairs for t in SLOTS}
+        capped_packed = tiles("capped_packed", [128, 4, BANK], BF16, range(2))
+        lower_packed = tiles("lower_packed", [128, 4, BANK], BF16, range(2))
         l_sb = keep.tile([128, 2, 4, K], BF16, name="l_sb")
         m_sb = keep.tile([K, J], BF16, name="m_sb")
         l_t = keep.tile([K, 8, 128], BF16, name="l_t")
         ident = keep.tile([128, 128], BF16, name="ident")
         y_fac = keep.tile([128, 2, 8], F32, name="y_fac")
-        g_b = keep.tile([128, 8], BF16, name="g_b")
-        t_b = keep.tile([128, 8], BF16, name="t_b")
-        g_f = keep.tile([128, 8], F32, name="g_f")
-        g_c = keep.tile([128, 8], F32, name="g_c")
+        g_sb = keep.tile([128, 8], BF16, name="g_sb")
+        tau_sb = keep.tile([128, 8], BF16, name="tau_sb")
+        g_over_t = keep.tile([128, 8], F32, name="g_over_t")
         g_abs = keep.tile([128, 8], F32, name="g_abs")
         width = keep.tile([128, 8], F32, name="width")
-        width2 = keep.tile([128, 8], F32, name="width2")
+        span_down = keep.tile([128, 8], F32, name="span_down")
         w_code = keep.tile([128, 2, 2 * P], U8, name="w_code", align_bytes=64)
         w_sc = keep.tile([128, 2, P], U8, name="w_sc", align_bytes=64)
 
+        x_v = x.rearrange("(q p j) n -> q p j n", q=2, p=128, j=4)
+        y_v = y_bytes.rearrange("(q p j) n -> q p (j n)", q=2, p=128, j=4)
+
         def load_y(q):
-            for a, rows in Y_LOADS:
-                if a == q:
+            for of_pass, rows in Y_LOADS:
+                if of_pass == q:
                     nc.sync.dma_start(out=y_raw[q, rows[0]][:], in_=y_v[q][:, J * rows[0] : J * (rows[-1] + 1)])
 
         def load_x(q, s):
             nc.sync.dma_start(out=x_raw[q, s][:], in_=x_v[q][:, :, BANK * s : BANK * (s + 1)])
+
+        def load_by_slot(tile, vector):
+            nc.sync.dma_start(out=tile[:].rearrange("p (s t) -> p s t", s=2), in_=vector.rearrange("(s p t) -> p s t", s=2, p=128, t=4))
 
         load_y(0)
         load_x(0, 0)
@@ -81,10 +91,10 @@ def tile_lowrankplussoftthresholdedcrosscovarianc_d2p_kernel(
         load_x(1, 0)
         nc.sync.dma_start(out=l_sb[:], in_=l.rearrange("(s p t) k -> p s t k", s=2, p=128, t=4))
         load_x(0, 1)
-        nc.sync.dma_start(out=m_sb[:], in_=m)
-        nc.sync.dma_start(out=g_b[:].rearrange("p (s t) -> p s t", s=2), in_=g.rearrange("(s p t) -> p s t", s=2, p=128, t=4))
-        nc.sync.dma_start(out=t_b[:].rearrange("p (s t) -> p s t", s=2), in_=tau.rearrange("(s p t) -> p s t", s=2, p=128, t=4))
+        load_by_slot(g_sb, g)
+        load_by_slot(tau_sb, tau)
         load_x(1, 1)
+        nc.sync.dma_start(out=m_sb[:], in_=m)
         nc.sync.dma_start(out=w_code[:].bitcast(I32), in_=w_words.bitcast(I32).rearrange("s p n -> p s n"))
         nc.gpsimd.memset(w_sc[:].bitcast(I32), 0)
         for i in range(4):
@@ -96,31 +106,40 @@ def tile_lowrankplussoftthresholdedcrosscovarianc_d2p_kernel(
             nc.scalar.dma_start(out=y_fac[:, q, :], in_=y_scale[4 * q : 4 * q + 4, :].unsqueeze(1).to_broadcast([4, 32, 8]))
         make_identity(nc, ident[:])
 
-        vcopy = nc.vector.tensor_copy
-        scopy = nc.scalar.copy
+        vector_copy = nc.vector.tensor_copy
+        scalar_copy = nc.scalar.copy
 
-        def vscale(out, in_, scale):
-            nc.vector.tensor_scalar(out=out, in0=in_, scalar1=scale, scalar2=None, op0=ALU.mult)
+        def gpsimd_copy(out, in_):
+            nc.gpsimd.tensor_scalar(out=out, in0=in_, scalar1=1.0, scalar2=0.0, op0=ALU.mult, op1=ALU.add)
 
-        def sscale(out, in_, scale):
-            nc.scalar.activation(out=out, in_=in_, func=ACT.Copy, scale=scale)
+        def vector_scale(out, in_, factor):
+            nc.vector.tensor_scalar(out=out, in0=in_, scalar1=factor, scalar2=None, op0=ALU.mult)
 
-        def gscale(out, in_, scale):
-            nc.gpsimd.tensor_scalar(out=out, in0=in_, scalar1=scale, scalar2=0.0, op0=ALU.mult, op1=ALU.add)
+        def scalar_scale(out, in_, factor):
+            nc.scalar.activation(out=out, in_=in_, func=ACT.Copy, scale=factor)
 
-        def gcopy(out, in_):
-            gscale(out, in_, 1.0)
+        def scalar_shift(out, in_, term):
+            nc.scalar.activation(out=out, in_=in_, func=ACT.Identity, bias=term)
 
-        def y_widen(q, rows, h, copy):
+        def gpsimd_shift(out, in_, term):
+            nc.gpsimd.tensor_scalar(out=out, in0=in_, scalar1=1.0, scalar2=term, op0=ALU.mult, op1=ALU.add)
+
+        def of_slot(tile, s, t):
+            return tile[:, 4 * s + t : 4 * s + t + 1]
+
+        def bank(ring, name, dtype=F32, columns=BANK):
+            return psum.tile([128, columns], dtype, name=name, tag=ring[0], bufs=ring[1])
+
+        def y_widen(q, h, rows, copy):
             for j in rows:
-                first = max(r[0] for a, r in Y_LOADS if a == q and r[0] <= j)
+                first = max(r[0] for of_pass, r in Y_LOADS if of_pass == q and r[0] <= j)
                 lo = (j - first) * J + BANK * h
                 copy(out=y_wide[q][:, j, BANK * h : BANK * (h + 1)], in_=y_raw[q, first][:, lo : lo + BANK].bitcast(FP8))
 
-        def y_lay(q, h, scaled_copy, blocks=range(4)):
+        def y_lay(q, h, blocks, scale):
             for b in blocks:
                 col = 4 * h + b
-                scaled_copy(
+                scale(
                     y_laid[q, h][:, BLOCK * b : BLOCK * (b + 1), :].rearrange("p (c i) j -> p c j i", i=4),
                     y_wide[q][:, :, BLOCK * col : BLOCK * (col + 1)].rearrange("p j (c i) -> p c j i", i=4),
                     y_fac[:, q, col : col + 1],
@@ -132,59 +151,38 @@ def tile_lowrankplussoftthresholdedcrosscovarianc_d2p_kernel(
                 out=y_code[q][:, cols].bitcast(FP8X4), scales=y_sc[q][:, cols], in_=y_laid[q, h][:].rearrange("p n j -> p (n j)")
             )
 
-        def x_lay(q, s, copy):
-            dst = x_laid[q, s][:].rearrange("p (t r e j) -> p r t e j", t=4, e=2, j=4)
-            src = x_raw[q, s][:].rearrange("p j (r e t) -> p r t e j", e=2, t=4)
-            copy(out=dst, in_=src)
-
-        def x_slot(q, s, t):
-            return x_raw[q, s][:].rearrange("p j (r t) -> p t r j", t=4)[:, t]
-
-        def x_lay_slot(q, s, t, copy):
-            copy(out=x_laid[q, s][:, BANK * t : BANK * (t + 1)].rearrange("p (r j) -> p r j", j=4), in_=x_slot(q, s, t))
-
-        x_ps = {}
-
-        def x_pass(q, s, ts):
-            ps = psum.tile([128, 2 * BANK], BF16, name="ps_x", tag="c", bufs=3)
-            x_ps[q, s, ts[0]] = ps
-            for i, t in enumerate(ts):
-                nc.tensor.matmul(
-                    ps[:, BANK * i : BANK * (i + 1)].rearrange("p (r j) -> p r j", j=4), ident[:], x_slot(q, s, t), start=True, stop=True
-                )
-
-        def x_fetch(q, s, ts, copy):
-            copy(out=x_laid[q, s][:, BANK * ts[0] : BANK * (ts[-1] + 1)], in_=x_ps[q, s, ts[0]][:, : BANK * len(ts)])
+        def x_lay(q, s):
+            vector_copy(
+                out=x_laid[q, s][:].rearrange("p (t u e j) -> p u t e j", t=4, e=2, j=4),
+                in_=x_raw[q, s][:].rearrange("p j (u e t) -> p u t e j", e=2, t=4),
+            )
 
         def x_quant(q, s):
             nc.vector.quantize_mx(out=x_code[q, s][:].bitcast(FP8X4), scales=x_sc[q, s][:], in_=x_laid[q, s][:])
 
-        def low_rank_weights():
-            ps = psum.tile([128, 2 * BANK], BF16, name="ps_l", tag="o", bufs=2)
+        def turn_l():
+            ps = bank(OUT, "ps_l", BF16, 2 * BANK)
             for s in range(2):
-                for t in range(4):
+                for t in SLOTS:
                     nc.tensor.transpose(ps[:, 128 * (4 * s + t) : 128 * (4 * s + t + 1)], l_sb[:, s, t, :], ident[:])
-            scopy(out=l_t[:].rearrange("p t n -> p (t n)"), in_=ps[:])
+            scalar_copy(out=l_t[:].rearrange("p t n -> p (t n)"), in_=ps[:])
 
-        def row_factors():
-            nc.scalar.activation(out=g_f[:], in_=g_b[:], func=ACT.Copy)
-            nc.scalar.activation(out=g_c[:], in_=g_b[:], func=ACT.Copy, scale=1.0 / T)
-            nc.scalar.activation(out=g_abs[:], in_=g_b[:], func=ACT.Abs)
+        def factors_of_g():
+            nc.scalar.activation(out=g_over_t[:], in_=g_sb[:], func=ACT.Copy, scale=1.0 / T)
+            nc.scalar.activation(out=g_abs[:], in_=g_sb[:], func=ACT.Abs)
 
         def widths():
-            nc.vector.tensor_tensor(out=width[:], in0=g_abs[:], in1=t_b[:], op=ALU.mult)
-            nc.vector.scalar_tensor_tensor(out=width2[:], in0=t_b[:], scalar=-2.0, in1=g_abs[:], op0=ALU.mult, op1=ALU.mult)
+            nc.vector.tensor_tensor(out=width[:], in0=g_abs[:], in1=tau_sb[:], op=ALU.mult)
+            nc.vector.scalar_tensor_tensor(out=span_down[:], in0=tau_sb[:], scalar=-2.0, in1=g_abs[:], op0=ALU.mult, op1=ALU.mult)
 
-        f_ps, capped, sig, sig_laid, o_ps = {}, {}, {}, {}, {}
+        cross_ps, low_ps, out_ps, capped_wide, sig, sig_laid = {}, {}, {}, {}, {}, {}
 
-        c_ps = {}
-
-        def cross_pass(h, s, t, q, tag="c", bufs=3):
+        def cross_pass(h, s, t, q, ring=CROSS):
             cols = slice(BANK * h, BANK * (h + 1))
             if q == 0:
-                c_ps[h, s, t] = psum.tile([128, BANK], F32, name="ps_c", tag=tag, bufs=bufs)
+                cross_ps[h, s, t] = bank(ring, "ps_cross")
             nc.tensor.matmul_mx(
-                out=c_ps[h, s, t][:],
+                out=cross_ps[h, s, t][:],
                 lhsT=x_code[q, s][:, 128 * t : 128 * t + 128].bitcast(FP8X4),
                 lhsT_scale=x_sc[q, s][:, 128 * t : 128 * t + 128],
                 rhs=y_code[q][:, cols].bitcast(FP8X4),
@@ -194,235 +192,249 @@ def tile_lowrankplussoftthresholdedcrosscovarianc_d2p_kernel(
             )
 
         def lift(h, s, t):
-            col = slice(4 * s + t, 4 * s + t + 1)
-            nc.scalar.activation(out=c_up[h, s, t][:], in_=c_ps[h, s, t][:], func=ACT.Identity, scale=g_c[:, col], bias=width[:, col])
+            nc.scalar.activation(
+                out=upper[h, s, t][:], in_=cross_ps[h, s, t][:], func=ACT.Identity, scale=of_slot(g_over_t, s, t), bias=of_slot(width, s, t)
+            )
 
-        def cross_and_lift(h, s, t, *bank):
-            cross_pass(h, s, t, 0, *bank)
+        def cross_and_lift(h, s, t, ring=CROSS):
+            cross_pass(h, s, t, 0, ring)
             cross_pass(h, s, t, 1)
             lift(h, s, t)
 
-        f_banks = [(k, s, range(lo, lo + BANK // w)) for k, (c0, w) in enumerate(CAPS) for s in range(2) for lo in range(0, 4, BANK // w)]
+        def low_rank(k, s, slots, ring=LOW):
+            lo, w = CAP_SPANS[k]
+            ps = bank(ring, "ps_low")
+            for i, t in enumerate(slots):
+                low_ps[k, s, t] = ps[:, w * i : w * (i + 1)]
+                nc.tensor.matmul(low_ps[k, s, t], l_t[:, 4 * s + t, :], m_sb[:, lo : lo + w], start=True, stop=True)
 
-        def low_rank(banks, tag="f", bufs=3):
-            for i in banks:
-                k, s, ts = f_banks[i]
-                lo, w = CAPS[k]
-                ps = psum.tile([128, BANK], F32, name="ps_f", tag=tag, bufs=bufs)
-                for a, t in enumerate(ts):
-                    f_ps[k, s, t] = ps[:, w * a : w * (a + 1)]
-                    nc.tensor.matmul(f_ps[k, s, t], l_t[:, 4 * s + t, :], m_sb[:, lo : lo + w], start=True, stop=True)
+        def in_half(span):
+            lo, w = span
+            return lo // BANK, slice(lo % BANK, lo % BANK + w)
 
-        def cap(k, s, t):
-            lo, w = CAPS[k]
-            h, cols = lo // BANK, slice(lo % BANK, lo % BANK + w)
-            if (h, s) == (0, 1):
-                capped[s, t] = work.tile([128, BANK], F32, name="capped", bufs=4)
+        def cap(k, s, t, packed=True):
+            h, cols = in_half(CAP_SPANS[k])
+            if not packed:
+                capped_wide[t] = work.tile([128, BANK], F32, name=f"capped_wide_{t}")
             nc.vector.scalar_tensor_tensor(
-                out=capped[s, t][:] if (h, s) == (0, 1) else capped_b[s][:, t, cols],
-                in0=f_ps[k, s, t],
-                scalar=g_f[:, 4 * s + t : 4 * s + t + 1],
-                in1=c_up[h, s, t][:, cols],
+                out=capped_packed[s][:, t, cols] if packed else capped_wide[t][:],
+                in0=low_ps[k, s, t],
+                scalar=of_slot(g_sb, s, t),
+                in1=upper[h, s, t][:, cols],
                 op0=ALU.mult,
                 op1=ALU.min,
             )
 
-        def floors(k, s, *midway):
-            lo, w = CHUNKS[k]
-            h, cols = lo // BANK, slice(lo % BANK, lo % BANK + w)
-            sig[k, s] = work.tile([128, 4, w], BF16, name=f"sig_{k}{s}", bufs=1, align_bytes=64)
-            for t in range(4):
-                if t == 3:
-                    for step, *args in midway:
-                        step(*args)
+        def lower(k, s, slots, shift):
+            h, cols = in_half(CAP_SPANS[k])
+            for t in slots:
+                shift(lower_packed[s][:, t, cols], upper[h, s, t][:, cols], of_slot(span_down, s, t))
+
+        def new_sig(k, s):
+            sig[k, s] = work.tile([128, 4, CHUNKS[k][1]], BF16, name=f"sig_{k}{s}", align_bytes=64)
+            return sig[k, s]
+
+        def laid_sig(k, s):
+            if (k, s) not in sig_laid:
+                sig_laid[k, s] = work.tile([128, CHUNKS[k][1], 4], BF16, name=f"sig_laid_{k}{s}", align_bytes=64)
+            return sig_laid[k, s]
+
+        def floor_by_slot(k, s):
+            h, cols = in_half(CHUNKS[k])
+            dst = new_sig(k, s)
+            for t in SLOTS:
                 nc.vector.scalar_tensor_tensor(
-                    out=sig[k, s][:, t, :],
-                    in0=c_up[h, s, t][:, cols],
-                    scalar=width2[:, 4 * s + t : 4 * s + t + 1],
-                    in1=capped[s, t][:],
+                    out=dst[:, t, :],
+                    in0=upper[h, s, t][:, cols],
+                    scalar=of_slot(span_down, s, t),
+                    in1=capped_wide[t][:],
                     op0=ALU.add,
                     op1=ALU.max,
                 )
 
-        def sshift(out, in_, bias):
-            nc.scalar.activation(out=out, in_=in_, func=ACT.Identity, bias=bias)
-
-        def gshift(out, in_, bias):
-            nc.gpsimd.tensor_scalar(out=out, in0=in_, scalar1=1.0, scalar2=bias, op0=ALU.mult, op1=ALU.add)
-
-        def lower(k, s, ts=range(4), shift=sshift):
-            lo, w = CAPS[k]
-            cols = slice(lo % BANK, lo % BANK + w)
-            for t in ts:
-                shift(lower_b[s][:, t, cols], c_up[lo // BANK, s, t][:, cols], width2[:, 4 * s + t : 4 * s + t + 1])
-
         def floor_packed(k, s):
-            lo, w = CHUNKS[k]
-            cols = slice(lo % BANK, lo % BANK + w)
-            sig[k, s] = work.tile([128, 4, w], BF16, name=f"sig_{k}{s}", bufs=1, align_bytes=64)
-            nc.vector.tensor_tensor(out=sig[k, s][:], in0=capped_b[s][:, :, cols], in1=lower_b[s][:, :, cols], op=ALU.max)
+            cols = in_half(CHUNKS[k])[1]
+            nc.vector.tensor_tensor(out=new_sig(k, s)[:], in0=capped_packed[s][:, :, cols], in1=lower_packed[s][:, :, cols], op=ALU.max)
 
-        def floor_laid(k, s):
-            lo, w = CHUNKS[k]
-            cols = slice(lo % BANK, lo % BANK + w)
-            sig_laid[k, s] = work.tile([128, w, 4], BF16, name=f"sig_laid_{k}{s}", bufs=1, align_bytes=64)
+        def floor_and_lay(k, s):
+            cols = in_half(CHUNKS[k])[1]
             nc.vector.tensor_tensor(
-                out=sig_laid[k, s][:].rearrange("p (c i) t -> p c t i", i=4),
-                in0=capped_b[s][:, :, cols].rearrange("p t (c i) -> p c t i", i=4),
-                in1=lower_b[s][:, :, cols].rearrange("p t (c i) -> p c t i", i=4),
+                out=laid_sig(k, s)[:].rearrange("p (c i) t -> p c t i", i=4),
+                in0=capped_packed[s][:, :, cols].rearrange("p t (c i) -> p c t i", i=4),
+                in1=lower_packed[s][:, :, cols].rearrange("p t (c i) -> p c t i", i=4),
                 op=ALU.max,
             )
 
-        def caps(h, s, *beside):
-            for t in range(4):
-                cap(h, s, t)
-                for step, *args in beside[t] if beside else ():
-                    step(*args)
-
-        def lifts(h, s, ts=range(4)):
-            return [(cross_and_lift, h, s, t) for t in ts]
-
-        def s_lay(k, s, lo, hi, copy):
-            if (k, s) not in sig_laid:
-                sig_laid[k, s] = work.tile([128, CHUNKS[k][1], 4], BF16, name=f"sig_laid_{k}{s}", bufs=1, align_bytes=64)
-            run = 1 if copy is gcopy else 4
+        def sig_lay(k, s, lo, hi, copy):
+            run = 1 if copy is gpsimd_copy else 4
             copy(
-                out=sig_laid[k, s][:, lo:hi, :].rearrange("p (c i) t -> p c t i", i=run),
+                out=laid_sig(k, s)[:, lo:hi, :].rearrange("p (c i) t -> p c t i", i=run),
                 in_=sig[k, s][:, :, lo:hi].rearrange("p t (c i) -> p c t i", i=run),
             )
 
-        def s_quant(k, s, lo, hi):
-            cols = slice(CHUNKS[k][0] + lo, CHUNKS[k][0] + hi)
+        def sig_quant(k, s):
+            lo, w = CHUNKS[k]
             nc.vector.quantize_mx(
-                out=s_code[s][:, cols].bitcast(FP8X4),
-                scales=s_sc[s][:, cols],
-                in_=sig_laid[k, s][:, lo:hi, :].rearrange("p n t -> p (n t)"),
+                out=sig_code[s][:, lo : lo + w].bitcast(FP8X4),
+                scales=sig_sc[s][:, lo : lo + w],
+                in_=sig_laid[k, s][:].rearrange("p n t -> p (n t)"),
             )
 
-        def exposure(s, bs, lo, hi, tag="c", bufs=3):
+        def exposure(k, s, blocks, ring=None):
+            lo, w = CHUNKS[k]
             if s == 0:
-                o_ps[bs[0], lo] = psum.tile([128, BANK], F32, name="ps_o", tag=tag, bufs=bufs)
-            step = BANK if hi - lo == BANK else BLOCK
-            parts = [(b, c) for b in bs for c in range(lo, hi, step)]
+                out_ps[k, blocks[0]] = bank(ring, "ps_out")
+            step = BANK if w == BANK else BLOCK
+            parts = [(b, c) for b in blocks for c in range(lo, lo + w, step)]
             for i, (b, c) in enumerate(parts):
                 nc.tensor.matmul_mx(
-                    out=o_ps[bs[0], lo][:, step * i : step * (i + 1)],
+                    out=out_ps[k, blocks[0]][:, step * i : step * (i + 1)],
                     lhsT=w_code[:, s, 256 * b : 256 * b + 256].bitcast(FP4X4),
                     lhsT_scale=w_sc[:, s, 128 * b : 128 * b + 128],
-                    rhs=s_code[s][:, c : c + step].bitcast(FP8X4),
-                    rhs_scale=s_sc[s][:, c : c + step],
+                    rhs=sig_code[s][:, c : c + step].bitcast(FP8X4),
+                    rhs_scale=sig_sc[s][:, c : c + step],
                     start=(s == 0 and i == 0),
                     stop=(s == 1 and i == len(parts) - 1),
                 )
 
-        def store(bs, lo, hi, copy):
-            n = len(bs) * (hi - lo)
-            o_sb = work.tile([128, BANK], F32, name="o_sb", bufs=8)
-            copy(out=o_sb[:, :n], in_=o_ps[bs[0], lo][:, :n])
+        def store(k, blocks, copy):
+            lo, w = CHUNKS[k]
+            n = len(blocks) * w
+            staged = work.tile([128, BANK], F32, name="staged", bufs=8)
+            copy(out=staged[:, :n], in_=out_ps[k, blocks[0]][:, :n])
             nc.sync.dma_start(
-                out=out[128 * bs[0] : 128 * (bs[-1] + 1), lo:hi].rearrange("(b p) n -> p b n", p=128),
-                in_=o_sb[:, :n].rearrange("p (b n) -> p b n", b=len(bs)),
+                out=out[128 * blocks[0] : 128 * (blocks[-1] + 1), lo : lo + w].rearrange("(b p) n -> p b n", p=128),
+                in_=staged[:, :n].rearrange("p (b n) -> p b n", b=len(blocks)),
             )
 
 
-        y_widen(0, (0, 1, 2, 3), 0, vcopy)
-        y_widen(0, (3,), 1, vcopy)
-        y_widen(0, (0, 1, 2), 1, scopy)
-        y_lay(0, 0, vscale)
-        y_lay(0, 1, sscale, (0, 1))
-        y_widen(1, (0, 1, 2, 3), 0, scopy)
-        x_lay(0, 0, vcopy)
+        y_widen(0, 0, (0, 1, 2, 3), vector_copy)
+        y_widen(0, 1, (3,), vector_copy)
+        y_widen(0, 1, (0, 1, 2), scalar_copy)
+        y_lay(0, 0, (0, 1, 2), vector_scale)
+        y_lay(0, 0, (3,), scalar_scale)
+        y_lay(0, 1, (0,), scalar_scale)
+        y_widen(1, 0, (0, 1, 2, 3), scalar_copy)
+        x_lay(0, 0)
         y_quant(0, 0)
-        y_lay(0, 1, vscale, (3,))
-        x_lay(1, 0, vcopy)
+        y_lay(0, 1, (2, 3), vector_scale)
+        x_lay(1, 0)
         x_quant(0, 0)
-        y_lay(0, 1, sscale, (2,))
-        y_lay(1, 0, sscale, (0, 1, 2, 3))
-        low_rank_weights()
+        y_lay(0, 1, (1,), scalar_scale)
+        y_lay(1, 0, (0, 1, 2, 3), scalar_scale)
+        turn_l()
         x_quant(1, 0)
-        row_factors()
-        x_lay(0, 1, vcopy)
+        factors_of_g()
+        x_lay(0, 1)
         y_quant(1, 0)
-        for t in range(3):
+        for t in range(CROSS[1]):
             cross_pass(0, 0, t, 0)
-        low_rank((0, 1))
-        y_widen(1, (0, 1, 2), 1, scopy)
+        y_widen(1, 1, (0, 1, 2), scalar_copy)
         widths()
-        x_lay(1, 1, vcopy)
-        for t in range(3):
+        x_lay(1, 1)
+        for t in range(CROSS[1]):
             cross_pass(0, 0, t, 1)
             lift(0, 0, t)
+            low_rank(0, 0, (t,))
         cross_and_lift(0, 0, 3)
-        low_rank((2,))
-        low_rank((3, 4), "o", 2)
+        low_rank(0, 0, (3,), OUT)
+        low_rank(0, 1, (0,), OUT)
         x_quant(0, 1)
         x_quant(1, 1)
-        y_widen(1, (3,), 1, scopy)
-        lower(0, 0, (0,))
-        lower(0, 0, (1, 2, 3), gshift)
+        y_widen(1, 1, (3,), scalar_copy)
 
-        every = (0, 1, 2, 3)
-        y_lay(1, 1, sscale, (0, 1))
-        caps(0, 0, [], lifts(0, 1, [0]), lifts(0, 1, [1]), lifts(0, 1, [2]))
-        y_lay(1, 1, vscale, (2, 3))
+        lower(0, 0, (0,), scalar_shift)
+        lower(0, 0, (1, 2, 3), gpsimd_shift)
+        y_lay(1, 1, (0, 1), scalar_scale)
+        for t in SLOTS:
+            cap(0, 0, t)
+            if t > 0:
+                cross_and_lift(0, 1, t - 1)
+        y_lay(1, 1, (2, 3), vector_scale)
         y_quant(0, 1)
-        cross_and_lift(0, 1, 3, "o", 2)
-        low_rank((5, 6, 7))
+        cross_and_lift(0, 1, 3, OUT)
+        for t in (1, 2, 3):
+            low_rank(0, 1, (t,))
         y_quant(1, 1)
         floor_packed(0, 0)
-        s_lay(0, 0, 0, G00, gcopy)
+
+        sig_lay(0, 0, 0, GPSIMD_COLUMNS[0], gpsimd_copy)
         cross_and_lift(1, 0, 0)
-        caps(0, 1, lifts(1, 0, [1]), lifts(1, 0, [2]) + [(low_rank, (8,), "o", 2)], lifts(1, 0, [3]) + [(low_rank, (9,), "o", 2)], lifts(1, 1, [0]))
-        s_lay(0, 0, G00, 512, scopy)
-        for t in range(1, 4):
+        cap(0, 1, 0, packed=False)
+        cross_and_lift(1, 0, 1)
+        cap(0, 1, 1, packed=False)
+        cross_and_lift(1, 0, 2)
+        low_rank(1, 0, (0, 1), OUT)
+        cap(0, 1, 2, packed=False)
+        cross_and_lift(1, 0, 3)
+        low_rank(1, 0, (2, 3), OUT)
+        sig_lay(0, 0, GPSIMD_COLUMNS[0], BANK, scalar_copy)
+        cap(0, 1, 3, packed=False)
+        for t in SLOTS:
             cross_and_lift(1, 1, t)
-            low_rank((9 + t,))
-        floors(0, 1)
-        s_quant(0, 0, 0, 512)
-        s_lay(0, 1, 0, G01, gcopy)
-        caps(1, 0)
-        lower(1, 0)
-        lower(1, 1)
-        for b in (2, 3, 0, 1):
-            exposure(0, (b,), 0, 512, *(("o", 2) if b < 2 else ("c", 3)))
-        caps(1, 1)
-        low_rank((13, 14))
-        s_lay(0, 1, G01, 512, vcopy)
+        low_rank(1, 1, (0, 1))
+        low_rank(1, 1, (2, 3))
+        low_rank(2, 0, (0, 1))
+        floor_by_slot(0, 1)
+        sig_quant(0, 0)
+
+        sig_lay(0, 1, 0, GPSIMD_COLUMNS[1], gpsimd_copy)
+        for t in SLOTS:
+            cap(1, 0, t)
+        lower(1, 0, SLOTS, scalar_shift)
+        lower(1, 1, SLOTS, scalar_shift)
+        for b, ring in ((2, CROSS), (3, CROSS), (0, OUT), (1, OUT)):
+            exposure(0, 0, (b,), ring)
+        for t in SLOTS:
+            cap(1, 1, t)
+        low_rank(2, 0, (2, 3))
+        low_rank(2, 1, (0, 1))
+        sig_lay(0, 1, GPSIMD_COLUMNS[1], BANK, vector_copy)
         floor_packed(1, 0)
-        s_quant(0, 1, 0, 512)
-        for b in every:
-            exposure(1, (b,), 0, 512)
+        sig_quant(0, 1)
+        for b in ROW_BLOCKS:
+            exposure(0, 1, (b,))
         floor_packed(1, 1)
-        s_lay(1, 1, 0, 256, gcopy)
-        lower(2, 0)
-        s_lay(1, 0, 0, 256, scopy)
-        store((0,), 0, 512, scopy)
-        store((1,), 0, 512, scopy)
-        lower(2, 1)
-        store((2,), 0, 512, scopy)
-        store((3,), 0, 512, scopy)
-        caps(2, 0, [], [(low_rank, (15,))], [], [])
-        caps(2, 1, [], [(s_quant, 1, 0, 0, 256), (s_quant, 1, 1, 0, 256)], [], [])
-        exposure(0, (0, 1), 512, 768)
-        exposure(1, (0, 1), 512, 768)
-        exposure(0, (2, 3), 512, 768, "o", 2)
-        exposure(1, (2, 3), 512, 768)
-        floor_laid(2, 0)
-        floor_laid(2, 1)
-        store((0, 1), 512, 768, scopy)
-        store((2, 3), 512, 768, scopy)
-        s_quant(2, 0, 0, 128)
-        exposure(0, every, 768, 896, "o", 2)
-        s_quant(2, 1, 0, 128)
-        exposure(1, every, 768, 896)
-        store(every, 768, 896, scopy)
-        floor_laid(3, 0)
-        floor_laid(3, 1)
-        s_quant(3, 0, 0, 128)
-        exposure(0, (0, 1), 896, 1024)
-        exposure(0, (2, 3), 896, 1024)
-        s_quant(3, 1, 0, 128)
-        exposure(1, (0, 1), 896, 1024)
-        exposure(1, (2, 3), 896, 1024)
-        store((0, 1), 896, 1024, vcopy)
-        store((2, 3), 896, 1024, scopy)
+
+        sig_lay(1, 1, 0, CHUNKS[1][1], gpsimd_copy)
+        lower(2, 0, SLOTS, scalar_shift)
+        sig_lay(1, 0, 0, CHUNKS[1][1], scalar_copy)
+        store(0, (0,), scalar_copy)
+        store(0, (1,), scalar_copy)
+        lower(2, 1, SLOTS, scalar_shift)
+        store(0, (2,), scalar_copy)
+        store(0, (3,), scalar_copy)
+        cap(2, 0, 0)
+        cap(2, 0, 1)
+        low_rank(2, 1, (2, 3))
+        cap(2, 0, 2)
+        cap(2, 0, 3)
+        cap(2, 1, 0)
+        cap(2, 1, 1)
+        sig_quant(1, 0)
+        sig_quant(1, 1)
+        cap(2, 1, 2)
+        cap(2, 1, 3)
+        for blocks, ring in (((0, 1), CROSS), ((2, 3), OUT)):
+            exposure(1, 0, blocks, ring)
+            exposure(1, 1, blocks)
+
+        floor_and_lay(2, 0)
+        floor_and_lay(2, 1)
+        store(1, (0, 1), scalar_copy)
+        store(1, (2, 3), scalar_copy)
+        sig_quant(2, 0)
+        exposure(2, 0, ROW_BLOCKS, OUT)
+        sig_quant(2, 1)
+        exposure(2, 1, ROW_BLOCKS)
+        store(2, ROW_BLOCKS, scalar_copy)
+        floor_and_lay(3, 0)
+        floor_and_lay(3, 1)
+        sig_quant(3, 0)
+        for b, ring in zip(ROW_BLOCKS, (CROSS, CROSS, LOW, LOW)):
+            exposure(3, 0, (b,), ring)
+        sig_quant(3, 1)
+        for b in ROW_BLOCKS:
+            exposure(3, 1, (b,))
+        for b in ROW_BLOCKS:
+            store(3, (b,), scalar_copy if b % 2 else vector_copy)

@@ -157,6 +157,25 @@ def tile_lowrankplussoftthresholdedcrosscovarianc_d2p_kernel(
                 in_=x_raw[q, s][:].rearrange("p j (u e t) -> p u t e j", e=2, t=4),
             )
 
+        pair_ps = {}
+
+        def x_pair(q, s, a):
+            pair_ps[q, s, a] = bank(CROSS, "ps_pair", BF16, 2 * BANK)
+            for u in range(2):
+                nc.tensor.matmul(
+                    pair_ps[q, s, a][:, BANK * u : BANK * (u + 1)].rearrange("p (c e) -> p e c", e=2),
+                    ident[:],
+                    x_raw[q, s][:, 2 * u : 2 * u + 2, 256 * a : 256 * (a + 1)],
+                    start=True,
+                    stop=True,
+                )
+
+        def x_fetch(q, s, a):
+            scalar_copy(
+                out=x_laid[q, s][:].bitcast(F32).rearrange("p (t r u) -> p t r u", t=4, u=2)[:, :, 64 * a : 64 * (a + 1), :],
+                in_=pair_ps[q, s, a][:].bitcast(F32).rearrange("p (u r t) -> p t r u", u=2, t=4),
+            )
+
         def x_quant(q, s):
             nc.vector.quantize_mx(out=x_code[q, s][:].bitcast(FP8X4), scales=x_sc[q, s][:], in_=x_laid[q, s][:])
 
@@ -311,46 +330,56 @@ def tile_lowrankplussoftthresholdedcrosscovarianc_d2p_kernel(
         y_widen(0, 0, (0, 1, 2, 3), vector_copy)
         y_widen(0, 1, (3,), vector_copy)
         y_widen(0, 1, (0, 1, 2), scalar_copy)
-        y_lay(0, 0, (0, 1, 2), vector_scale)
-        y_lay(0, 0, (3,), scalar_scale)
-        y_lay(0, 1, (0,), scalar_scale)
-        y_widen(1, 0, (0, 1, 2, 3), scalar_copy)
-        x_lay(0, 0)
+        y_lay(0, 0, (0, 1, 2, 3), vector_scale)
+        y_lay(0, 1, (0, 1), scalar_scale)
+        x_pair(0, 0, 0)
+        x_pair(0, 0, 1)
+        y_widen(1, 0, (0, 1, 2, 3), vector_copy)
+        y_widen(1, 1, (0,), scalar_copy)
+        x_fetch(0, 0, 0)
+        y_lay(0, 1, (2,), scalar_scale)
+        x_fetch(0, 0, 1)
         y_quant(0, 0)
-        y_lay(0, 1, (2, 3), vector_scale)
-        x_lay(1, 0)
+        y_lay(0, 1, (3,), scalar_scale)
+        x_pair(1, 0, 0)
+        x_pair(1, 0, 1)
+        y_lay(1, 0, (0, 1, 2, 3), vector_scale)
+        y_widen(1, 1, (1,), scalar_copy)
+        x_fetch(1, 0, 0)
+        y_widen(1, 1, (2,), scalar_copy)
+        x_fetch(1, 0, 1)
         x_quant(0, 0)
-        y_lay(0, 1, (1,), scalar_scale)
-        y_lay(1, 0, (0, 1, 2, 3), scalar_scale)
-        turn_l()
-        x_quant(1, 0)
-        factors_of_g()
-        x_lay(0, 1)
         y_quant(1, 0)
+        factors_of_g()
+        turn_l()
+        y_widen(1, 1, (3,), scalar_copy)
+        x_lay(0, 1)
+        x_quant(1, 0)
         for t in range(CROSS[1]):
             cross_pass(0, 0, t, 0)
-        y_widen(1, 1, (0, 1, 2), scalar_copy)
+        low_rank(0, 0, (0,))
         widths()
         x_lay(1, 1)
+        x_quant(0, 1)
+        y_lay(1, 1, (0,), scalar_scale)
         for t in range(CROSS[1]):
             cross_pass(0, 0, t, 1)
             lift(0, 0, t)
-            low_rank(0, 0, (t,))
+        low_rank(0, 0, (1,))
         cross_and_lift(0, 0, 3)
+        low_rank(0, 0, (2,))
         low_rank(0, 0, (3,), OUT)
         low_rank(0, 1, (0,), OUT)
-        x_quant(0, 1)
         x_quant(1, 1)
-        y_widen(1, 1, (3,), scalar_copy)
+        y_lay(1, 1, (1, 2), scalar_scale)
 
         lower(0, 0, (0,), scalar_shift)
         lower(0, 0, (1, 2, 3), gpsimd_shift)
-        y_lay(1, 1, (0, 1), scalar_scale)
         for t in SLOTS:
             cap(0, 0, t)
             if t > 0:
                 cross_and_lift(0, 1, t - 1)
-        y_lay(1, 1, (2, 3), vector_scale)
+        y_lay(1, 1, (3,), vector_scale)
         y_quant(0, 1)
         cross_and_lift(0, 1, 3, OUT)
         for t in (1, 2, 3):

@@ -21,11 +21,8 @@ BANK = 512
 BLOCK = 128
 SLOTS = range(4)
 ROW_BLOCKS = range(4)
-CROSS, LOW, OUT = ("cross", 3), ("low", 3), ("out", 2)
 Y_LOADS = ((0, (0,)), (0, (1,)), (0, (2,)), (0, (3,)), (1, (0, 1)), (1, (2, 3)))
-CAP_SPANS = ((0, 512), (512, 256), (768, 256))
-CHUNKS = ((0, 512), (512, 256), (768, 128), (896, 128))
-GPSIMD_COLUMNS = (384, 464)
+UNITS = (((0,), 0, 512), ((1,), 0, 512), ((0, 1), 512, 256)) + tuple(((s,), lo, 128) for lo in (768, 896) for s in range(2))
 
 
 def tile_lowrankplussoftthresholdedcrosscovarianc_d2p_kernel(
@@ -34,7 +31,6 @@ def tile_lowrankplussoftthresholdedcrosscovarianc_d2p_kernel(
     nc = tc.nc
     with ExitStack() as ctx:
         keep = ctx.enter_context(tc.tile_pool(name="keep", bufs=1))
-        work = ctx.enter_context(tc.tile_pool(name="work", bufs=1))
         psum = ctx.enter_context(tc.psum_pool(name="psum", bufs=1))
         ctx.enter_context(tc.manual_schedule())
 
@@ -44,19 +40,21 @@ def tile_lowrankplussoftthresholdedcrosscovarianc_d2p_kernel(
             return {key: keep.tile(shape, dtype, name=f"{name}_{i}", align_bytes=64) for i, key in enumerate(keys)}
 
         x_raw = tiles("x_raw", [128, 4, BANK], BF16, pairs)
-        y_raw = {(q, rows[0]): keep.tile([128, len(rows) * J], U8, name=f"y_raw_{q}{rows[0]}", align_bytes=64) for q, rows in Y_LOADS}
-        y_wide = tiles("y_wide", [128, 4, J], BF16, range(2))
+        y_raw = {(q, rows[0]): keep.tile([128, len(rows), J], U8, name=f"y_raw_{q}{rows[0]}", align_bytes=64) for q, rows in Y_LOADS}
+        y_wide = tiles("y_wide", [128, 4, BANK], BF16, pairs)
         x_laid = tiles("x_laid", [128, 4 * BANK], BF16, pairs)
         y_laid = tiles("y_laid", [128, BANK, 4], BF16, pairs)
         x_code = tiles("x_code", [128, BANK], U32, pairs)
         x_sc = tiles("x_sc", [128, BANK], U8, pairs)
-        y_code = tiles("y_code", [128, J], U32, range(2))
-        y_sc = tiles("y_sc", [128, J], U8, range(2))
-        sig_code = tiles("sig_code", [128, J], U32, range(2))
-        sig_sc = tiles("sig_sc", [128, J], U8, range(2))
-        upper = {(h, s, t): keep.tile([128, BANK], F32, name=f"upper_{h}{s}{t}") for h, s in pairs for t in SLOTS}
-        capped_packed = tiles("capped_packed", [128, 4, BANK], BF16, range(2))
-        lower_packed = tiles("lower_packed", [128, 4, BANK], BF16, range(2))
+        y_code = tiles("y_code", [128, BANK], U32, pairs)
+        y_sc = tiles("y_sc", [128, BANK], U8, pairs)
+        upper = {(s, t): keep.tile([128, J], F32, name=f"upper_{s}{t}") for s in range(2) for t in SLOTS}
+        capped = keep.tile([128, 2, 4, J], BF16, name="capped")
+        lowered = keep.tile([128, 2, 4, J], BF16, name="lowered")
+        floored = keep.tile([128, 2, 4, J], BF16, name="floored")
+        sig_laid = {u: keep.tile([128, len(u[0]), u[2], 4], BF16, name=f"sig_laid_{i}", align_bytes=64) for i, u in enumerate(UNITS)}
+        sig_code = {u: keep.tile([128, len(u[0]), u[2]], U32, name=f"sig_code_{i}", align_bytes=64) for i, u in enumerate(UNITS)}
+        sig_sc = {u: keep.tile([128, len(u[0]), u[2]], U8, name=f"sig_sc_{i}", align_bytes=64) for i, u in enumerate(UNITS)}
         l_sb = keep.tile([128, 2, 4, K], BF16, name="l_sb")
         m_sb = keep.tile([K, J], BF16, name="m_sb")
         l_t = keep.tile([K, 8, 128], BF16, name="l_t")
@@ -72,12 +70,12 @@ def tile_lowrankplussoftthresholdedcrosscovarianc_d2p_kernel(
         w_sc = keep.tile([128, 2, P], U8, name="w_sc", align_bytes=64)
 
         x_v = x.rearrange("(q p j) n -> q p j n", q=2, p=128, j=4)
-        y_v = y_bytes.rearrange("(q p j) n -> q p (j n)", q=2, p=128, j=4)
+        y_v = y_bytes.rearrange("(q p j) n -> q p j n", q=2, p=128, j=4)
 
         def load_y(q):
             for of_pass, rows in Y_LOADS:
                 if of_pass == q:
-                    nc.sync.dma_start(out=y_raw[q, rows[0]][:], in_=y_v[q][:, J * rows[0] : J * (rows[-1] + 1)])
+                    nc.sync.dma_start(out=y_raw[q, rows[0]][:], in_=y_v[q][:, rows[0] : rows[-1] + 1, :])
 
         def load_x(q, s):
             nc.sync.dma_start(out=x_raw[q, s][:], in_=x_v[q][:, :, BANK * s : BANK * (s + 1)])
@@ -85,26 +83,21 @@ def tile_lowrankplussoftthresholdedcrosscovarianc_d2p_kernel(
         def load_by_slot(tile, vector):
             nc.sync.dma_start(out=tile[:].rearrange("p (s t) -> p s t", s=2), in_=vector.rearrange("(s p t) -> p s t", s=2, p=128, t=4))
 
-        load_y(0)
-        load_x(0, 0)
-        load_y(1)
-        load_x(1, 0)
-        nc.sync.dma_start(out=l_sb[:], in_=l.rearrange("(s p t) k -> p s t k", s=2, p=128, t=4))
-        load_x(0, 1)
-        load_by_slot(g_sb, g)
-        load_by_slot(tau_sb, tau)
-        load_x(1, 1)
-        nc.sync.dma_start(out=m_sb[:], in_=m)
-        nc.sync.dma_start(out=w_code[:].bitcast(I32), in_=w_words.bitcast(I32).rearrange("s p n -> p s n"))
-        nc.gpsimd.memset(w_sc[:].bitcast(I32), 0)
-        for i in range(4):
-            nc.sync.dma_start(
-                out=w_sc[32 * i : 32 * i + 4].bitcast(I32),
-                in_=w_scales[:, 4 * i : 4 * i + 4, :].bitcast(I32).rearrange("s r n -> r s n"),
-            )
-        for q in range(2):
-            nc.scalar.dma_start(out=y_fac[:, q, :], in_=y_scale[4 * q : 4 * q + 4, :].unsqueeze(1).to_broadcast([4, 32, 8]))
-        make_identity(nc, ident[:])
+        def load_l():
+            nc.sync.dma_start(out=l_sb[:], in_=l.rearrange("(s p t) k -> p s t k", s=2, p=128, t=4))
+
+        def load_w():
+            nc.sync.dma_start(out=w_code[:].bitcast(I32), in_=w_words.bitcast(I32).rearrange("s p n -> p s n"))
+            nc.gpsimd.memset(w_sc[:].bitcast(I32), 0)
+            for i in range(4):
+                nc.sync.dma_start(
+                    out=w_sc[32 * i : 32 * i + 4].bitcast(I32),
+                    in_=w_scales[:, 4 * i : 4 * i + 4, :].bitcast(I32).rearrange("s r n -> r s n"),
+                )
+
+        def load_y_scale():
+            for q in range(2):
+                nc.scalar.dma_start(out=y_fac[:, q, :], in_=y_scale[4 * q : 4 * q + 4, :].unsqueeze(1).to_broadcast([4, 32, 8]))
 
         vector_copy = nc.vector.tensor_copy
         scalar_copy = nc.scalar.copy
@@ -127,40 +120,36 @@ def tile_lowrankplussoftthresholdedcrosscovarianc_d2p_kernel(
         def of_slot(tile, s, t):
             return tile[:, 4 * s + t : 4 * s + t + 1]
 
-        def bank(ring, name, dtype=F32, columns=BANK):
-            return psum.tile([128, columns], dtype, name=name, tag=ring[0], bufs=ring[1])
+        def bank(i, name, dtype=F32, columns=BANK):
+            return psum.tile([128, columns], dtype, name=name, tag=f"bank_{i}")
 
         def y_widen(q, h, rows, copy):
             for j in rows:
                 first = max(r[0] for of_pass, r in Y_LOADS if of_pass == q and r[0] <= j)
-                lo = (j - first) * J + BANK * h
-                copy(out=y_wide[q][:, j, BANK * h : BANK * (h + 1)], in_=y_raw[q, first][:, lo : lo + BANK].bitcast(FP8))
+                copy(out=y_wide[q, h][:, j, :], in_=y_raw[q, first][:, j - first, BANK * h : BANK * (h + 1)].bitcast(FP8))
 
         def y_lay(q, h, blocks, scale):
             for b in blocks:
-                col = 4 * h + b
+                cols = slice(BLOCK * b, BLOCK * (b + 1))
                 scale(
-                    y_laid[q, h][:, BLOCK * b : BLOCK * (b + 1), :].rearrange("p (c i) j -> p c j i", i=4),
-                    y_wide[q][:, :, BLOCK * col : BLOCK * (col + 1)].rearrange("p j (c i) -> p c j i", i=4),
-                    y_fac[:, q, col : col + 1],
+                    y_laid[q, h][:, cols, :].rearrange("p (c i) j -> p c j i", i=4),
+                    y_wide[q, h][:, :, cols].rearrange("p j (c i) -> p c j i", i=4),
+                    y_fac[:, q, 4 * h + b : 4 * h + b + 1],
                 )
 
         def y_quant(q, h):
-            cols = slice(BANK * h, BANK * (h + 1))
-            nc.vector.quantize_mx(
-                out=y_code[q][:, cols].bitcast(FP8X4), scales=y_sc[q][:, cols], in_=y_laid[q, h][:].rearrange("p n j -> p (n j)")
-            )
+            nc.vector.quantize_mx(out=y_code[q, h][:].bitcast(FP8X4), scales=y_sc[q, h][:], in_=y_laid[q, h][:].rearrange("p n j -> p (n j)"))
 
-        def x_lay(q, s):
+        def x_lay(q, s, a0, a1):
             vector_copy(
-                out=x_laid[q, s][:].rearrange("p (t u e j) -> p u t e j", t=4, e=2, j=4),
-                in_=x_raw[q, s][:].rearrange("p j (u e t) -> p u t e j", e=2, t=4),
+                out=x_laid[q, s][:].rearrange("p (t u e j) -> p u t e j", t=4, e=2, j=4)[:, 32 * a0 : 32 * a1],
+                in_=x_raw[q, s][:].rearrange("p j (u e t) -> p u t e j", e=2, t=4)[:, 32 * a0 : 32 * a1],
             )
 
         pair_ps = {}
 
-        def x_pair(q, s, a):
-            pair_ps[q, s, a] = bank(CROSS, "ps_pair", BF16, 2 * BANK)
+        def x_pair(q, s, a, i):
+            pair_ps[q, s, a] = bank(i, "ps_pair", BF16, 2 * BANK)
             for u in range(2):
                 nc.tensor.matmul(
                     pair_ps[q, s, a][:, BANK * u : BANK * (u + 1)].rearrange("p (c e) -> p e c", e=2),
@@ -179,291 +168,276 @@ def tile_lowrankplussoftthresholdedcrosscovarianc_d2p_kernel(
         def x_quant(q, s):
             nc.vector.quantize_mx(out=x_code[q, s][:].bitcast(FP8X4), scales=x_sc[q, s][:], in_=x_laid[q, s][:])
 
-        def turn_l():
-            ps = bank(OUT, "ps_l", BF16, 2 * BANK)
+        turn_ps = {}
+
+        def turn_l(i):
+            turn_ps[0] = bank(i, "ps_l", BF16, 2 * BANK)
             for s in range(2):
                 for t in SLOTS:
-                    nc.tensor.transpose(ps[:, 128 * (4 * s + t) : 128 * (4 * s + t + 1)], l_sb[:, s, t, :], ident[:])
-            scalar_copy(out=l_t[:].rearrange("p t n -> p (t n)"), in_=ps[:])
+                    nc.tensor.transpose(turn_ps[0][:, 128 * (4 * s + t) : 128 * (4 * s + t + 1)], l_sb[:, s, t, :], ident[:])
+
+        def fetch_l():
+            scalar_copy(out=l_t[:].rearrange("p t n -> p (t n)"), in_=turn_ps[0][:])
 
         def factors_of_g():
-            nc.scalar.activation(out=g_over_t[:], in_=g_sb[:], func=ACT.Copy, scale=1.0 / T)
-            nc.scalar.activation(out=g_abs[:], in_=g_sb[:], func=ACT.Abs)
+            vector_scale(g_over_t[:], g_sb[:], 1.0 / T)
+            nc.vector.scalar_tensor_tensor(out=g_abs[:], in0=g_sb[:], scalar=-1.0, in1=g_sb[:], op0=ALU.mult, op1=ALU.max)
 
         def widths():
             nc.vector.tensor_tensor(out=width[:], in0=g_abs[:], in1=tau_sb[:], op=ALU.mult)
+
+        def spans():
             nc.vector.scalar_tensor_tensor(out=span_down[:], in0=tau_sb[:], scalar=-2.0, in1=g_abs[:], op0=ALU.mult, op1=ALU.mult)
 
-        cross_ps, low_ps, out_ps, capped_wide, sig, sig_laid = {}, {}, {}, {}, {}, {}
+        cross_ps, low_ps, out_ps = {}, {}, {}
 
-        def cross_pass(h, s, t, q, ring=CROSS):
-            cols = slice(BANK * h, BANK * (h + 1))
+        def cross_pass(h, s, t, q, i=None):
             if q == 0:
-                cross_ps[h, s, t] = bank(ring, "ps_cross")
+                cross_ps[h, s, t] = bank(i, "ps_cross")
             nc.tensor.matmul_mx(
                 out=cross_ps[h, s, t][:],
                 lhsT=x_code[q, s][:, 128 * t : 128 * t + 128].bitcast(FP8X4),
                 lhsT_scale=x_sc[q, s][:, 128 * t : 128 * t + 128],
-                rhs=y_code[q][:, cols].bitcast(FP8X4),
-                rhs_scale=y_sc[q][:, cols],
+                rhs=y_code[q, h][:].bitcast(FP8X4),
+                rhs_scale=y_sc[q, h][:],
                 start=(q == 0),
                 stop=(q == 1),
             )
 
+        def cross(h, s, t, i):
+            cross_pass(h, s, t, 0, i)
+            cross_pass(h, s, t, 1)
+
+        def half(h):
+            return slice(BANK * h, BANK * (h + 1))
+
         def lift(h, s, t):
             nc.scalar.activation(
-                out=upper[h, s, t][:], in_=cross_ps[h, s, t][:], func=ACT.Identity, scale=of_slot(g_over_t, s, t), bias=of_slot(width, s, t)
+                out=upper[s, t][:, half(h)], in_=cross_ps[h, s, t][:], func=ACT.Identity, scale=of_slot(g_over_t, s, t), bias=of_slot(width, s, t)
             )
 
-        def cross_and_lift(h, s, t, ring=CROSS):
-            cross_pass(h, s, t, 0, ring)
-            cross_pass(h, s, t, 1)
-            lift(h, s, t)
+        def low_rank(s, slots, lo, hi, i):
+            ps = bank(i, "ps_low")
+            for n, t in enumerate(slots):
+                low_ps[s, t, lo] = ps[:, (hi - lo) * n : (hi - lo) * (n + 1)]
+                nc.tensor.matmul(low_ps[s, t, lo], l_t[:, 4 * s + t, :], m_sb[:, lo:hi], start=True, stop=True)
 
-        def low_rank(k, s, slots, ring=LOW):
-            lo, w = CAP_SPANS[k]
-            ps = bank(ring, "ps_low")
-            for i, t in enumerate(slots):
-                low_ps[k, s, t] = ps[:, w * i : w * (i + 1)]
-                nc.tensor.matmul(low_ps[k, s, t], l_t[:, 4 * s + t, :], m_sb[:, lo : lo + w], start=True, stop=True)
-
-        def in_half(span):
-            lo, w = span
-            return lo // BANK, slice(lo % BANK, lo % BANK + w)
-
-        def cap(k, s, t, packed=True):
-            h, cols = in_half(CAP_SPANS[k])
-            if not packed:
-                capped_wide[t] = work.tile([128, BANK], F32, name=f"capped_wide_{t}")
+        def cap(s, t, lo, hi):
             nc.vector.scalar_tensor_tensor(
-                out=capped_packed[s][:, t, cols] if packed else capped_wide[t][:],
-                in0=low_ps[k, s, t],
-                scalar=of_slot(g_sb, s, t),
-                in1=upper[h, s, t][:, cols],
-                op0=ALU.mult,
-                op1=ALU.min,
+                out=capped[:, s, t, lo:hi], in0=low_ps[s, t, lo], scalar=of_slot(g_sb, s, t), in1=upper[s, t][:, lo:hi], op0=ALU.mult, op1=ALU.min
             )
 
-        def lower(k, s, slots, shift):
-            h, cols = in_half(CAP_SPANS[k])
+        def lower(s, slots, lo, hi, shift):
             for t in slots:
-                shift(lower_packed[s][:, t, cols], upper[h, s, t][:, cols], of_slot(span_down, s, t))
+                shift(lowered[:, s, t, lo:hi], upper[s, t][:, lo:hi], of_slot(span_down, s, t))
 
-        def new_sig(k, s):
-            sig[k, s] = work.tile([128, 4, CHUNKS[k][1]], BF16, name=f"sig_{k}{s}", align_bytes=64)
-            return sig[k, s]
+        def floor(groups, lo, hi):
+            part = (slice(None), slice(groups[0], groups[-1] + 1), slice(None), slice(lo, hi))
+            nc.vector.tensor_tensor(out=floored[part], in0=capped[part], in1=lowered[part], op=ALU.max)
 
-        def laid_sig(k, s):
-            if (k, s) not in sig_laid:
-                sig_laid[k, s] = work.tile([128, CHUNKS[k][1], 4], BF16, name=f"sig_laid_{k}{s}", align_bytes=64)
-            return sig_laid[k, s]
-
-        def floor_by_slot(k, s):
-            h, cols = in_half(CHUNKS[k])
-            dst = new_sig(k, s)
-            for t in SLOTS:
-                nc.vector.scalar_tensor_tensor(
-                    out=dst[:, t, :],
-                    in0=upper[h, s, t][:, cols],
-                    scalar=of_slot(span_down, s, t),
-                    in1=capped_wide[t][:],
-                    op0=ALU.add,
-                    op1=ALU.max,
-                )
-
-        def floor_packed(k, s):
-            cols = in_half(CHUNKS[k])[1]
-            nc.vector.tensor_tensor(out=new_sig(k, s)[:], in0=capped_packed[s][:, :, cols], in1=lower_packed[s][:, :, cols], op=ALU.max)
-
-        def floor_and_lay(k, s):
-            cols = in_half(CHUNKS[k])[1]
-            nc.vector.tensor_tensor(
-                out=laid_sig(k, s)[:].rearrange("p (c i) t -> p c t i", i=4),
-                in0=capped_packed[s][:, :, cols].rearrange("p t (c i) -> p c t i", i=4),
-                in1=lower_packed[s][:, :, cols].rearrange("p t (c i) -> p c t i", i=4),
-                op=ALU.max,
+        def floor_by_slot(s, t, lo, hi):
+            nc.vector.scalar_tensor_tensor(
+                out=floored[:, s, t, lo:hi], in0=upper[s, t][:, lo:hi], scalar=of_slot(span_down, s, t), in1=capped[:, s, t, lo:hi], op0=ALU.add, op1=ALU.max
             )
 
-        def sig_lay(k, s, lo, hi, copy):
+        def unit_of(s, lo):
+            return [u for u in UNITS if s in u[0] and u[1] <= lo < u[1] + u[2]][0]
+
+        def in_unit(tiles_by_unit, s, lo, hi):
+            u = unit_of(s, lo)
+            return tiles_by_unit[u][:, u[0].index(s), lo - u[1] : hi - u[1]]
+
+        def laid(s, lo, hi, run):
+            return in_unit(sig_laid, s, lo, hi).rearrange("p (c i) t -> p c t i", i=run)
+
+        def by_slot(tile, s, lo, hi, run):
+            return tile[:, s, :, lo:hi].rearrange("p t (c i) -> p c t i", i=run)
+
+        def floor_and_lay(s, lo, hi):
+            nc.vector.tensor_tensor(out=laid(s, lo, hi, 4), in0=by_slot(capped, s, lo, hi, 4), in1=by_slot(lowered, s, lo, hi, 4), op=ALU.max)
+
+        def sig_lay(s, lo, hi, copy):
             run = 1 if copy is gpsimd_copy else 4
-            copy(
-                out=laid_sig(k, s)[:, lo:hi, :].rearrange("p (c i) t -> p c t i", i=run),
-                in_=sig[k, s][:, :, lo:hi].rearrange("p t (c i) -> p c t i", i=run),
-            )
+            copy(out=laid(s, lo, hi, run), in_=by_slot(floored, s, lo, hi, run))
 
-        def sig_quant(k, s):
-            lo, w = CHUNKS[k]
+        def sig_quant(s, lo):
+            u = unit_of(s, lo)
             nc.vector.quantize_mx(
-                out=sig_code[s][:, lo : lo + w].bitcast(FP8X4),
-                scales=sig_sc[s][:, lo : lo + w],
-                in_=sig_laid[k, s][:].rearrange("p n t -> p (n t)"),
+                out=sig_code[u][:].rearrange("p s n -> p (s n)").bitcast(FP8X4),
+                scales=sig_sc[u][:].rearrange("p s n -> p (s n)"),
+                in_=sig_laid[u][:].rearrange("p s n t -> p (s n t)"),
             )
 
-        def exposure(k, s, blocks, ring=None):
-            lo, w = CHUNKS[k]
+        def exposure(lo, hi, s, blocks, i=None):
+            w = hi - lo
             if s == 0:
-                out_ps[k, blocks[0]] = bank(ring, "ps_out")
-            step = BANK if w == BANK else BLOCK
-            parts = [(b, c) for b in blocks for c in range(lo, lo + w, step)]
-            for i, (b, c) in enumerate(parts):
+                out_ps[lo, blocks[0]] = bank(i, "ps_out")
+            for n, b in enumerate(blocks):
                 nc.tensor.matmul_mx(
-                    out=out_ps[k, blocks[0]][:, step * i : step * (i + 1)],
+                    out=out_ps[lo, blocks[0]][:, w * n : w * (n + 1)],
                     lhsT=w_code[:, s, 256 * b : 256 * b + 256].bitcast(FP4X4),
                     lhsT_scale=w_sc[:, s, 128 * b : 128 * b + 128],
-                    rhs=sig_code[s][:, c : c + step].bitcast(FP8X4),
-                    rhs_scale=sig_sc[s][:, c : c + step],
-                    start=(s == 0 and i == 0),
-                    stop=(s == 1 and i == len(parts) - 1),
+                    rhs=in_unit(sig_code, s, lo, hi).bitcast(FP8X4),
+                    rhs_scale=in_unit(sig_sc, s, lo, hi),
+                    start=(s == 0 and n == 0),
+                    stop=(s == 1 and n == len(blocks) - 1),
                 )
 
-        def store(k, blocks, copy):
-            lo, w = CHUNKS[k]
-            n = len(blocks) * w
-            staged = work.tile([128, BANK], F32, name="staged", bufs=8)
-            copy(out=staged[:, :n], in_=out_ps[k, blocks[0]][:, :n])
-            nc.sync.dma_start(
-                out=out[128 * blocks[0] : 128 * (blocks[-1] + 1), lo : lo + w].rearrange("(b p) n -> p b n", p=128),
-                in_=staged[:, :n].rearrange("p (b n) -> p b n", b=len(blocks)),
+        def both_passes(lo, hi, blocks, i):
+            exposure(lo, hi, 0, blocks, i)
+            exposure(lo, hi, 1, blocks)
+
+        def store(lo, hi, blocks, copy, queue=nc.sync):
+            n = len(blocks) * (hi - lo)
+            staged = keep.tile([128, n], F32, name=f"staged_{lo}_{blocks[0]}")
+            copy(out=staged[:], in_=out_ps[lo, blocks[0]][:, :n])
+            queue.dma_start(
+                out=out[128 * blocks[0] : 128 * (blocks[-1] + 1), lo:hi].rearrange("(b p) n -> p b n", p=128),
+                in_=staged[:].rearrange("p (b n) -> p b n", b=len(blocks)),
             )
 
 
-        y_widen(0, 0, (0, 1, 2, 3), vector_copy)
-        y_widen(0, 1, (3,), vector_copy)
-        y_widen(0, 1, (0, 1, 2), scalar_copy)
-        y_lay(0, 0, (0, 1, 2, 3), vector_scale)
+        load_y(0)
+        load_x(0, 0)
+        load_y(1)
+        load_x(1, 0)
+        load_l()
+        load_by_slot(g_sb, g)
+        load_by_slot(tau_sb, tau)
+        load_x(0, 1)
+        load_x(1, 1)
+        nc.sync.dma_start(out=m_sb[:], in_=m)
+        load_w()
+        load_y_scale()
+        make_identity(nc, ident[:])
+
+        y_widen(0, 0, range(4), vector_copy)
+        y_widen(0, 1, range(4), scalar_copy)
+        y_lay(0, 0, range(4), vector_scale)
         y_lay(0, 1, (0, 1), scalar_scale)
-        x_pair(0, 0, 0)
-        x_pair(0, 0, 1)
-        y_widen(1, 0, (0, 1, 2, 3), vector_copy)
-        y_widen(1, 1, (0,), scalar_copy)
-        x_fetch(0, 0, 0)
-        y_lay(0, 1, (2,), scalar_scale)
-        x_fetch(0, 0, 1)
+        x_pair(0, 0, 0, 0)
+        x_pair(0, 0, 1, 1)
+        y_widen(1, 0, range(4), scalar_copy)
+        y_lay(0, 1, (2, 3), vector_scale)
         y_quant(0, 0)
-        y_lay(0, 1, (3,), scalar_scale)
-        x_pair(1, 0, 0)
-        x_pair(1, 0, 1)
-        y_lay(1, 0, (0, 1, 2, 3), vector_scale)
-        y_widen(1, 1, (1,), scalar_copy)
-        x_fetch(1, 0, 0)
-        y_widen(1, 1, (2,), scalar_copy)
-        x_fetch(1, 0, 1)
-        x_quant(0, 0)
-        y_quant(1, 0)
-        factors_of_g()
-        turn_l()
-        y_widen(1, 1, (3,), scalar_copy)
-        x_lay(0, 1)
-        x_quant(1, 0)
-        for t in range(CROSS[1]):
-            cross_pass(0, 0, t, 0)
-        low_rank(0, 0, (0,))
-        widths()
-        x_lay(1, 1)
-        x_quant(0, 1)
-        y_lay(1, 1, (0,), scalar_scale)
-        for t in range(CROSS[1]):
-            cross_pass(0, 0, t, 1)
-            lift(0, 0, t)
-        low_rank(0, 0, (1,))
-        cross_and_lift(0, 0, 3)
-        low_rank(0, 0, (2,))
-        low_rank(0, 0, (3,), OUT)
-        low_rank(0, 1, (0,), OUT)
-        x_quant(1, 1)
-        y_lay(1, 1, (1, 2), scalar_scale)
-
-        lower(0, 0, (0,), scalar_shift)
-        lower(0, 0, (1, 2, 3), gpsimd_shift)
-        for t in SLOTS:
-            cap(0, 0, t)
-            if t > 0:
-                cross_and_lift(0, 1, t - 1)
-        y_lay(1, 1, (3,), vector_scale)
         y_quant(0, 1)
-        cross_and_lift(0, 1, 3, OUT)
-        for t in (1, 2, 3):
-            low_rank(0, 1, (t,))
+        x_fetch(0, 0, 0)
+        x_fetch(0, 0, 1)
+        y_lay(1, 0, range(4), vector_scale)
+        x_pair(1, 0, 0, 2)
+        x_pair(1, 0, 1, 3)
+        y_widen(1, 1, (0, 1), scalar_copy)
+        x_quant(0, 0)
+        factors_of_g()
+        y_quant(1, 0)
+        widths()
+        x_fetch(1, 0, 0)
+        x_fetch(1, 0, 1)
+        turn_l(0)
+        for t in (0, 1):
+            cross_pass(0, 0, t, 0, 4 + t)
+        x_pair(0, 1, 0, 1)
+        y_widen(1, 1, (2, 3), scalar_copy)
+        x_quant(1, 0)
+        fetch_l()
+        for t in (0, 1):
+            cross_pass(0, 0, t, 1)
+        for t in (2, 3):
+            cross(0, 0, t, 4 + t)
+        x_fetch(0, 1, 0)
+        x_lay(0, 1, 1, 2)
+        x_lay(1, 1, 0, 2)
+        for t in SLOTS:
+            lift(0, 0, t)
+        x_quant(0, 1)
+        y_lay(1, 1, (2, 3), vector_scale)
+        spans()
+        x_quant(1, 1)
+        for t in SLOTS:
+            low_rank(0, (t,), 0, 512, (2, 3, 0, 1)[t])
+
+        LOW_BANKS, CROSS_BANKS = (2, 3, 0, 1), (4, 5, 6, 7)
+        lower(0, (0, 1, 2), 0, 512, gpsimd_shift)
+        y_lay(1, 1, (0, 1), scalar_scale)
+        lower(0, (3,), 0, 512, scalar_shift)
+        for t in SLOTS:
+            cap(0, t, 0, 512)
+            cross(0, 1, t, CROSS_BANKS[t])
+            lift(0, 1, t)
+        for t in SLOTS:
+            low_rank(1, (t,), 0, 512, LOW_BANKS[t])
         y_quant(1, 1)
-        floor_packed(0, 0)
-
-        sig_lay(0, 0, 0, GPSIMD_COLUMNS[0], gpsimd_copy)
-        cross_and_lift(1, 0, 0)
-        cap(0, 1, 0, packed=False)
-        cross_and_lift(1, 0, 1)
-        cap(0, 1, 1, packed=False)
-        cross_and_lift(1, 0, 2)
-        low_rank(1, 0, (0, 1), OUT)
-        cap(0, 1, 2, packed=False)
-        cross_and_lift(1, 0, 3)
-        low_rank(1, 0, (2, 3), OUT)
-        sig_lay(0, 0, GPSIMD_COLUMNS[0], BANK, scalar_copy)
-        cap(0, 1, 3, packed=False)
+        floor((0,), 0, 384)
+        floor((0,), 384, 512)
+        sig_lay(0, 0, 384, gpsimd_copy)
         for t in SLOTS:
-            cross_and_lift(1, 1, t)
-        low_rank(1, 1, (0, 1))
-        low_rank(1, 1, (2, 3))
-        low_rank(2, 0, (0, 1))
-        floor_by_slot(0, 1)
+            cap(1, t, 0, 512)
+            cross(1, 0, t, CROSS_BANKS[t])
+            lift(1, 0, t)
+        sig_lay(0, 384, 512, scalar_copy)
+        low_rank(0, (0, 1), 512, 768, 2)
+        low_rank(0, (2, 3), 512, 768, 3)
+        for t in SLOTS:
+            cross(1, 1, t, CROSS_BANKS[t])
+            lift(1, 1, t)
+        low_rank(1, (0, 1), 512, 768, 0)
+        low_rank(1, (2, 3), 512, 768, 1)
+        for t in SLOTS:
+            floor_by_slot(1, t, 0, 512)
         sig_quant(0, 0)
-
-        sig_lay(0, 1, 0, GPSIMD_COLUMNS[1], gpsimd_copy)
+        sig_lay(1, 0, 512, gpsimd_copy)
         for t in SLOTS:
-            cap(1, 0, t)
-        lower(1, 0, SLOTS, scalar_shift)
-        lower(1, 1, SLOTS, scalar_shift)
-        for b, ring in ((2, CROSS), (3, CROSS), (0, OUT), (1, OUT)):
-            exposure(0, 0, (b,), ring)
+            cap(0, t, 512, 768)
+        lower(0, SLOTS, 512, 768, scalar_shift)
+        for b in (0, 1):
+            exposure(0, 512, 0, (b,), CROSS_BANKS[b])
+        low_rank(0, (0, 1), 768, J, 2)
+        low_rank(0, (2, 3), 768, J, 3)
+        for b in (2, 3):
+            exposure(0, 512, 0, (b,), CROSS_BANKS[b])
         for t in SLOTS:
-            cap(1, 1, t)
-        low_rank(2, 0, (2, 3))
-        low_rank(2, 1, (0, 1))
-        sig_lay(0, 1, GPSIMD_COLUMNS[1], BANK, vector_copy)
-        floor_packed(1, 0)
-        sig_quant(0, 1)
-        for b in ROW_BLOCKS:
-            exposure(0, 1, (b,))
-        floor_packed(1, 1)
-
-        sig_lay(1, 1, 0, CHUNKS[1][1], gpsimd_copy)
-        lower(2, 0, SLOTS, scalar_shift)
-        sig_lay(1, 0, 0, CHUNKS[1][1], scalar_copy)
-        store(0, (0,), scalar_copy)
-        store(0, (1,), scalar_copy)
-        lower(2, 1, SLOTS, scalar_shift)
-        store(0, (2,), scalar_copy)
-        store(0, (3,), scalar_copy)
-        cap(2, 0, 0)
-        cap(2, 0, 1)
-        low_rank(2, 1, (2, 3))
-        cap(2, 0, 2)
-        cap(2, 0, 3)
-        cap(2, 1, 0)
-        cap(2, 1, 1)
+            cap(1, t, 512, 768)
+        low_rank(1, (0, 1), 768, J, 0)
+        low_rank(1, (2, 3), 768, J, 1)
+        lower(1, SLOTS, 512, 768, scalar_shift)
+        cap(0, 0, 768, J)
+        floor((0,), 512, 768)
         sig_quant(1, 0)
-        sig_quant(1, 1)
-        cap(2, 1, 2)
-        cap(2, 1, 3)
-        for blocks, ring in (((0, 1), CROSS), ((2, 3), OUT)):
-            exposure(1, 0, blocks, ring)
-            exposure(1, 1, blocks)
-
-        floor_and_lay(2, 0)
-        floor_and_lay(2, 1)
-        store(1, (0, 1), scalar_copy)
-        store(1, (2, 3), scalar_copy)
-        sig_quant(2, 0)
-        exposure(2, 0, ROW_BLOCKS, OUT)
-        sig_quant(2, 1)
-        exposure(2, 1, ROW_BLOCKS)
-        store(2, ROW_BLOCKS, scalar_copy)
-        floor_and_lay(3, 0)
-        floor_and_lay(3, 1)
-        sig_quant(3, 0)
-        for b, ring in zip(ROW_BLOCKS, (CROSS, CROSS, LOW, LOW)):
-            exposure(3, 0, (b,), ring)
-        sig_quant(3, 1)
         for b in ROW_BLOCKS:
-            exposure(3, 1, (b,))
+            exposure(0, 512, 1, (b,))
+        floor((1,), 512, 768)
+        sig_lay(1, 512, 768, gpsimd_copy)
+        lower(0, SLOTS, 768, J, scalar_shift)
+        sig_lay(0, 512, 768, scalar_copy)
+        store(0, 512, (0,), scalar_copy)
+        lower(1, SLOTS, 768, J, scalar_shift)
+        store(0, 512, (1,), scalar_copy)
+        store(0, 512, (2,), scalar_copy)
+        store(0, 512, (3,), scalar_copy)
+        for t in (1, 2, 3):
+            cap(0, t, 768, J)
+        for t in (0, 1, 2):
+            cap(1, t, 768, J)
+        sig_quant(0, 512)
+        cap(1, 3, 768, J)
+        both_passes(512, 768, (0, 1), 2)
+        both_passes(512, 768, (2, 3), 3)
+        floor_and_lay(0, 768, 896)
+        floor_and_lay(1, 768, 896)
+        store(512, 768, (0, 1), scalar_copy)
+        store(512, 768, (2, 3), scalar_copy)
+        sig_quant(0, 768)
+        exposure(768, 896, 0, ROW_BLOCKS, 1)
+        sig_quant(1, 768)
+        exposure(768, 896, 1, ROW_BLOCKS)
+        store(768, 896, ROW_BLOCKS, scalar_copy)
+        floor_and_lay(0, 896, J)
+        floor_and_lay(1, 896, J)
+        sig_quant(0, 896)
         for b in ROW_BLOCKS:
-            store(3, (b,), scalar_copy if b % 2 else vector_copy)
+            exposure(896, J, 0, (b,), CROSS_BANKS[b])
+        sig_quant(1, 896)
+        for b in ROW_BLOCKS:
+            exposure(896, J, 1, (b,))
+        for b in ROW_BLOCKS:
+            store(896, J, (b,), scalar_copy if b % 2 else vector_copy)

@@ -344,13 +344,14 @@ def tile_lowrankplussoftthresholdedcrosscovarianc_d2p_kernel(
             cross_pass(0, 0, t, 1)
         for t in (2, 3):
             cross(0, 0, t, 4 + t)
-        x_fetch(0, 1, 0)
         x_lay(0, 1, 1, 2)
         x_lay(1, 1, 0, 2)
-        for t in SLOTS:
+        lift(0, 0, 0)
+        x_fetch(0, 1, 0)
+        for t in (1, 2, 3):
             lift(0, 0, t)
-        x_quant(0, 1)
         y_lay(1, 1, (2, 3), vector_scale)
+        x_quant(0, 1)
         spans()
         x_quant(1, 1)
         for t in SLOTS:

@@ -21,8 +21,9 @@ BANK = 512
 BLOCK = 128
 SLOTS = range(4)
 ROW_BLOCKS = range(4)
-Y_LOADS = ((0, (0,)), (0, (1,)), (0, (2,)), (0, (3,)), (1, (0, 1)), (1, (2, 3)))
+Y_LOADS = ((0, (0, 1)), (0, (2, 3)), (1, (0, 1)), (1, (2, 3)))
 UNITS = (((0,), 0, 512), ((1,), 0, 512), ((0, 1), 512, 256)) + tuple(((s,), lo, 128) for lo in (768, 896) for s in range(2))
+X_BOTH, Y_BOTH = ((0, 1), (1, 1)), ((0, 0), (0, 1))
 
 
 def tile_lowrankplussoftthresholdedcrosscovarianc_d2p_kernel(
@@ -41,13 +42,17 @@ def tile_lowrankplussoftthresholdedcrosscovarianc_d2p_kernel(
 
         x_raw = tiles("x_raw", [128, 4, BANK], BF16, pairs)
         y_raw = {(q, rows[0]): keep.tile([128, len(rows), J], U8, name=f"y_raw_{q}{rows[0]}", align_bytes=64) for q, rows in Y_LOADS}
-        y_wide = tiles("y_wide", [128, 4, BANK], BF16, pairs)
-        x_laid = tiles("x_laid", [128, 4 * BANK], BF16, pairs)
-        y_laid = tiles("y_laid", [128, BANK, 4], BF16, pairs)
-        x_code = tiles("x_code", [128, BANK], U32, pairs)
-        x_sc = tiles("x_sc", [128, BANK], U8, pairs)
-        y_code = tiles("y_code", [128, BANK], U32, pairs)
-        y_sc = tiles("y_sc", [128, BANK], U8, pairs)
+        y_wide = tiles("y_wide", [128, 4, J], BF16, range(2))
+
+        def runs(name, words, dtype, together):
+            made = tiles(name, [128, words], dtype, [key for key in pairs if key not in together])
+            made[together] = keep.tile([128, 2 * words], dtype, name=f"{name}_both", align_bytes=64)
+            for i, key in enumerate(together):
+                made[key] = made[together][:, words * i : words * (i + 1)]
+            return made
+
+        x_laid, x_code, x_sc = runs("x_laid", 4 * BANK, BF16, X_BOTH), runs("x_code", BANK, U32, X_BOTH), runs("x_sc", BANK, U8, X_BOTH)
+        y_laid, y_code, y_sc = runs("y_laid", 4 * BANK, BF16, Y_BOTH), runs("y_code", BANK, U32, Y_BOTH), runs("y_sc", BANK, U8, Y_BOTH)
         upper = {(s, t): keep.tile([128, J], F32, name=f"upper_{s}{t}") for s in range(2) for t in SLOTS}
         capped = keep.tile([128, 2, 4, J], BF16, name="capped")
         lowered = keep.tile([128, 2, 4, J], BF16, name="lowered")
@@ -123,22 +128,21 @@ def tile_lowrankplussoftthresholdedcrosscovarianc_d2p_kernel(
         def bank(i, name, dtype=F32, columns=BANK):
             return psum.tile([128, columns], dtype, name=name, tag=f"bank_{i}")
 
-        def y_widen(q, h, rows, copy):
-            for j in rows:
-                first = max(r[0] for of_pass, r in Y_LOADS if of_pass == q and r[0] <= j)
-                copy(out=y_wide[q, h][:, j, :], in_=y_raw[q, first][:, j - first, BANK * h : BANK * (h + 1)].bitcast(FP8))
+        def y_widen(q, j0, j1, lo, hi, copy):
+            first = max(r[0] for of_pass, r in Y_LOADS if of_pass == q and r[0] <= j0)
+            copy(out=y_wide[q][:, j0:j1, lo:hi], in_=y_raw[q, first][:, j0 - first : j1 - first, lo:hi].bitcast(FP8))
 
         def y_lay(q, h, blocks, scale):
             for b in blocks:
-                cols = slice(BLOCK * b, BLOCK * (b + 1))
+                lo = BANK * h + BLOCK * b
                 scale(
-                    y_laid[q, h][:, cols, :].rearrange("p (c i) j -> p c j i", i=4),
-                    y_wide[q, h][:, :, cols].rearrange("p j (c i) -> p c j i", i=4),
+                    y_laid[q, h][:, 4 * BLOCK * b : 4 * BLOCK * (b + 1)].rearrange("p (c i j) -> p c j i", i=4, j=4),
+                    y_wide[q][:, :, lo : lo + BLOCK].rearrange("p j (c i) -> p c j i", i=4),
                     y_fac[:, q, 4 * h + b : 4 * h + b + 1],
                 )
 
-        def y_quant(q, h):
-            nc.vector.quantize_mx(out=y_code[q, h][:].bitcast(FP8X4), scales=y_sc[q, h][:], in_=y_laid[q, h][:].rearrange("p n j -> p (n j)"))
+        def y_quant(key):
+            nc.vector.quantize_mx(out=y_code[key][:].bitcast(FP8X4), scales=y_sc[key][:], in_=y_laid[key][:])
 
         def x_lay(q, s, a0, a1):
             vector_copy(
@@ -165,8 +169,8 @@ def tile_lowrankplussoftthresholdedcrosscovarianc_d2p_kernel(
                 in_=pair_ps[q, s, a][:].bitcast(F32).rearrange("p (u r t) -> p t r u", u=2, t=4),
             )
 
-        def x_quant(q, s):
-            nc.vector.quantize_mx(out=x_code[q, s][:].bitcast(FP8X4), scales=x_sc[q, s][:], in_=x_laid[q, s][:])
+        def x_quant(key):
+            nc.vector.quantize_mx(out=x_code[key][:].bitcast(FP8X4), scales=x_sc[key][:], in_=x_laid[key][:])
 
         turn_ps = {}
 
@@ -311,25 +315,29 @@ def tile_lowrankplussoftthresholdedcrosscovarianc_d2p_kernel(
         load_y_scale()
         make_identity(nc, ident[:])
 
-        y_widen(0, 0, range(4), vector_copy)
-        y_widen(0, 1, range(4), scalar_copy)
+        y_widen(0, 0, 1, 0, J, vector_copy)
+        y_widen(0, 1, 2, 0, J, scalar_copy)
+        y_widen(0, 2, 3, 0, J, vector_copy)
+        y_widen(0, 3, 4, 0, BANK, vector_copy)
+        y_widen(0, 3, 4, BANK, J, scalar_copy)
+        y_lay(0, 1, (1, 2, 3), scalar_scale)
+        y_lay(0, 1, (0,), vector_scale)
         y_lay(0, 0, range(4), vector_scale)
-        y_lay(0, 1, (0, 1), scalar_scale)
         x_pair(0, 0, 0, 0)
         x_pair(0, 0, 1, 1)
-        y_widen(1, 0, range(4), scalar_copy)
-        y_lay(0, 1, (2, 3), vector_scale)
-        y_quant(0, 0)
-        y_quant(0, 1)
+        y_widen(1, 0, 1, 0, J, vector_copy)
+        y_widen(1, 1, 2, 0, J, scalar_copy)
+        y_widen(1, 2, 3, 0, BANK, vector_copy)
+        y_widen(1, 3, 4, 0, J, scalar_copy)
+        y_quant(Y_BOTH)
         x_fetch(0, 0, 0)
         x_fetch(0, 0, 1)
         y_lay(1, 0, range(4), vector_scale)
         x_pair(1, 0, 0, 2)
         x_pair(1, 0, 1, 3)
-        y_widen(1, 1, (0, 1), scalar_copy)
-        x_quant(0, 0)
+        x_quant((0, 0))
         factors_of_g()
-        y_quant(1, 0)
+        y_quant((1, 0))
         widths()
         x_fetch(1, 0, 0)
         x_fetch(1, 0, 1)
@@ -337,9 +345,10 @@ def tile_lowrankplussoftthresholdedcrosscovarianc_d2p_kernel(
         for t in (0, 1):
             cross_pass(0, 0, t, 0, 4 + t)
         x_pair(0, 1, 0, 1)
-        y_widen(1, 1, (2, 3), scalar_copy)
-        x_quant(1, 0)
+        y_widen(1, 2, 3, BANK, J, scalar_copy)
+        x_quant((1, 0))
         fetch_l()
+        y_lay(1, 1, (0,), scalar_scale)
         for t in (0, 1):
             cross_pass(0, 0, t, 1)
         for t in (2, 3):
@@ -350,16 +359,16 @@ def tile_lowrankplussoftthresholdedcrosscovarianc_d2p_kernel(
         x_fetch(0, 1, 0)
         for t in (1, 2, 3):
             lift(0, 0, t)
-        y_lay(1, 1, (2, 3), vector_scale)
-        x_quant(0, 1)
+        y_lay(1, 1, (3,), vector_scale)
+        x_quant((0, 1))
         spans()
-        x_quant(1, 1)
+        x_quant((1, 1))
         for t in SLOTS:
             low_rank(0, (t,), 0, 512, (2, 3, 0, 1)[t])
 
         LOW_BANKS, CROSS_BANKS = (2, 3, 0, 1), (4, 5, 6, 7)
         lower(0, (0, 1, 2), 0, 512, gpsimd_shift)
-        y_lay(1, 1, (0, 1), scalar_scale)
+        y_lay(1, 1, (1, 2), scalar_scale)
         lower(0, (3,), 0, 512, scalar_shift)
         for t in SLOTS:
             cap(0, t, 0, 512)
@@ -367,7 +376,7 @@ def tile_lowrankplussoftthresholdedcrosscovarianc_d2p_kernel(
             lift(0, 1, t)
         for t in SLOTS:
             low_rank(1, (t,), 0, 512, LOW_BANKS[t])
-        y_quant(1, 1)
+        y_quant((1, 1))
         floor((0,), 0, 384)
         floor((0,), 384, 512)
         sig_lay(0, 0, 384, gpsimd_copy)
@@ -394,25 +403,25 @@ def tile_lowrankplussoftthresholdedcrosscovarianc_d2p_kernel(
             exposure(0, 512, 0, (b,), CROSS_BANKS[b])
         low_rank(0, (0, 1), 768, J, 2)
         low_rank(0, (2, 3), 768, J, 3)
-        for b in (2, 3):
-            exposure(0, 512, 0, (b,), CROSS_BANKS[b])
         for t in SLOTS:
             cap(1, t, 512, 768)
         low_rank(1, (0, 1), 768, J, 0)
         low_rank(1, (2, 3), 768, J, 1)
+        for b in (2, 3):
+            exposure(0, 512, 0, (b,), CROSS_BANKS[b])
         lower(1, SLOTS, 512, 768, scalar_shift)
         cap(0, 0, 768, J)
         floor((0,), 512, 768)
+        floor((1,), 512, 768)
         sig_quant(1, 0)
         for b in ROW_BLOCKS:
             exposure(0, 512, 1, (b,))
-        floor((1,), 512, 768)
         sig_lay(1, 512, 768, gpsimd_copy)
         lower(0, SLOTS, 768, J, scalar_shift)
         sig_lay(0, 512, 768, scalar_copy)
         store(0, 512, (0,), scalar_copy)
-        lower(1, SLOTS, 768, J, scalar_shift)
         store(0, 512, (1,), scalar_copy)
+        lower(1, SLOTS, 768, J, scalar_shift)
         store(0, 512, (2,), scalar_copy)
         store(0, 512, (3,), scalar_copy)
         for t in (1, 2, 3):

@@ -23,7 +23,7 @@ SLOTS = range(4)
 ROW_BLOCKS = range(4)
 Y_LOADS = ((0, (0, 1)), (0, (2, 3)), (1, (0, 1)), (1, (2, 3)))
 UNITS = (((0,), 0, 512), ((1,), 0, 512), ((0, 1), 512, 256)) + tuple(((s,), lo, 128) for lo in (768, 896) for s in range(2))
-X_BOTH, Y_BOTH = ((0, 1), (1, 1)), ((0, 0), (0, 1))
+Y_BOTH = ((0, 0), (0, 1))
 
 
 def tile_lowrankplussoftthresholdedcrosscovarianc_d2p_kernel(
@@ -51,7 +51,7 @@ def tile_lowrankplussoftthresholdedcrosscovarianc_d2p_kernel(
                 made[key] = made[together][:, words * i : words * (i + 1)]
             return made
 
-        x_laid, x_code, x_sc = runs("x_laid", 4 * BANK, BF16, X_BOTH), runs("x_code", BANK, U32, X_BOTH), runs("x_sc", BANK, U8, X_BOTH)
+        x_laid, x_code, x_sc = tiles("x_laid", [128, 4 * BANK], BF16, pairs), tiles("x_code", [128, BANK], U32, pairs), tiles("x_sc", [128, BANK], U8, pairs)
         y_laid, y_code, y_sc = runs("y_laid", 4 * BANK, BF16, Y_BOTH), runs("y_code", BANK, U32, Y_BOTH), runs("y_sc", BANK, U8, Y_BOTH)
         upper = {(s, t): keep.tile([128, J], F32, name=f"upper_{s}{t}") for s in range(2) for t in SLOTS}
         capped = keep.tile([128, 2, 4, J], BF16, name="capped")
@@ -146,8 +146,8 @@ def tile_lowrankplussoftthresholdedcrosscovarianc_d2p_kernel(
 
         def x_lay(q, s, a0, a1):
             vector_copy(
-                out=x_laid[q, s][:].rearrange("p (t u e j) -> p u t e j", t=4, e=2, j=4)[:, 32 * a0 : 32 * a1],
-                in_=x_raw[q, s][:].rearrange("p j (u e t) -> p u t e j", e=2, t=4)[:, 32 * a0 : 32 * a1],
+                out=x_laid[q, s][:].rearrange("p (t u e j) -> p u j e t", t=4, e=2, j=4)[:, 32 * a0 : 32 * a1],
+                in_=x_raw[q, s][:].rearrange("p j (u e t) -> p u j e t", e=2, t=4)[:, 32 * a0 : 32 * a1],
             )
 
         pair_ps = {}
@@ -264,6 +264,24 @@ def tile_lowrankplussoftthresholdedcrosscovarianc_d2p_kernel(
             run = 1 if copy is gpsimd_copy else 4
             copy(out=laid(s, lo, hi, run), in_=by_slot(floored, s, lo, hi, run))
 
+        def sig_pair(s, lo, hi, i):
+            w = hi - lo
+            pair_ps[s, lo] = bank(i, "ps_pair", BF16, 4 * w)
+            for u in range(2):
+                nc.tensor.matmul(
+                    pair_ps[s, lo][:, 2 * w * u : 2 * w * (u + 1)].rearrange("p (c e) -> p e c", e=2),
+                    ident[:],
+                    floored[:, s, 2 * u : 2 * u + 2, lo:hi],
+                    start=True,
+                    stop=True,
+                )
+
+        def sig_fetch(s, lo, hi):
+            scalar_copy(
+                out=in_unit(sig_laid, s, lo, hi).bitcast(F32),
+                in_=pair_ps[s, lo][:].bitcast(F32).rearrange("p (u c) -> p c u", u=2),
+            )
+
         def sig_quant(s, lo):
             u = unit_of(s, lo)
             nc.vector.quantize_mx(
@@ -360,9 +378,9 @@ def tile_lowrankplussoftthresholdedcrosscovarianc_d2p_kernel(
         for t in (1, 2, 3):
             lift(0, 0, t)
         y_lay(1, 1, (3,), vector_scale)
-        x_quant((0, 1))
-        spans()
         x_quant((1, 1))
+        spans()
+        x_quant((0, 1))
         for t in SLOTS:
             low_rank(0, (t,), 0, 512, (2, 3, 0, 1)[t])
 
@@ -419,9 +437,10 @@ def tile_lowrankplussoftthresholdedcrosscovarianc_d2p_kernel(
         sig_lay(1, 512, 768, gpsimd_copy)
         lower(0, SLOTS, 768, J, scalar_shift)
         sig_lay(0, 512, 768, scalar_copy)
+        lower(1, (0, 1), 768, J, scalar_shift)
         store(0, 512, (0,), scalar_copy)
         store(0, 512, (1,), scalar_copy)
-        lower(1, SLOTS, 768, J, scalar_shift)
+        lower(1, (2, 3), 768, J, scalar_shift)
         store(0, 512, (2,), scalar_copy)
         store(0, 512, (3,), scalar_copy)
         for t in (1, 2, 3):

@@ -358,15 +358,15 @@ def tile_lowrankplussoftthresholdedcrosscovarianc_d2p_kernel(
         y_quant((1, 0))
         widths()
         x_fetch(1, 0, 0)
+        y_widen(1, 2, 3, BANK, J, scalar_copy)
         x_fetch(1, 0, 1)
         turn_l(0)
         for t in (0, 1):
             cross_pass(0, 0, t, 0, 4 + t)
         x_pair(0, 1, 0, 1)
-        y_widen(1, 2, 3, BANK, J, scalar_copy)
         x_quant((1, 0))
         fetch_l()
-        y_lay(1, 1, (0,), scalar_scale)
+        y_lay(1, 1, (0, 1), scalar_scale)
         for t in (0, 1):
             cross_pass(0, 0, t, 1)
         for t in (2, 3):
@@ -379,15 +379,17 @@ def tile_lowrankplussoftthresholdedcrosscovarianc_d2p_kernel(
             lift(0, 0, t)
         y_lay(1, 1, (3,), vector_scale)
         x_quant((1, 1))
-        spans()
         x_quant((0, 1))
+        spans()
+        y_lay(1, 1, (2,), vector_scale)
         for t in SLOTS:
             low_rank(0, (t,), 0, 512, (2, 3, 0, 1)[t])
 
         LOW_BANKS, CROSS_BANKS = (2, 3, 0, 1), (4, 5, 6, 7)
-        lower(0, (0, 1, 2), 0, 512, gpsimd_shift)
-        y_lay(1, 1, (1, 2), scalar_scale)
+        lower(0, (0, 1), 0, 512, gpsimd_shift)
+        lower(0, (2,), 0, 256, gpsimd_shift)
         lower(0, (3,), 0, 512, scalar_shift)
+        lower(0, (2,), 256, 512, scalar_shift)
         for t in SLOTS:
             cap(0, t, 0, 512)
             cross(0, 1, t, CROSS_BANKS[t])
@@ -439,8 +441,8 @@ def tile_lowrankplussoftthresholdedcrosscovarianc_d2p_kernel(
         sig_lay(0, 512, 768, scalar_copy)
         lower(1, (0, 1), 768, J, scalar_shift)
         store(0, 512, (0,), scalar_copy)
-        store(0, 512, (1,), scalar_copy)
         lower(1, (2, 3), 768, J, scalar_shift)
+        store(0, 512, (1,), scalar_copy)
         store(0, 512, (2,), scalar_copy)
         store(0, 512, (3,), scalar_copy)
         for t in (1, 2, 3):

@@ -379,17 +379,15 @@ def tile_lowrankplussoftthresholdedcrosscovarianc_d2p_kernel(
             lift(0, 0, t)
         y_lay(1, 1, (3,), vector_scale)
         x_quant((1, 1))
-        x_quant((0, 1))
         spans()
-        y_lay(1, 1, (2,), vector_scale)
+        x_quant((0, 1))
         for t in SLOTS:
             low_rank(0, (t,), 0, 512, (2, 3, 0, 1)[t])
 
         LOW_BANKS, CROSS_BANKS = (2, 3, 0, 1), (4, 5, 6, 7)
-        lower(0, (0, 1), 0, 512, gpsimd_shift)
-        lower(0, (2,), 0, 256, gpsimd_shift)
+        lower(0, (0, 1, 2), 0, 512, gpsimd_shift)
+        y_lay(1, 1, (2,), scalar_scale)
         lower(0, (3,), 0, 512, scalar_shift)
-        lower(0, (2,), 256, 512, scalar_shift)
         for t in SLOTS:
             cap(0, t, 0, 512)
             cross(0, 1, t, CROSS_BANKS[t])

@@ -385,9 +385,11 @@ def tile_lowrankplussoftthresholdedcrosscovarianc_d2p_kernel(
             low_rank(0, (t,), 0, 512, (2, 3, 0, 1)[t])
 
         LOW_BANKS, CROSS_BANKS = (2, 3, 0, 1), (4, 5, 6, 7)
-        lower(0, (0, 1, 2), 0, 512, gpsimd_shift)
+        lower(0, (0, 1), 0, 512, gpsimd_shift)
+        lower(0, (2,), 0, 256, gpsimd_shift)
         y_lay(1, 1, (2,), scalar_scale)
         lower(0, (3,), 0, 512, scalar_shift)
+        lower(0, (2,), 256, 512, scalar_shift)
         for t in SLOTS:
             cap(0, t, 0, 512)
             cross(0, 1, t, CROSS_BANKS[t])

@@ -21,9 +21,7 @@ BANK = 512
 BLOCK = 128
 SLOTS = range(4)
 ROW_BLOCKS = range(4)
-Y_LOADS = ((0, (0, 1)), (0, (2, 3)), (1, (0, 1)), (1, (2, 3)))
-UNITS = (((0,), 0, 512), ((1,), 0, 512), ((0, 1), 512, 256)) + tuple(((s,), lo, 128) for lo in (768, 896) for s in range(2))
-Y_BOTH = ((0, 0), (0, 1))
+Y_LOADS = ((0, 0, J), (1, 0, J))
 
 
 def tile_lowrankplussoftthresholdedcrosscovarianc_d2p_kernel(
@@ -41,30 +39,20 @@ def tile_lowrankplussoftthresholdedcrosscovarianc_d2p_kernel(
             return {key: keep.tile(shape, dtype, name=f"{name}_{i}", align_bytes=64) for i, key in enumerate(keys)}
 
         x_raw = tiles("x_raw", [128, 4, BANK], BF16, pairs)
-        y_raw = {(q, rows[0]): keep.tile([128, len(rows), J], U8, name=f"y_raw_{q}{rows[0]}", align_bytes=64) for q, rows in Y_LOADS}
-        y_wide = tiles("y_wide", [128, 4, J], BF16, range(2))
-
-        def runs(name, words, dtype, together):
-            made = tiles(name, [128, words], dtype, [key for key in pairs if key not in together])
-            made[together] = keep.tile([128, 2 * words], dtype, name=f"{name}_both", align_bytes=64)
-            for i, key in enumerate(together):
-                made[key] = made[together][:, words * i : words * (i + 1)]
-            return made
-
-        x_laid, x_code, x_sc = tiles("x_laid", [128, 4 * BANK], BF16, pairs), tiles("x_code", [128, BANK], U32, pairs), tiles("x_sc", [128, BANK], U8, pairs)
-        y_laid, y_code, y_sc = runs("y_laid", 4 * BANK, BF16, Y_BOTH), runs("y_code", BANK, U32, Y_BOTH), runs("y_sc", BANK, U8, Y_BOTH)
+        y_raw = {(q, lo): keep.tile([128, 4, hi - lo], U8, name=f"y_raw_{q}_{lo}", align_bytes=64) for q, lo, hi in Y_LOADS}
+        x_laid, x_code, x_sc = tiles("x_laid", [128, 4 * BANK], BF16, pairs[:3]), tiles("x_code", [128, BANK], U32, pairs), tiles("x_sc", [128, BANK], U8, pairs)
+        y_laid, y_code, y_sc = tiles("y_laid", [128, 4 * J], BF16, range(2)), tiles("y_code", [128, J], U32, range(2)), tiles("y_sc", [128, J], U8, range(2))
+        x_laid[1, 1] = x_laid[0, 1]
         upper = {(s, t): keep.tile([128, J], F32, name=f"upper_{s}{t}") for s in range(2) for t in SLOTS}
-        capped = keep.tile([128, 2, 4, J], BF16, name="capped")
-        lowered = keep.tile([128, 2, 4, J], BF16, name="lowered")
-        floored = keep.tile([128, 2, 4, J], BF16, name="floored")
-        sig_laid = {u: keep.tile([128, len(u[0]), u[2], 4], BF16, name=f"sig_laid_{i}", align_bytes=64) for i, u in enumerate(UNITS)}
-        sig_code = {u: keep.tile([128, len(u[0]), u[2]], U32, name=f"sig_code_{i}", align_bytes=64) for i, u in enumerate(UNITS)}
-        sig_sc = {u: keep.tile([128, len(u[0]), u[2]], U8, name=f"sig_sc_{i}", align_bytes=64) for i, u in enumerate(UNITS)}
+        capped = tiles("capped", [128, 4, J], BF16, range(2))
+        lowered = tiles("lowered", [128, 4, J], BF16, range(2))
+        floored = tiles("floored", [128, 4, J], BF16, range(2))
+        sig_laid, sig_code, sig_sc = tiles("sig_laid", [128, 4 * J], BF16, range(2)), tiles("sig_code", [128, J], U32, range(2)), tiles("sig_sc", [128, J], U8, range(2))
         l_sb = keep.tile([128, 2, 4, K], BF16, name="l_sb")
         m_sb = keep.tile([K, J], BF16, name="m_sb")
         l_t = keep.tile([K, 8, 128], BF16, name="l_t")
         ident = keep.tile([128, 128], BF16, name="ident")
-        y_fac = keep.tile([128, 2, 8], F32, name="y_fac")
+        y_fac = tiles("y_fac", [128, 8], F32, range(2))
         g_sb = keep.tile([128, 8], BF16, name="g_sb")
         tau_sb = keep.tile([128, 8], BF16, name="tau_sb")
         g_over_t = keep.tile([128, 8], F32, name="g_over_t")
@@ -77,19 +65,21 @@ def tile_lowrankplussoftthresholdedcrosscovarianc_d2p_kernel(
         x_v = x.rearrange("(q p j) n -> q p j n", q=2, p=128, j=4)
         y_v = y_bytes.rearrange("(q p j) n -> q p j n", q=2, p=128, j=4)
 
-        def load_y(q):
-            for of_pass, rows in Y_LOADS:
-                if of_pass == q:
-                    nc.sync.dma_start(out=y_raw[q, rows[0]][:], in_=y_v[q][:, rows[0] : rows[-1] + 1, :])
+        def load_y(i):
+            q, lo, hi = Y_LOADS[i]
+            nc.sync.dma_start(out=y_raw[q, lo][:], in_=y_v[q][:, :, lo:hi])
 
         def load_x(q, s):
             nc.sync.dma_start(out=x_raw[q, s][:], in_=x_v[q][:, :, BANK * s : BANK * (s + 1)])
 
-        def load_by_slot(tile, vector):
-            nc.sync.dma_start(out=tile[:].rearrange("p (s t) -> p s t", s=2), in_=vector.rearrange("(s p t) -> p s t", s=2, p=128, t=4))
+        def load_by_slot(tile, vector, queue):
+            queue.dma_start(out=tile[:].rearrange("p (s t) -> p s t", s=2), in_=vector.rearrange("(s p t) -> p s t", s=2, p=128, t=4))
 
         def load_l():
             nc.sync.dma_start(out=l_sb[:], in_=l.rearrange("(s p t) k -> p s t k", s=2, p=128, t=4))
+
+        def load_m():
+            nc.sync.dma_start(out=m_sb[:], in_=m)
 
         def load_w():
             nc.sync.dma_start(out=w_code[:].bitcast(I32), in_=w_words.bitcast(I32).rearrange("s p n -> p s n"))
@@ -100,21 +90,14 @@ def tile_lowrankplussoftthresholdedcrosscovarianc_d2p_kernel(
                     in_=w_scales[:, 4 * i : 4 * i + 4, :].bitcast(I32).rearrange("s r n -> r s n"),
                 )
 
-        def load_y_scale():
-            for q in range(2):
-                nc.scalar.dma_start(out=y_fac[:, q, :], in_=y_scale[4 * q : 4 * q + 4, :].unsqueeze(1).to_broadcast([4, 32, 8]))
+        def load_y_scale(q):
+            nc.scalar.dma_start(out=y_fac[q][:], in_=y_scale[4 * q : 4 * q + 4, :].unsqueeze(1).to_broadcast([4, 32, 8]))
 
         vector_copy = nc.vector.tensor_copy
         scalar_copy = nc.scalar.copy
 
         def gpsimd_copy(out, in_):
             nc.gpsimd.tensor_scalar(out=out, in0=in_, scalar1=1.0, scalar2=0.0, op0=ALU.mult, op1=ALU.add)
-
-        def vector_scale(out, in_, factor):
-            nc.vector.tensor_scalar(out=out, in0=in_, scalar1=factor, scalar2=None, op0=ALU.mult)
-
-        def scalar_scale(out, in_, factor):
-            nc.scalar.activation(out=out, in_=in_, func=ACT.Copy, scale=factor)
 
         def scalar_shift(out, in_, term):
             nc.scalar.activation(out=out, in_=in_, func=ACT.Identity, bias=term)
@@ -128,49 +111,61 @@ def tile_lowrankplussoftthresholdedcrosscovarianc_d2p_kernel(
         def bank(i, name, dtype=F32, columns=BANK):
             return psum.tile([128, columns], dtype, name=name, tag=f"bank_{i}")
 
-        def y_widen(q, j0, j1, lo, hi, copy):
-            first = max(r[0] for of_pass, r in Y_LOADS if of_pass == q and r[0] <= j0)
-            copy(out=y_wide[q][:, j0:j1, lo:hi], in_=y_raw[q, first][:, j0 - first : j1 - first, lo:hi].bitcast(FP8))
+        def words(laid, lo, hi):
+            return laid[:, 4 * lo : 4 * hi]
 
-        def y_lay(q, h, blocks, scale):
+        def quantise(code, scale, laid, lo, hi):
+            nc.vector.quantize_mx(out=code[:, lo:hi].bitcast(FP8X4), scales=scale[:, lo:hi], in_=words(laid, lo, hi))
+
+        def y_lay(q, blocks):
             for b in blocks:
-                lo = BANK * h + BLOCK * b
-                scale(
-                    y_laid[q, h][:, 4 * BLOCK * b : 4 * BLOCK * (b + 1)].rearrange("p (c i j) -> p c j i", i=4, j=4),
-                    y_wide[q][:, :, lo : lo + BLOCK].rearrange("p j (c i) -> p c j i", i=4),
-                    y_fac[:, q, 4 * h + b : 4 * h + b + 1],
+                lo = BLOCK * b
+                first = max(a for of_pass, a, z in Y_LOADS if of_pass == q and a <= lo)
+                nc.vector.tensor_scalar(
+                    out=words(y_laid[q], lo, lo + BLOCK).rearrange("p (c i j) -> p c j i", i=4, j=4),
+                    in0=y_raw[q, first][:, :, lo - first : lo - first + BLOCK].bitcast(FP8).rearrange("p j (c i) -> p c j i", i=4),
+                    scalar1=y_fac[q][:, b : b + 1],
+                    scalar2=None,
+                    op0=ALU.mult,
                 )
 
-        def y_quant(key):
-            nc.vector.quantize_mx(out=y_code[key][:].bitcast(FP8X4), scales=y_sc[key][:], in_=y_laid[key][:])
+        def y_quant(q, lo, hi):
+            quantise(y_code[q], y_sc[q], y_laid[q], lo, hi)
 
-        def x_lay(q, s, a0, a1):
-            vector_copy(
-                out=x_laid[q, s][:].rearrange("p (t u e j) -> p u j e t", t=4, e=2, j=4)[:, 32 * a0 : 32 * a1],
-                in_=x_raw[q, s][:].rearrange("p j (u e t) -> p u j e t", e=2, t=4)[:, 32 * a0 : 32 * a1],
+        def x_lay(q, s, lo, hi, copy):
+            copy(
+                out=x_laid[q, s][:].rearrange("p (t u e j) -> p u j e t", t=4, e=2, j=4)[:, lo // 8 : hi // 8],
+                in_=x_raw[q, s][:].rearrange("p j (u e t) -> p u j e t", e=2, t=4)[:, lo // 8 : hi // 8],
+            )
+
+        def x_lay_in_order(q, s, lo, hi):
+            gpsimd_copy(
+                out=x_laid[q, s][:].rearrange("p (t r j) -> p r t j", t=4, j=4)[:, lo // 4 : hi // 4],
+                in_=x_raw[q, s][:].rearrange("p j (r t) -> p r t j", t=4)[:, lo // 4 : hi // 4],
             )
 
         pair_ps = {}
 
-        def x_pair(q, s, a, i):
-            pair_ps[q, s, a] = bank(i, "ps_pair", BF16, 2 * BANK)
+        def x_pair(q, s, lo, hi, i):
+            n = hi - lo
+            pair_ps[q, s, lo] = bank(i, "ps_pair", BF16, 4 * n)
             for u in range(2):
                 nc.tensor.matmul(
-                    pair_ps[q, s, a][:, BANK * u : BANK * (u + 1)].rearrange("p (c e) -> p e c", e=2),
+                    pair_ps[q, s, lo][:, 2 * n * u : 2 * n * (u + 1)].rearrange("p (c e) -> p e c", e=2),
                     ident[:],
-                    x_raw[q, s][:, 2 * u : 2 * u + 2, 256 * a : 256 * (a + 1)],
+                    x_raw[q, s][:, 2 * u : 2 * u + 2, lo:hi],
                     start=True,
                     stop=True,
                 )
 
-        def x_fetch(q, s, a):
-            scalar_copy(
-                out=x_laid[q, s][:].bitcast(F32).rearrange("p (t r u) -> p t r u", t=4, u=2)[:, :, 64 * a : 64 * (a + 1), :],
-                in_=pair_ps[q, s, a][:].bitcast(F32).rearrange("p (u r t) -> p t r u", u=2, t=4),
+        def x_fetch(q, s, lo, hi, copy):
+            copy(
+                out=x_laid[q, s][:].bitcast(F32).rearrange("p (t r u) -> p t r u", t=4, u=2)[:, :, lo // 4 : hi // 4, :],
+                in_=pair_ps[q, s, lo][:].bitcast(F32).rearrange("p (u r t) -> p t r u", u=2, t=4),
             )
 
-        def x_quant(key):
-            nc.vector.quantize_mx(out=x_code[key][:].bitcast(FP8X4), scales=x_sc[key][:], in_=x_laid[key][:])
+        def x_quant(q, s):
+            quantise(x_code[q, s], x_sc[q, s], x_laid[q, s], 0, BANK)
 
         turn_ps = {}
 
@@ -184,16 +179,19 @@ def tile_lowrankplussoftthresholdedcrosscovarianc_d2p_kernel(
             scalar_copy(out=l_t[:].rearrange("p t n -> p (t n)"), in_=turn_ps[0][:])
 
         def factors_of_g():
-            vector_scale(g_over_t[:], g_sb[:], 1.0 / T)
-            nc.vector.scalar_tensor_tensor(out=g_abs[:], in0=g_sb[:], scalar=-1.0, in1=g_sb[:], op0=ALU.mult, op1=ALU.max)
+            nc.scalar.activation(out=g_over_t[:], in_=g_sb[:], func=ACT.Copy, scale=1.0 / T)
+            nc.scalar.activation(out=g_abs[:], in_=g_sb[:], func=ACT.Abs)
 
         def widths():
             nc.vector.tensor_tensor(out=width[:], in0=g_abs[:], in1=tau_sb[:], op=ALU.mult)
 
         def spans():
-            nc.vector.scalar_tensor_tensor(out=span_down[:], in0=tau_sb[:], scalar=-2.0, in1=g_abs[:], op0=ALU.mult, op1=ALU.mult)
+            nc.scalar.activation(out=span_down[:], in_=width[:], func=ACT.Copy, scale=-2.0)
 
         cross_ps, low_ps, out_ps = {}, {}, {}
+
+        def half(h):
+            return slice(BANK * h, BANK * (h + 1))
 
         def cross_pass(h, s, t, q, i=None):
             if q == 0:
@@ -202,8 +200,8 @@ def tile_lowrankplussoftthresholdedcrosscovarianc_d2p_kernel(
                 out=cross_ps[h, s, t][:],
                 lhsT=x_code[q, s][:, 128 * t : 128 * t + 128].bitcast(FP8X4),
                 lhsT_scale=x_sc[q, s][:, 128 * t : 128 * t + 128],
-                rhs=y_code[q, h][:].bitcast(FP8X4),
-                rhs_scale=y_sc[q, h][:],
+                rhs=y_code[q][:, half(h)].bitcast(FP8X4),
+                rhs_scale=y_sc[q][:, half(h)],
                 start=(q == 0),
                 stop=(q == 1),
             )
@@ -211,9 +209,6 @@ def tile_lowrankplussoftthresholdedcrosscovarianc_d2p_kernel(
         def cross(h, s, t, i):
             cross_pass(h, s, t, 0, i)
             cross_pass(h, s, t, 1)
-
-        def half(h):
-            return slice(BANK * h, BANK * (h + 1))
 
         def lift(h, s, t):
             nc.scalar.activation(
@@ -228,86 +223,70 @@ def tile_lowrankplussoftthresholdedcrosscovarianc_d2p_kernel(
 
         def cap(s, t, lo, hi):
             nc.vector.scalar_tensor_tensor(
-                out=capped[:, s, t, lo:hi], in0=low_ps[s, t, lo], scalar=of_slot(g_sb, s, t), in1=upper[s, t][:, lo:hi], op0=ALU.mult, op1=ALU.min
+                out=capped[s][:, t, lo:hi], in0=low_ps[s, t, lo], scalar=of_slot(g_sb, s, t), in1=upper[s, t][:, lo:hi], op0=ALU.mult, op1=ALU.min
             )
 
         def lower(s, slots, lo, hi, shift):
             for t in slots:
-                shift(lowered[:, s, t, lo:hi], upper[s, t][:, lo:hi], of_slot(span_down, s, t))
+                shift(lowered[s][:, t, lo:hi], upper[s, t][:, lo:hi], of_slot(span_down, s, t))
 
-        def floor(groups, lo, hi):
-            part = (slice(None), slice(groups[0], groups[-1] + 1), slice(None), slice(lo, hi))
-            nc.vector.tensor_tensor(out=floored[part], in0=capped[part], in1=lowered[part], op=ALU.max)
+        def floor(s, slots, lo, hi):
+            part = (slice(None), slice(slots[0], slots[-1] + 1), slice(lo, hi))
+            nc.vector.tensor_tensor(out=floored[s][part], in0=capped[s][part], in1=lowered[s][part], op=ALU.max)
 
         def floor_by_slot(s, t, lo, hi):
             nc.vector.scalar_tensor_tensor(
-                out=floored[:, s, t, lo:hi], in0=upper[s, t][:, lo:hi], scalar=of_slot(span_down, s, t), in1=capped[:, s, t, lo:hi], op0=ALU.add, op1=ALU.max
+                out=floored[s][:, t, lo:hi], in0=upper[s, t][:, lo:hi], scalar=of_slot(span_down, s, t), in1=capped[s][:, t, lo:hi], op0=ALU.add, op1=ALU.max
             )
 
-        def unit_of(s, lo):
-            return [u for u in UNITS if s in u[0] and u[1] <= lo < u[1] + u[2]][0]
-
-        def in_unit(tiles_by_unit, s, lo, hi):
-            u = unit_of(s, lo)
-            return tiles_by_unit[u][:, u[0].index(s), lo - u[1] : hi - u[1]]
-
         def laid(s, lo, hi, run):
-            return in_unit(sig_laid, s, lo, hi).rearrange("p (c i) t -> p c t i", i=run)
+            return words(sig_laid[s], lo, hi).rearrange("p (c i t) -> p c t i", i=run, t=4)
 
-        def by_slot(tile, s, lo, hi, run):
-            return tile[:, s, :, lo:hi].rearrange("p t (c i) -> p c t i", i=run)
+        def by_slot(tile, lo, hi, run):
+            return tile[:, :, lo:hi].rearrange("p t (c i) -> p c t i", i=run)
 
         def floor_and_lay(s, lo, hi):
-            nc.vector.tensor_tensor(out=laid(s, lo, hi, 4), in0=by_slot(capped, s, lo, hi, 4), in1=by_slot(lowered, s, lo, hi, 4), op=ALU.max)
+            nc.vector.tensor_tensor(out=laid(s, lo, hi, 4), in0=by_slot(capped[s], lo, hi, 4), in1=by_slot(lowered[s], lo, hi, 4), op=ALU.max)
 
         def sig_lay(s, lo, hi, copy):
             run = 1 if copy is gpsimd_copy else 4
-            copy(out=laid(s, lo, hi, run), in_=by_slot(floored, s, lo, hi, run))
+            copy(out=laid(s, lo, hi, run), in_=by_slot(floored[s], lo, hi, run))
 
         def sig_pair(s, lo, hi, i):
-            w = hi - lo
-            pair_ps[s, lo] = bank(i, "ps_pair", BF16, 4 * w)
+            n = hi - lo
+            pair_ps[s, lo] = bank(i, "ps_pair", BF16, 4 * n)
             for u in range(2):
                 nc.tensor.matmul(
-                    pair_ps[s, lo][:, 2 * w * u : 2 * w * (u + 1)].rearrange("p (c e) -> p e c", e=2),
+                    pair_ps[s, lo][:, 2 * n * u : 2 * n * (u + 1)].rearrange("p (c e) -> p e c", e=2),
                     ident[:],
-                    floored[:, s, 2 * u : 2 * u + 2, lo:hi],
+                    floored[s][:, 2 * u : 2 * u + 2, lo:hi],
                     start=True,
                     stop=True,
                 )
 
         def sig_fetch(s, lo, hi):
             scalar_copy(
-                out=in_unit(sig_laid, s, lo, hi).bitcast(F32),
+                out=words(sig_laid[s], lo, hi).bitcast(F32).rearrange("p (c u) -> p c u", u=2),
                 in_=pair_ps[s, lo][:].bitcast(F32).rearrange("p (u c) -> p c u", u=2),
             )
 
-        def sig_quant(s, lo):
-            u = unit_of(s, lo)
-            nc.vector.quantize_mx(
-                out=sig_code[u][:].rearrange("p s n -> p (s n)").bitcast(FP8X4),
-                scales=sig_sc[u][:].rearrange("p s n -> p (s n)"),
-                in_=sig_laid[u][:].rearrange("p s n t -> p (s n t)"),
-            )
+        def sig_quant(s, lo, hi):
+            quantise(sig_code[s], sig_sc[s], sig_laid[s], lo, hi)
 
         def exposure(lo, hi, s, blocks, i=None):
-            w = hi - lo
+            n = hi - lo
             if s == 0:
                 out_ps[lo, blocks[0]] = bank(i, "ps_out")
-            for n, b in enumerate(blocks):
+            for k, b in enumerate(blocks):
                 nc.tensor.matmul_mx(
-                    out=out_ps[lo, blocks[0]][:, w * n : w * (n + 1)],
+                    out=out_ps[lo, blocks[0]][:, n * k : n * (k + 1)],
                     lhsT=w_code[:, s, 256 * b : 256 * b + 256].bitcast(FP4X4),
                     lhsT_scale=w_sc[:, s, 128 * b : 128 * b + 128],
-                    rhs=in_unit(sig_code, s, lo, hi).bitcast(FP8X4),
-                    rhs_scale=in_unit(sig_sc, s, lo, hi),
-                    start=(s == 0 and n == 0),
-                    stop=(s == 1 and n == len(blocks) - 1),
+                    rhs=sig_code[s][:, lo:hi].bitcast(FP8X4),
+                    rhs_scale=sig_sc[s][:, lo:hi],
+                    start=(s == 0 and k == 0),
+                    stop=(s == 1 and k == len(blocks) - 1),
                 )
-
-        def both_passes(lo, hi, blocks, i):
-            exposure(lo, hi, 0, blocks, i)
-            exposure(lo, hi, 1, blocks)
 
         def store(lo, hi, blocks, copy, queue=nc.sync):
             n = len(blocks) * (hi - lo)
@@ -318,156 +297,138 @@ def tile_lowrankplussoftthresholdedcrosscovarianc_d2p_kernel(
                 in_=staged[:].rearrange("p (b n) -> p b n", b=len(blocks)),
             )
 
-
+        load_y_scale(0)
+        load_y_scale(1)
+        load_by_slot(g_sb, g, nc.scalar)
+        load_by_slot(tau_sb, tau, nc.scalar)
         load_y(0)
         load_x(0, 0)
         load_y(1)
         load_x(1, 0)
         load_l()
-        load_by_slot(g_sb, g)
-        load_by_slot(tau_sb, tau)
         load_x(0, 1)
+        load_m()
         load_x(1, 1)
-        nc.sync.dma_start(out=m_sb[:], in_=m)
         load_w()
-        load_y_scale()
         make_identity(nc, ident[:])
 
-        y_widen(0, 0, 1, 0, J, vector_copy)
-        y_widen(0, 1, 2, 0, J, scalar_copy)
-        y_widen(0, 2, 3, 0, J, vector_copy)
-        y_widen(0, 3, 4, 0, BANK, vector_copy)
-        y_widen(0, 3, 4, BANK, J, scalar_copy)
-        y_lay(0, 1, (1, 2, 3), scalar_scale)
-        y_lay(0, 1, (0,), vector_scale)
-        y_lay(0, 0, range(4), vector_scale)
-        x_pair(0, 0, 0, 0)
-        x_pair(0, 0, 1, 1)
-        y_widen(1, 0, 1, 0, J, vector_copy)
-        y_widen(1, 1, 2, 0, J, scalar_copy)
-        y_widen(1, 2, 3, 0, BANK, vector_copy)
-        y_widen(1, 3, 4, 0, J, scalar_copy)
-        y_quant(Y_BOTH)
-        x_fetch(0, 0, 0)
-        x_fetch(0, 0, 1)
-        y_lay(1, 0, range(4), vector_scale)
-        x_pair(1, 0, 0, 2)
-        x_pair(1, 0, 1, 3)
-        x_quant((0, 0))
+        RING = (4, 5, 6, 7)
+        y_lay(0, range(8))
+        x_pair(0, 0, 256, 512, 0)
+        x_lay(0, 0, 0, 256, scalar_copy)
         factors_of_g()
-        y_quant((1, 0))
+        x_fetch(0, 0, 256, 512, scalar_copy)
+        y_quant(0, 0, 512)
+        y_lay(1, range(4))
+        x_pair(1, 0, 256, 512, 1)
+        turn_l(2)
+        x_lay(1, 0, 0, 256, scalar_copy)
+        x_fetch(1, 0, 256, 512, scalar_copy)
         widths()
-        x_fetch(1, 0, 0)
-        y_widen(1, 2, 3, BANK, J, scalar_copy)
-        x_fetch(1, 0, 1)
-        turn_l(0)
-        for t in (0, 1):
-            cross_pass(0, 0, t, 0, 4 + t)
-        x_pair(0, 1, 0, 1)
-        x_quant((1, 0))
+        x_quant(0, 0)
         fetch_l()
-        y_lay(1, 1, (0, 1), scalar_scale)
-        for t in (0, 1):
-            cross_pass(0, 0, t, 1)
-        for t in (2, 3):
-            cross(0, 0, t, 4 + t)
-        x_lay(0, 1, 1, 2)
-        x_lay(1, 1, 0, 2)
-        lift(0, 0, 0)
-        x_fetch(0, 1, 0)
-        for t in (1, 2, 3):
-            lift(0, 0, t)
-        y_lay(1, 1, (3,), vector_scale)
-        x_quant((1, 1))
         spans()
-        x_quant((0, 1))
+        y_quant(1, 0, 512)
+        x_lay(0, 1, 256, 512, vector_copy)
         for t in SLOTS:
-            low_rank(0, (t,), 0, 512, (2, 3, 0, 1)[t])
-
-        LOW_BANKS, CROSS_BANKS = (2, 3, 0, 1), (4, 5, 6, 7)
-        lower(0, (0, 1), 0, 512, gpsimd_shift)
-        lower(0, (2,), 0, 256, gpsimd_shift)
-        y_lay(1, 1, (2,), scalar_scale)
-        lower(0, (3,), 0, 512, scalar_shift)
-        lower(0, (2,), 256, 512, scalar_shift)
+            cross_pass(0, 0, t, 0, RING[t])
+        x_lay(0, 1, 0, 256, scalar_copy)
+        x_quant(1, 0)
+        for t in SLOTS:
+            cross_pass(0, 0, t, 1)
+            low_rank(0, (t,), 0, 512, (3, 0, 1, 2)[t])
+        y_lay(1, (4, 5))
+        for t in SLOTS:
+            lift(0, 0, t)
+        y_quant(0, 512, J)
+        x_quant(0, 1)
+        x_lay_in_order(1, 1, 0, 320)
         for t in SLOTS:
             cap(0, t, 0, 512)
-            cross(0, 1, t, CROSS_BANKS[t])
-            lift(0, 1, t)
+        x_pair(1, 1, 320, 512, RING[0])
+        x_fetch(1, 1, 320, 512, scalar_copy)
+        lower(0, (0, 1, 2), 0, 512, scalar_shift)
+        for t in (1, 2, 3):
+            cross_pass(0, 1, t, 0, RING[t])
+        cross_pass(0, 1, 0, 0, RING[0])
+        y_lay(1, (6,))
+        x_quant(1, 1)
+        y_lay(1, (7,))
         for t in SLOTS:
-            low_rank(1, (t,), 0, 512, LOW_BANKS[t])
-        y_quant((1, 1))
-        floor((0,), 0, 384)
-        floor((0,), 384, 512)
+            cross_pass(0, 1, t, 1)
+            low_rank(1, (t,), 0, 512, (3, 0, 1, 2)[t])
+            lift(0, 1, t)
+        floor_by_slot(0, 3, 0, 512)
+        floor(0, (0, 1, 2), 0, 512)
+        y_quant(1, 512, J)
         sig_lay(0, 0, 384, gpsimd_copy)
         for t in SLOTS:
             cap(1, t, 0, 512)
-            cross(1, 0, t, CROSS_BANKS[t])
+        lower(1, (0, 1, 2), 0, 512, scalar_shift)
+        for t in SLOTS:
+            cross(1, 0, t, RING[t])
             lift(1, 0, t)
-        sig_lay(0, 384, 512, scalar_copy)
-        low_rank(0, (0, 1), 512, 768, 2)
-        low_rank(0, (2, 3), 512, 768, 3)
+            low_rank(0, (t,), 512, J, (3, 0, 1, 2)[t])
         for t in SLOTS:
-            cross(1, 1, t, CROSS_BANKS[t])
+            cross(1, 1, t, RING[t])
             lift(1, 1, t)
-        low_rank(1, (0, 1), 512, 768, 0)
-        low_rank(1, (2, 3), 512, 768, 1)
-        for t in SLOTS:
-            floor_by_slot(1, t, 0, 512)
-        sig_quant(0, 0)
+        sig_lay(0, 384, 512, vector_copy)
+        floor_by_slot(1, 3, 0, 512)
+        floor(1, (0, 1, 2), 0, 512)
+        sig_quant(0, 0, 512)
         sig_lay(1, 0, 512, gpsimd_copy)
+        lower(0, (0,), 512, 768, gpsimd_shift)
         for t in SLOTS:
-            cap(0, t, 512, 768)
-        lower(0, SLOTS, 512, 768, scalar_shift)
-        for b in (0, 1):
-            exposure(0, 512, 0, (b,), CROSS_BANKS[b])
-        low_rank(0, (0, 1), 768, J, 2)
-        low_rank(0, (2, 3), 768, J, 3)
+            cap(0, t, 512, J)
+        low_rank(1, (0, 1), 512, 768, 3)
+        low_rank(1, (2, 3), 512, 768, 0)
+        low_rank(1, (0, 1), 768, J, 1)
+        low_rank(1, (2, 3), 768, J, 2)
         for t in SLOTS:
             cap(1, t, 512, 768)
-        low_rank(1, (0, 1), 768, J, 0)
-        low_rank(1, (2, 3), 768, J, 1)
-        for b in (2, 3):
-            exposure(0, 512, 0, (b,), CROSS_BANKS[b])
-        lower(1, SLOTS, 512, 768, scalar_shift)
-        cap(0, 0, 768, J)
-        floor((0,), 512, 768)
-        floor((1,), 512, 768)
-        sig_quant(1, 0)
+        for b in ROW_BLOCKS:
+            exposure(0, 512, 0, (b,), RING[b])
+        sig_quant(1, 0, 512)
         for b in ROW_BLOCKS:
             exposure(0, 512, 1, (b,))
-        sig_lay(1, 512, 768, gpsimd_copy)
-        lower(0, SLOTS, 768, J, scalar_shift)
-        sig_lay(0, 512, 768, scalar_copy)
-        lower(1, (0, 1), 768, J, scalar_shift)
-        store(0, 512, (0,), scalar_copy)
-        lower(1, (2, 3), 768, J, scalar_shift)
-        store(0, 512, (1,), scalar_copy)
-        store(0, 512, (2,), scalar_copy)
-        store(0, 512, (3,), scalar_copy)
-        for t in (1, 2, 3):
-            cap(0, t, 768, J)
-        for t in (0, 1, 2):
+        lower(0, (1, 2, 3), 512, 768, scalar_shift)
+        lower(1, (0, 1, 2), 512, 768, scalar_shift)
+        floor(0, SLOTS, 512, 768)
+        sig_pair(0, 512, 768, 3)
+        floor_by_slot(1, 3, 512, 768)
+        floor(1, (0, 1, 2), 512, 768)
+        sig_lay(1, 512, 704, gpsimd_copy)
+        for t in SLOTS:
             cap(1, t, 768, J)
-        sig_quant(0, 512)
-        cap(1, 3, 768, J)
-        both_passes(512, 768, (0, 1), 2)
-        both_passes(512, 768, (2, 3), 3)
+        lower(0, SLOTS, 768, J, scalar_shift)
+        store(0, 512, (0,), scalar_copy)
+        lower(1, (0, 1), 768, J, scalar_shift)
+        sig_fetch(0, 512, 768)
+        lower(1, (2, 3), 768, J, scalar_shift)
+        for b in (1, 2, 3):
+            store(0, 512, (b,), scalar_copy)
+        sig_lay(1, 704, 768, vector_copy)
         floor_and_lay(0, 768, 896)
+        sig_quant(1, 512, 768)
+        sig_quant(0, 512, 768)
+        exposure(512, 768, 0, (0, 1), 0)
+        exposure(512, 768, 1, (0, 1))
+        exposure(512, 768, 0, (2, 3), 3)
+        exposure(512, 768, 1, (2, 3))
+        sig_quant(0, 768, 896)
+        exposure(768, 896, 0, ROW_BLOCKS, 1)
         floor_and_lay(1, 768, 896)
         store(512, 768, (0, 1), scalar_copy)
         store(512, 768, (2, 3), scalar_copy)
-        sig_quant(0, 768)
-        exposure(768, 896, 0, ROW_BLOCKS, 1)
-        sig_quant(1, 768)
+        floor_and_lay(0, 896, J)
+        sig_quant(1, 768, 896)
         exposure(768, 896, 1, ROW_BLOCKS)
         store(768, 896, ROW_BLOCKS, scalar_copy)
-        floor_and_lay(0, 896, J)
         floor_and_lay(1, 896, J)
-        sig_quant(0, 896)
+        sig_quant(0, 896, J)
         for b in ROW_BLOCKS:
-            exposure(896, J, 0, (b,), CROSS_BANKS[b])
-        sig_quant(1, 896)
+            exposure(896, J, 0, (b,), RING[b])
+        sig_quant(1, 896, J)
         for b in ROW_BLOCKS:
             exposure(896, J, 1, (b,))
         for b in ROW_BLOCKS:

@@ -275,7 +275,7 @@ def tile_lowrankplussoftthresholdedcrosscovarianc_d2p_kernel(
 
         def exposure(lo, hi, s, blocks, i=None):
             n = hi - lo
-            if s == 0:
+            if i is not None:
                 out_ps[lo, blocks[0]] = bank(i, "ps_out")
             for k, b in enumerate(blocks):
                 nc.tensor.matmul_mx(
@@ -284,8 +284,8 @@ def tile_lowrankplussoftthresholdedcrosscovarianc_d2p_kernel(
                     lhsT_scale=w_sc[:, s, 128 * b : 128 * b + 128],
                     rhs=sig_code[s][:, lo:hi].bitcast(FP8X4),
                     rhs_scale=sig_sc[s][:, lo:hi],
-                    start=(s == 0 and k == 0),
-                    stop=(s == 1 and k == len(blocks) - 1),
+                    start=(i is not None and k == 0),
+                    stop=(i is None and k == len(blocks) - 1),
                 )
 
         def store(lo, hi, blocks, copy, queue=nc.sync):
@@ -299,64 +299,73 @@ def tile_lowrankplussoftthresholdedcrosscovarianc_d2p_kernel(
 
         load_y_scale(0)
         load_y_scale(1)
-        load_by_slot(g_sb, g, nc.scalar)
-        load_by_slot(tau_sb, tau, nc.scalar)
         load_y(0)
         load_x(0, 0)
         load_y(1)
         load_x(1, 0)
         load_l()
+        load_by_slot(g_sb, g, nc.sync)
+        load_by_slot(tau_sb, tau, nc.sync)
         load_x(0, 1)
-        load_m()
         load_x(1, 1)
+        load_m()
         load_w()
         make_identity(nc, ident[:])
 
-        RING = (4, 5, 6, 7)
+        RING, LOW = (4, 5, 6, 7), (3, 0, 1, 2)
         y_lay(0, range(8))
-        x_pair(0, 0, 256, 512, 0)
-        x_lay(0, 0, 0, 256, scalar_copy)
-        factors_of_g()
-        x_fetch(0, 0, 256, 512, scalar_copy)
+        x_pair(0, 0, 128, 384, 0)
+        x_pair(0, 0, 384, 512, 1)
+        x_lay(0, 0, 0, 128, scalar_copy)
+        x_fetch(0, 0, 128, 384, scalar_copy)
+        x_fetch(0, 0, 384, 512, scalar_copy)
         y_quant(0, 0, 512)
-        y_lay(1, range(4))
-        x_pair(1, 0, 256, 512, 1)
-        turn_l(2)
-        x_lay(1, 0, 0, 256, scalar_copy)
-        x_fetch(1, 0, 256, 512, scalar_copy)
-        widths()
+        y_lay(1, (0, 1))
         x_quant(0, 0)
-        fetch_l()
-        spans()
-        y_quant(1, 0, 512)
-        x_lay(0, 1, 256, 512, vector_copy)
+        y_lay(1, (2, 3))
+        x_pair(1, 0, 256, 512, 2)
         for t in SLOTS:
             cross_pass(0, 0, t, 0, RING[t])
-        x_lay(0, 1, 0, 256, scalar_copy)
+        turn_l(LOW[0])
+        x_lay(1, 0, 0, 256, scalar_copy)
+        x_fetch(1, 0, 256, 512, scalar_copy)
+        factors_of_g()
+        y_lay(1, (4,))
+        y_quant(1, 0, 512)
         x_quant(1, 0)
-        for t in SLOTS:
+        widths()
+        x_pair(0, 1, 384, 512, 1)
+        x_lay(0, 1, 0, 256, scalar_copy)
+        fetch_l()
+        x_fetch(0, 1, 384, 512, scalar_copy)
+        x_lay(0, 1, 256, 384, vector_copy)
+        y_lay(1, (5,))
+        LOW = (0, 1, 2, 3)
+        cross_pass(0, 0, 0, 1)
+        for t in (1, 2, 3):
             cross_pass(0, 0, t, 1)
-            low_rank(0, (t,), 0, 512, (3, 0, 1, 2)[t])
-        y_lay(1, (4, 5))
-        for t in SLOTS:
+            low_rank(0, (t - 1,), 0, 512, LOW[t - 1])
+        lift(0, 0, 0)
+        x_pair(1, 1, 320, 512, RING[0])
+        low_rank(0, (3,), 0, 512, LOW[3])
+        spans()
+        for t in (1, 2, 3):
             lift(0, 0, t)
         y_quant(0, 512, J)
         x_quant(0, 1)
         x_lay_in_order(1, 1, 0, 320)
         for t in SLOTS:
             cap(0, t, 0, 512)
-        x_pair(1, 1, 320, 512, RING[0])
         x_fetch(1, 1, 320, 512, scalar_copy)
         lower(0, (0, 1, 2), 0, 512, scalar_shift)
         for t in (1, 2, 3):
             cross_pass(0, 1, t, 0, RING[t])
         cross_pass(0, 1, 0, 0, RING[0])
-        y_lay(1, (6,))
         x_quant(1, 1)
-        y_lay(1, (7,))
+        y_lay(1, (6, 7))
         for t in SLOTS:
             cross_pass(0, 1, t, 1)
-            low_rank(1, (t,), 0, 512, (3, 0, 1, 2)[t])
+            low_rank(1, (t,), 0, 512, LOW[t])
             lift(0, 1, t)
         floor_by_slot(0, 3, 0, 512)
         floor(0, (0, 1, 2), 0, 512)
@@ -368,7 +377,7 @@ def tile_lowrankplussoftthresholdedcrosscovarianc_d2p_kernel(
         for t in SLOTS:
             cross(1, 0, t, RING[t])
             lift(1, 0, t)
-            low_rank(0, (t,), 512, J, (3, 0, 1, 2)[t])
+            low_rank(0, (t,), 512, J, LOW[t])
         for t in SLOTS:
             cross(1, 1, t, RING[t])
             lift(1, 1, t)
@@ -380,54 +389,57 @@ def tile_lowrankplussoftthresholdedcrosscovarianc_d2p_kernel(
         lower(0, (0,), 512, 768, gpsimd_shift)
         for t in SLOTS:
             cap(0, t, 512, J)
-        low_rank(1, (0, 1), 512, 768, 3)
-        low_rank(1, (2, 3), 512, 768, 0)
-        low_rank(1, (0, 1), 768, J, 1)
-        low_rank(1, (2, 3), 768, J, 2)
+        low_rank(1, (0, 1), 512, 768, LOW[0])
+        low_rank(1, (2, 3), 512, 768, LOW[1])
+        low_rank(1, (0, 1), 768, J, LOW[2])
+        low_rank(1, (2, 3), 768, J, LOW[3])
         for t in SLOTS:
             cap(1, t, 512, 768)
-        for b in ROW_BLOCKS:
+        for b in (0, 1):
             exposure(0, 512, 0, (b,), RING[b])
         sig_quant(1, 0, 512)
-        for b in ROW_BLOCKS:
+        for b in (0, 1):
             exposure(0, 512, 1, (b,))
         lower(0, (1, 2, 3), 512, 768, scalar_shift)
         lower(1, (0, 1, 2), 512, 768, scalar_shift)
         floor(0, SLOTS, 512, 768)
-        sig_pair(0, 512, 768, 3)
+        sig_pair(0, 512, 768, RING[2])
         floor_by_slot(1, 3, 512, 768)
         floor(1, (0, 1, 2), 512, 768)
-        sig_lay(1, 512, 704, gpsimd_copy)
+        sig_lay(1, 512, 768, gpsimd_copy)
         for t in SLOTS:
             cap(1, t, 768, J)
+        for b in (2, 3):
+            exposure(0, 512, 0, (b,), LOW[b])
+            exposure(0, 512, 1, (b,))
         lower(0, SLOTS, 768, J, scalar_shift)
         store(0, 512, (0,), scalar_copy)
-        lower(1, (0, 1), 768, J, scalar_shift)
+        store(0, 512, (1,), vector_copy)
         sig_fetch(0, 512, 768)
-        lower(1, (2, 3), 768, J, scalar_shift)
-        for b in (1, 2, 3):
+        lower(1, SLOTS, 768, J, scalar_shift)
+        for b in (2, 3):
             store(0, 512, (b,), scalar_copy)
-        sig_lay(1, 704, 768, vector_copy)
-        floor_and_lay(0, 768, 896)
-        sig_quant(1, 512, 768)
         sig_quant(0, 512, 768)
-        exposure(512, 768, 0, (0, 1), 0)
+        exposure(512, 768, 0, (0, 1), LOW[0])
+        exposure(512, 768, 0, (2, 3), LOW[1])
+        sig_quant(1, 512, 768)
         exposure(512, 768, 1, (0, 1))
-        exposure(512, 768, 0, (2, 3), 3)
         exposure(512, 768, 1, (2, 3))
-        sig_quant(0, 768, 896)
-        exposure(768, 896, 0, ROW_BLOCKS, 1)
+        floor_and_lay(0, 768, 896)
         floor_and_lay(1, 768, 896)
+        sig_quant(0, 768, 896)
+        exposure(768, 896, 0, ROW_BLOCKS, RING[3])
         store(512, 768, (0, 1), scalar_copy)
         store(512, 768, (2, 3), scalar_copy)
-        floor_and_lay(0, 896, J)
         sig_quant(1, 768, 896)
         exposure(768, 896, 1, ROW_BLOCKS)
+        floor_and_lay(0, 896, J)
         store(768, 896, ROW_BLOCKS, scalar_copy)
         floor_and_lay(1, 896, J)
         sig_quant(0, 896, J)
+        LAST = (RING[0], RING[1], RING[2], LOW[2])
         for b in ROW_BLOCKS:
-            exposure(896, J, 0, (b,), RING[b])
+            exposure(896, J, 0, (b,), LAST[b])
         sig_quant(1, 896, J)
         for b in ROW_BLOCKS:
             exposure(896, J, 1, (b,))

@@ -122,8 +122,8 @@ def tile_lowrankplussoftthresholdedcrosscovarianc_d2p_kernel(
                 lo = BLOCK * b
                 first = max(a for of_pass, a, z in Y_LOADS if of_pass == q and a <= lo)
                 nc.vector.tensor_scalar(
-                    out=words(y_laid[q], lo, lo + BLOCK).rearrange("p (c i j) -> p c j i", i=4, j=4),
-                    in0=y_raw[q, first][:, :, lo - first : lo - first + BLOCK].bitcast(FP8).rearrange("p j (c i) -> p c j i", i=4),
+                    out=words(y_laid[q], lo, lo + BLOCK).rearrange("p (c i j) -> p c j i", i=8, j=4),
+                    in0=y_raw[q, first][:, :, lo - first : lo - first + BLOCK].bitcast(FP8).rearrange("p j (c i) -> p c j i", i=8),
                     scalar1=y_fac[q][:, b : b + 1],
                     scalar2=None,
                     op0=ALU.mult,

@@ -21,7 +21,7 @@ BANK = 512
 BLOCK = 128
 SLOTS = range(4)
 ROW_BLOCKS = range(4)
-Y_LOADS = ((0, 0, J), (1, 0, J))
+Y_LOADS = ((0, 0, J), (1, 0, BANK), (1, BANK, J))
 
 
 def tile_lowrankplussoftthresholdedcrosscovarianc_d2p_kernel(
@@ -136,6 +136,12 @@ def tile_lowrankplussoftthresholdedcrosscovarianc_d2p_kernel(
             copy(
                 out=x_laid[q, s][:].rearrange("p (t u e j) -> p u j e t", t=4, e=2, j=4)[:, lo // 8 : hi // 8],
                 in_=x_raw[q, s][:].rearrange("p j (u e t) -> p u j e t", e=2, t=4)[:, lo // 8 : hi // 8],
+            )
+
+        def x_lay_by_line(q, s, lo, hi):
+            scalar_copy(
+                out=x_laid[q, s][:].rearrange("p (t u e j) -> p t u j e", t=4, e=2, j=4)[:, :, lo // 8 : hi // 8],
+                in_=x_raw[q, s][:].rearrange("p j (u e t) -> p t u j e", e=2, t=4)[:, :, lo // 8 : hi // 8],
             )
 
         def x_lay_in_order(q, s, lo, hi):
@@ -306,40 +312,39 @@ def tile_lowrankplussoftthresholdedcrosscovarianc_d2p_kernel(
         load_l()
         load_by_slot(g_sb, g, nc.sync)
         load_by_slot(tau_sb, tau, nc.sync)
+        load_m()
         load_x(0, 1)
         load_x(1, 1)
-        load_m()
+        load_y(2)
         load_w()
         make_identity(nc, ident[:])
 
         RING, LOW = (4, 5, 6, 7), (3, 0, 1, 2)
-        y_lay(0, range(8))
+        y_lay(0, range(7))
         x_pair(0, 0, 128, 384, 0)
         x_pair(0, 0, 384, 512, 1)
-        x_lay(0, 0, 0, 128, scalar_copy)
+        x_lay_by_line(0, 0, 0, 128)
         x_fetch(0, 0, 128, 384, scalar_copy)
         x_fetch(0, 0, 384, 512, scalar_copy)
         y_quant(0, 0, 512)
-        y_lay(1, (0, 1))
+        y_lay(1, range(4))
         x_quant(0, 0)
-        y_lay(1, (2, 3))
         x_pair(1, 0, 256, 512, 2)
+        turn_l(LOW[0])
         for t in SLOTS:
             cross_pass(0, 0, t, 0, RING[t])
-        turn_l(LOW[0])
-        x_lay(1, 0, 0, 256, scalar_copy)
+        x_lay_by_line(1, 0, 0, 256)
         x_fetch(1, 0, 256, 512, scalar_copy)
         factors_of_g()
-        y_lay(1, (4,))
         y_quant(1, 0, 512)
+        y_lay(0, (7,))
         x_quant(1, 0)
         widths()
-        x_pair(0, 1, 384, 512, 1)
-        x_lay(0, 1, 0, 256, scalar_copy)
         fetch_l()
-        x_fetch(0, 1, 384, 512, scalar_copy)
-        x_lay(0, 1, 256, 384, vector_copy)
-        y_lay(1, (5,))
+        x_lay_by_line(0, 1, 320, 512)
+        spans()
+        x_lay(0, 1, 0, 320, vector_copy)
+        y_quant(0, 512, J)
         LOW = (0, 1, 2, 3)
         cross_pass(0, 0, 0, 1)
         for t in (1, 2, 3):
@@ -348,10 +353,8 @@ def tile_lowrankplussoftthresholdedcrosscovarianc_d2p_kernel(
         lift(0, 0, 0)
         x_pair(1, 1, 320, 512, RING[0])
         low_rank(0, (3,), 0, 512, LOW[3])
-        spans()
         for t in (1, 2, 3):
             lift(0, 0, t)
-        y_quant(0, 512, J)
         x_quant(0, 1)
         x_lay_in_order(1, 1, 0, 320)
         for t in SLOTS:
@@ -362,7 +365,7 @@ def tile_lowrankplussoftthresholdedcrosscovarianc_d2p_kernel(
             cross_pass(0, 1, t, 0, RING[t])
         cross_pass(0, 1, 0, 0, RING[0])
         x_quant(1, 1)
-        y_lay(1, (6, 7))
+        y_lay(1, range(4, 8))
         for t in SLOTS:
             cross_pass(0, 1, t, 1)
             low_rank(1, (t,), 0, 512, LOW[t])
@@ -373,7 +376,7 @@ def tile_lowrankplussoftthresholdedcrosscovarianc_d2p_kernel(
         sig_lay(0, 0, 384, gpsimd_copy)
         for t in SLOTS:
             cap(1, t, 0, 512)
-        lower(1, (0, 1, 2), 0, 512, scalar_shift)
+        lower(1, SLOTS, 0, 512, scalar_shift)
         for t in SLOTS:
             cross(1, 0, t, RING[t])
             lift(1, 0, t)
@@ -382,8 +385,7 @@ def tile_lowrankplussoftthresholdedcrosscovarianc_d2p_kernel(
             cross(1, 1, t, RING[t])
             lift(1, 1, t)
         sig_lay(0, 384, 512, vector_copy)
-        floor_by_slot(1, 3, 0, 512)
-        floor(1, (0, 1, 2), 0, 512)
+        floor(1, SLOTS, 0, 512)
         sig_quant(0, 0, 512)
         sig_lay(1, 0, 512, gpsimd_copy)
         lower(0, (0,), 512, 768, gpsimd_shift)

@@ -52,7 +52,9 @@ def tile_lowrankplussoftthresholdedcrosscovarianc_d2p_kernel(
         m_sb = keep.tile([K, J], BF16, name="m_sb")
         l_t = keep.tile([K, 8, 128], BF16, name="l_t")
         ident = keep.tile([128, 128], BF16, name="ident")
-        y_fac = tiles("y_fac", [128, 8], F32, range(2))
+        y_row = keep.tile([128, 16], F32, name="y_row")
+        y_fac = keep.tile([128, 16], F32, name="y_fac")
+        quarter_ones = keep.tile([128, 128], F32, name="quarter_ones")
         g_sb = keep.tile([128, 8], BF16, name="g_sb")
         tau_sb = keep.tile([128, 8], BF16, name="tau_sb")
         g_over_t = keep.tile([128, 8], F32, name="g_over_t")
@@ -90,8 +92,18 @@ def tile_lowrankplussoftthresholdedcrosscovarianc_d2p_kernel(
                     in_=w_scales[:, 4 * i : 4 * i + 4, :].bitcast(I32).rearrange("s r n -> r s n"),
                 )
 
-        def load_y_scale(q):
-            nc.scalar.dma_start(out=y_fac[q][:], in_=y_scale[4 * q : 4 * q + 4, :].unsqueeze(1).to_broadcast([4, 32, 8]))
+        def load_y_scale():
+            nc.sync.dma_start(out=y_row[31:128:32].rearrange("p (q b) -> p q b", q=2), in_=y_scale.rearrange("(q i) b -> i q b", q=2))
+
+        def spread_y_scale(i):
+            nc.vector.memset(quarter_ones[:], 0.0)
+            for first in range(0, 128, 32):
+                nc.vector.memset(y_row[first : first + 31], 0.0)
+            for first in range(0, 128, 32):
+                nc.vector.memset(quarter_ones[first : first + 32, first : first + 32], 1.0)
+            ps = bank(i, "ps_scale", F32, 16)
+            nc.tensor.matmul(ps[:], quarter_ones[:], y_row[:], start=True, stop=True)
+            nc.scalar.copy(out=y_fac[:], in_=ps[:])
 
         vector_copy = nc.vector.tensor_copy
         scalar_copy = nc.scalar.copy
@@ -117,17 +129,26 @@ def tile_lowrankplussoftthresholdedcrosscovarianc_d2p_kernel(
         def quantise(code, scale, laid, lo, hi):
             nc.vector.quantize_mx(out=code[:, lo:hi].bitcast(FP8X4), scales=scale[:, lo:hi], in_=words(laid, lo, hi))
 
+        def y_block(q, b):
+            lo = BLOCK * b
+            first = max(a for of_pass, a, z in Y_LOADS if of_pass == q and a <= lo)
+            return y_raw[q, first][:, :, lo - first : lo - first + BLOCK].bitcast(FP8), words(y_laid[q], lo, lo + BLOCK)
+
+        def y_scale_into(out, in0, q, b):
+            nc.vector.tensor_scalar(out=out, in0=in0, scalar1=y_fac[:, 8 * q + b : 8 * q + b + 1], scalar2=None, op0=ALU.mult)
+
         def y_lay(q, blocks):
             for b in blocks:
-                lo = BLOCK * b
-                first = max(a for of_pass, a, z in Y_LOADS if of_pass == q and a <= lo)
-                nc.vector.tensor_scalar(
-                    out=words(y_laid[q], lo, lo + BLOCK).rearrange("p (c i j) -> p c j i", i=8, j=4),
-                    in0=y_raw[q, first][:, :, lo - first : lo - first + BLOCK].bitcast(FP8).rearrange("p j (c i) -> p c j i", i=8),
-                    scalar1=y_fac[q][:, b : b + 1],
-                    scalar2=None,
-                    op0=ALU.mult,
-                )
+                codes, laid_words = y_block(q, b)
+                y_scale_into(laid_words.rearrange("p (c i j) -> p c j i", i=8, j=4), codes.rearrange("p j (c i) -> p c j i", i=8), q, b)
+
+        def y_widen(q, b):
+            codes, laid_words = y_block(q, b)
+            scalar_copy(out=laid_words.rearrange("p (c j) -> p c j", j=4), in_=codes.rearrange("p j c -> p c j"))
+
+        def y_finish(q, b):
+            laid_words = y_block(q, b)[1]
+            y_scale_into(laid_words, laid_words, q, b)
 
         def y_quant(q, lo, hi):
             quantise(y_code[q], y_sc[q], y_laid[q], lo, hi)
@@ -303,8 +324,7 @@ def tile_lowrankplussoftthresholdedcrosscovarianc_d2p_kernel(
                 in_=staged[:].rearrange("p (b n) -> p b n", b=len(blocks)),
             )
 
-        load_y_scale(0)
-        load_y_scale(1)
+        load_y_scale()
         load_y(0)
         load_x(0, 0)
         load_y(1)
@@ -318,6 +338,7 @@ def tile_lowrankplussoftthresholdedcrosscovarianc_d2p_kernel(
         load_y(2)
         load_w()
         make_identity(nc, ident[:])
+        spread_y_scale(7)
 
         RING, LOW = (4, 5, 6, 7), (3, 0, 1, 2)
         y_lay(0, range(7))

@@ -49,7 +49,7 @@ def tile_lowrankplussoftthresholdedcrosscovarianc_d2p_kernel(
         floored = tiles("floored", [128, 4, J], BF16, range(2))
         sig_laid, sig_code, sig_sc = tiles("sig_laid", [128, 4 * J], BF16, range(2)), tiles("sig_code", [128, J], U32, range(2)), tiles("sig_sc", [128, J], U8, range(2))
         l_sb = keep.tile([128, 2, 4, K], BF16, name="l_sb")
-        m_sb = keep.tile([K, J], BF16, name="m_sb")
+        m_sb = tiles("m_sb", [K, BANK], BF16, range(2))
         l_t = keep.tile([K, 8, 128], BF16, name="l_t")
         ident = keep.tile([128, 128], BF16, name="ident")
         y_row = keep.tile([128, 16], F32, name="y_row")
@@ -80,8 +80,8 @@ def tile_lowrankplussoftthresholdedcrosscovarianc_d2p_kernel(
         def load_l():
             nc.sync.dma_start(out=l_sb[:], in_=l.rearrange("(s p t) k -> p s t k", s=2, p=128, t=4))
 
-        def load_m():
-            nc.sync.dma_start(out=m_sb[:], in_=m)
+        def load_m(h):
+            nc.sync.dma_start(out=m_sb[h][:], in_=m[:, BANK * h : BANK * (h + 1)])
 
         def load_w():
             nc.sync.dma_start(out=w_code[:].bitcast(I32), in_=w_words.bitcast(I32).rearrange("s p n -> p s n"))
@@ -246,7 +246,7 @@ def tile_lowrankplussoftthresholdedcrosscovarianc_d2p_kernel(
             ps = bank(i, "ps_low")
             for n, t in enumerate(slots):
                 low_ps[s, t, lo] = ps[:, (hi - lo) * n : (hi - lo) * (n + 1)]
-                nc.tensor.matmul(low_ps[s, t, lo], l_t[:, 4 * s + t, :], m_sb[:, lo:hi], start=True, stop=True)
+                nc.tensor.matmul(low_ps[s, t, lo], l_t[:, 4 * s + t, :], m_sb[lo // BANK][:, lo % BANK : lo % BANK + hi - lo], start=True, stop=True)
 
         def cap(s, t, lo, hi):
             nc.vector.scalar_tensor_tensor(
@@ -332,23 +332,30 @@ def tile_lowrankplussoftthresholdedcrosscovarianc_d2p_kernel(
         load_l()
         load_by_slot(g_sb, g, nc.sync)
         load_by_slot(tau_sb, tau, nc.sync)
-        load_m()
         load_x(0, 1)
-        load_x(1, 1)
         load_y(2)
+        load_m(0)
+        load_x(1, 1)
+        load_m(1)
         load_w()
         make_identity(nc, ident[:])
         spread_y_scale(7)
 
         RING, LOW = (4, 5, 6, 7), (3, 0, 1, 2)
-        y_lay(0, range(7))
+        y_lay(0, range(5))
+        y_widen(0, 5)
+        y_widen(0, 6)
+        y_finish(0, 5)
         x_pair(0, 0, 128, 384, 0)
         x_pair(0, 0, 384, 512, 1)
         x_lay_by_line(0, 0, 0, 128)
+        y_widen(0, 7)
         x_fetch(0, 0, 128, 384, scalar_copy)
         x_fetch(0, 0, 384, 512, scalar_copy)
         y_quant(0, 0, 512)
+        y_finish(0, 6)
         y_lay(1, range(4))
+        y_finish(0, 7)
         x_quant(0, 0)
         x_pair(1, 0, 256, 512, 2)
         turn_l(LOW[0])
@@ -358,14 +365,14 @@ def tile_lowrankplussoftthresholdedcrosscovarianc_d2p_kernel(
         x_fetch(1, 0, 256, 512, scalar_copy)
         factors_of_g()
         y_quant(1, 0, 512)
-        y_lay(0, (7,))
+        y_quant(0, 512, J)
         x_quant(1, 0)
         widths()
         fetch_l()
-        x_lay_by_line(0, 1, 320, 512)
+        x_lay_by_line(0, 1, 256, 512)
         spans()
-        x_lay(0, 1, 0, 320, vector_copy)
-        y_quant(0, 512, J)
+        x_lay(0, 1, 0, 256, vector_copy)
+        y_lay(1, (4, 5))
         LOW = (0, 1, 2, 3)
         cross_pass(0, 0, 0, 1)
         for t in (1, 2, 3):
@@ -386,7 +393,7 @@ def tile_lowrankplussoftthresholdedcrosscovarianc_d2p_kernel(
             cross_pass(0, 1, t, 0, RING[t])
         cross_pass(0, 1, 0, 0, RING[0])
         x_quant(1, 1)
-        y_lay(1, range(4, 8))
+        y_lay(1, (6, 7))
         for t in SLOTS:
             cross_pass(0, 1, t, 1)
             low_rank(1, (t,), 0, 512, LOW[t])
@@ -397,7 +404,7 @@ def tile_lowrankplussoftthresholdedcrosscovarianc_d2p_kernel(
         sig_lay(0, 0, 384, gpsimd_copy)
         for t in SLOTS:
             cap(1, t, 0, 512)
-        lower(1, SLOTS, 0, 512, scalar_shift)
+        lower(1, (0, 1, 2), 0, 512, scalar_shift)
         for t in SLOTS:
             cross(1, 0, t, RING[t])
             lift(1, 0, t)
@@ -406,7 +413,8 @@ def tile_lowrankplussoftthresholdedcrosscovarianc_d2p_kernel(
             cross(1, 1, t, RING[t])
             lift(1, 1, t)
         sig_lay(0, 384, 512, vector_copy)
-        floor(1, SLOTS, 0, 512)
+        floor_by_slot(1, 3, 0, 512)
+        floor(1, (0, 1, 2), 0, 512)
         sig_quant(0, 0, 512)
         sig_lay(1, 0, 512, gpsimd_copy)
         lower(0, (0,), 512, 768, gpsimd_shift)

@@ -369,10 +369,10 @@ def tile_lowrankplussoftthresholdedcrosscovarianc_d2p_kernel(
         x_quant(1, 0)
         widths()
         fetch_l()
-        x_lay_by_line(0, 1, 256, 512)
+        x_lay_by_line(0, 1, 288, 512)
         spans()
-        x_lay(0, 1, 0, 256, vector_copy)
-        y_lay(1, (4, 5))
+        x_lay(0, 1, 0, 288, vector_copy)
+        y_lay(1, (4,))
         LOW = (0, 1, 2, 3)
         cross_pass(0, 0, 0, 1)
         for t in (1, 2, 3):
@@ -384,6 +384,7 @@ def tile_lowrankplussoftthresholdedcrosscovarianc_d2p_kernel(
         for t in (1, 2, 3):
             lift(0, 0, t)
         x_quant(0, 1)
+        y_lay(1, (5,))
         x_lay_in_order(1, 1, 0, 320)
         for t in SLOTS:
             cap(0, t, 0, 512)
@@ -446,16 +447,16 @@ def tile_lowrankplussoftthresholdedcrosscovarianc_d2p_kernel(
         lower(0, SLOTS, 768, J, scalar_shift)
         store(0, 512, (0,), scalar_copy)
         store(0, 512, (1,), vector_copy)
+        lower(1, (0,), 768, J, scalar_shift)
         sig_fetch(0, 512, 768)
-        lower(1, SLOTS, 768, J, scalar_shift)
+        lower(1, (1, 2, 3), 768, J, scalar_shift)
         for b in (2, 3):
             store(0, 512, (b,), scalar_copy)
-        sig_quant(0, 512, 768)
-        exposure(512, 768, 0, (0, 1), LOW[0])
-        exposure(512, 768, 0, (2, 3), LOW[1])
         sig_quant(1, 512, 768)
-        exposure(512, 768, 1, (0, 1))
-        exposure(512, 768, 1, (2, 3))
+        sig_quant(0, 512, 768)
+        for blocks, i in (((0, 1), LOW[0]), ((2, 3), LOW[1])):
+            exposure(512, 768, 1, blocks, i)
+            exposure(512, 768, 0, blocks)
         floor_and_lay(0, 768, 896)
         floor_and_lay(1, 768, 896)
         sig_quant(0, 768, 896)

@@ -54,7 +54,7 @@ def tile_lowrankplussoftthresholdedcrosscovarianc_d2p_kernel(
         ident = keep.tile([128, 128], BF16, name="ident")
         y_row = keep.tile([128, 16], F32, name="y_row")
         y_fac = keep.tile([128, 16], F32, name="y_fac")
-        quarter_ones = keep.tile([128, 128], F32, name="quarter_ones")
+        spreader = keep.tile([128, 128], F32, name="spreader")
         g_sb = keep.tile([128, 8], BF16, name="g_sb")
         tau_sb = keep.tile([128, 8], BF16, name="tau_sb")
         g_over_t = keep.tile([128, 8], F32, name="g_over_t")
@@ -85,7 +85,7 @@ def tile_lowrankplussoftthresholdedcrosscovarianc_d2p_kernel(
 
         def load_w():
             nc.sync.dma_start(out=w_code[:].bitcast(I32), in_=w_words.bitcast(I32).rearrange("s p n -> p s n"))
-            nc.gpsimd.memset(w_sc[:].bitcast(I32), 0)
+            nc.vector.memset(w_sc[:].bitcast(I32), 0)
             for i in range(4):
                 nc.sync.dma_start(
                     out=w_sc[32 * i : 32 * i + 4].bitcast(I32),
@@ -93,17 +93,25 @@ def tile_lowrankplussoftthresholdedcrosscovarianc_d2p_kernel(
                 )
 
         def load_y_scale():
-            nc.sync.dma_start(out=y_row[31:128:32].rearrange("p (q b) -> p q b", q=2), in_=y_scale.rearrange("(q i) b -> i q b", q=2))
+            nc.sync.dma_start(out=y_row[124:128].rearrange("p (q b) -> p q b", q=2), in_=y_scale.rearrange("(q i) b -> i q b", q=2))
+            nc.vector.memset(y_row[0:124], 0.0)
+
+        def make_spreader():
+            nc.gpsimd.memset(spreader[:], 0.0)
+            nc.gpsimd.affine_select(
+                out=spreader[:], in_=spreader[:], pattern=[[-1, 4], [0, 32]], compare_op=ALU.not_equal, fill=1.0, base=-124, channel_multiplier=1
+            )
 
         def spread_y_scale(i):
-            nc.vector.memset(quarter_ones[:], 0.0)
-            for first in range(0, 128, 32):
-                nc.vector.memset(y_row[first : first + 31], 0.0)
-            for first in range(0, 128, 32):
-                nc.vector.memset(quarter_ones[first : first + 32, first : first + 32], 1.0)
             ps = bank(i, "ps_scale", F32, 16)
-            nc.tensor.matmul(ps[:], quarter_ones[:], y_row[:], start=True, stop=True)
+            nc.tensor.matmul(ps[:], spreader[:], y_row[:], start=True, stop=True)
             nc.scalar.copy(out=y_fac[:], in_=ps[:])
+
+        def warm_up(i):
+            ps = bank(i, "ps_warm", F32, 384)
+            nc.tensor.matmul(
+                ps[:].rearrange("p (r n) -> p r n", r=3), spreader[:], spreader[:].unsqueeze(1).to_broadcast([128, 3, 128]), start=True, stop=True
+            )
 
         vector_copy = nc.vector.tensor_copy
         scalar_copy = nc.scalar.copy
@@ -338,8 +346,10 @@ def tile_lowrankplussoftthresholdedcrosscovarianc_d2p_kernel(
         load_x(1, 1)
         load_m(1)
         load_w()
+        make_spreader()
         make_identity(nc, ident[:])
         spread_y_scale(7)
+        warm_up(6)
 
         RING, LOW = (4, 5, 6, 7), (3, 0, 1, 2)
         y_lay(0, range(5))

@@ -71,8 +71,8 @@ def tile_lowrankplussoftthresholdedcrosscovarianc_d2p_kernel(
             q, lo, hi = Y_LOADS[i]
             nc.sync.dma_start(out=y_raw[q, lo][:], in_=y_v[q][:, :, lo:hi])
 
-        def load_x(q, s):
-            nc.sync.dma_start(out=x_raw[q, s][:], in_=x_v[q][:, :, BANK * s : BANK * (s + 1)])
+        def load_x(q, s, rows=slice(0, 4)):
+            nc.sync.dma_start(out=x_raw[q, s][:, rows], in_=x_v[q][:, rows, BANK * s : BANK * (s + 1)])
 
         def load_by_slot(tile, vector, queue):
             queue.dma_start(out=tile[:].rearrange("p (s t) -> p s t", s=2), in_=vector.rearrange("(s p t) -> p s t", s=2, p=128, t=4))
@@ -181,17 +181,21 @@ def tile_lowrankplussoftthresholdedcrosscovarianc_d2p_kernel(
 
         pair_ps = {}
 
-        def x_pair(q, s, lo, hi, i):
+        def x_pair_rows(q, s, lo, hi, u, i=None):
             n = hi - lo
-            pair_ps[q, s, lo] = bank(i, "ps_pair", BF16, 4 * n)
-            for u in range(2):
-                nc.tensor.matmul(
-                    pair_ps[q, s, lo][:, 2 * n * u : 2 * n * (u + 1)].rearrange("p (c e) -> p e c", e=2),
-                    ident[:],
-                    x_raw[q, s][:, 2 * u : 2 * u + 2, lo:hi],
-                    start=True,
-                    stop=True,
-                )
+            if u == 0:
+                pair_ps[q, s, lo] = bank(i, "ps_pair", BF16, 4 * n)
+            nc.tensor.matmul(
+                pair_ps[q, s, lo][:, 2 * n * u : 2 * n * (u + 1)].rearrange("p (c e) -> p e c", e=2),
+                ident[:],
+                x_raw[q, s][:, 2 * u : 2 * u + 2, lo:hi],
+                start=True,
+                stop=True,
+            )
+
+        def x_pair(q, s, lo, hi, i):
+            x_pair_rows(q, s, lo, hi, 0, i)
+            x_pair_rows(q, s, lo, hi, 1)
 
         def x_fetch(q, s, lo, hi, copy):
             copy(
@@ -336,7 +340,8 @@ def tile_lowrankplussoftthresholdedcrosscovarianc_d2p_kernel(
         load_y(0)
         load_x(0, 0)
         load_y(1)
-        load_x(1, 0)
+        load_x(1, 0, slice(0, 2))
+        load_x(1, 0, slice(2, 4))
         load_l()
         load_by_slot(g_sb, g, nc.sync)
         load_by_slot(tau_sb, tau, nc.sync)
@@ -379,9 +384,9 @@ def tile_lowrankplussoftthresholdedcrosscovarianc_d2p_kernel(
         x_quant(1, 0)
         widths()
         fetch_l()
-        x_lay_by_line(0, 1, 288, 512)
+        x_lay_by_line(0, 1, 256, 512)
         spans()
-        x_lay(0, 1, 0, 288, vector_copy)
+        x_lay(0, 1, 0, 256, vector_copy)
         y_lay(1, (4,))
         LOW = (0, 1, 2, 3)
         cross_pass(0, 0, 0, 1)
@@ -389,17 +394,18 @@ def tile_lowrankplussoftthresholdedcrosscovarianc_d2p_kernel(
             cross_pass(0, 0, t, 1)
             low_rank(0, (t - 1,), 0, 512, LOW[t - 1])
         lift(0, 0, 0)
-        x_pair(1, 1, 320, 512, RING[0])
+        x_pair(1, 1, 352, 512, RING[0])
         low_rank(0, (3,), 0, 512, LOW[3])
         for t in (1, 2, 3):
             lift(0, 0, t)
         x_quant(0, 1)
         y_lay(1, (5,))
-        x_lay_in_order(1, 1, 0, 320)
+        x_lay_in_order(1, 1, 0, 352)
         for t in SLOTS:
             cap(0, t, 0, 512)
-        x_fetch(1, 1, 320, 512, scalar_copy)
+        x_fetch(1, 1, 352, 512, scalar_copy)
         lower(0, (0, 1, 2), 0, 512, scalar_shift)
+        lower(0, (3,), 0, 256, scalar_shift)
         for t in (1, 2, 3):
             cross_pass(0, 1, t, 0, RING[t])
         cross_pass(0, 1, 0, 0, RING[0])
@@ -409,8 +415,9 @@ def tile_lowrankplussoftthresholdedcrosscovarianc_d2p_kernel(
             cross_pass(0, 1, t, 1)
             low_rank(1, (t,), 0, 512, LOW[t])
             lift(0, 1, t)
-        floor_by_slot(0, 3, 0, 512)
-        floor(0, (0, 1, 2), 0, 512)
+        floor_by_slot(0, 3, 256, 512)
+        floor(0, (0, 1, 2), 256, 512)
+        floor(0, SLOTS, 0, 256)
         y_quant(1, 512, J)
         sig_lay(0, 0, 384, gpsimd_copy)
         for t in SLOTS:

@@ -21,6 +21,7 @@ BANK = 512
 BLOCK = 128
 SLOTS = range(4)
 ROW_BLOCKS = range(4)
+CHUNKS = ((0, 512), (512, 768), (768, 896), (896, J))
 Y_LOADS = ((0, 0, J), (1, 0, BANK), (1, BANK, J))
 
 
@@ -41,13 +42,17 @@ def tile_lowrankplussoftthresholdedcrosscovarianc_d2p_kernel(
         x_raw = tiles("x_raw", [128, 4, BANK], BF16, pairs)
         y_raw = {(q, lo): keep.tile([128, 4, hi - lo], U8, name=f"y_raw_{q}_{lo}", align_bytes=64) for q, lo, hi in Y_LOADS}
         x_laid, x_code, x_sc = tiles("x_laid", [128, 4 * BANK], BF16, pairs[:3]), tiles("x_code", [128, BANK], U32, pairs), tiles("x_sc", [128, BANK], U8, pairs)
-        y_laid, y_code, y_sc = tiles("y_laid", [128, 4 * J], BF16, range(2)), tiles("y_code", [128, J], U32, range(2)), tiles("y_sc", [128, J], U8, range(2))
+        y_laid = keep.tile([128, 8 * J], BF16, name="y_laid", align_bytes=64)
+        y_code = keep.tile([128, 2 * J], U32, name="y_code", align_bytes=64)
+        y_sc = keep.tile([128, 2 * J], U8, name="y_sc", align_bytes=64)
         x_laid[1, 1] = x_laid[0, 1]
         upper = {(s, t): keep.tile([128, J], F32, name=f"upper_{s}{t}") for s in range(2) for t in SLOTS}
         capped = tiles("capped", [128, 4, J], BF16, range(2))
         lowered = tiles("lowered", [128, 4, J], BF16, range(2))
         floored = tiles("floored", [128, 4, J], BF16, range(2))
-        sig_laid, sig_code, sig_sc = tiles("sig_laid", [128, 4 * J], BF16, range(2)), tiles("sig_code", [128, J], U32, range(2)), tiles("sig_sc", [128, J], U8, range(2))
+        sig_laid = keep.tile([128, 8 * J], BF16, name="sig_laid", align_bytes=64)
+        sig_code = keep.tile([128, 2 * J], U32, name="sig_code", align_bytes=64)
+        sig_sc = keep.tile([128, 2 * J], U8, name="sig_sc", align_bytes=64)
         l_sb = keep.tile([128, 2, 4, K], BF16, name="l_sb")
         m_sb = tiles("m_sb", [K, BANK], BF16, range(2))
         l_t = keep.tile([K, 8, 128], BF16, name="l_t")
@@ -134,13 +139,23 @@ def tile_lowrankplussoftthresholdedcrosscovarianc_d2p_kernel(
         def words(laid, lo, hi):
             return laid[:, 4 * lo : 4 * hi]
 
+        def y_word(q, column):
+            return 2 * BANK * (column // BANK) + BANK * q + column % BANK
+
+        def sig_word(s, column):
+            first, end = [chunk for chunk in CHUNKS if chunk[0] <= column][-1]
+            return 2 * first + s * (end - first) + column - first
+
+        def sig_words(s, lo, hi):
+            return words(sig_laid, sig_word(s, lo), sig_word(s, lo) + hi - lo)
+
         def quantise(code, scale, laid, lo, hi):
             nc.vector.quantize_mx(out=code[:, lo:hi].bitcast(FP8X4), scales=scale[:, lo:hi], in_=words(laid, lo, hi))
 
         def y_block(q, b):
             lo = BLOCK * b
             first = max(a for of_pass, a, z in Y_LOADS if of_pass == q and a <= lo)
-            return y_raw[q, first][:, :, lo - first : lo - first + BLOCK].bitcast(FP8), words(y_laid[q], lo, lo + BLOCK)
+            return y_raw[q, first][:, :, lo - first : lo - first + BLOCK].bitcast(FP8), words(y_laid, y_word(q, lo), y_word(q, lo) + BLOCK)
 
         def y_scale_into(out, in0, q, b):
             nc.vector.tensor_scalar(out=out, in0=in0, scalar1=y_fac[:, 8 * q + b : 8 * q + b + 1], scalar2=None, op0=ALU.mult)
@@ -158,8 +173,8 @@ def tile_lowrankplussoftthresholdedcrosscovarianc_d2p_kernel(
             laid_words = y_block(q, b)[1]
             y_scale_into(laid_words, laid_words, q, b)
 
-        def y_quant(q, lo, hi):
-            quantise(y_code[q], y_sc[q], y_laid[q], lo, hi)
+        def y_quant(q, h, halves=1):
+            quantise(y_code, y_sc, y_laid, y_word(q, BANK * h), y_word(q, BANK * h) + BANK * halves)
 
         def x_lay(q, s, lo, hi, copy):
             copy(
@@ -229,29 +244,27 @@ def tile_lowrankplussoftthresholdedcrosscovarianc_d2p_kernel(
 
         cross_ps, low_ps, out_ps = {}, {}, {}
 
-        def half(h):
-            return slice(BANK * h, BANK * (h + 1))
-
-        def cross_pass(h, s, t, q, i=None):
-            if q == 0:
-                cross_ps[h, s, t] = bank(i, "ps_cross")
+        def cross_pass(s, t, lo, hi, q, i=None):
+            if i is not None:
+                cross_ps[s, t, lo] = bank(i, "ps_cross")[:, : hi - lo]
+            part = slice(y_word(q, lo), y_word(q, lo) + hi - lo)
             nc.tensor.matmul_mx(
-                out=cross_ps[h, s, t][:],
+                out=cross_ps[s, t, lo],
                 lhsT=x_code[q, s][:, 128 * t : 128 * t + 128].bitcast(FP8X4),
                 lhsT_scale=x_sc[q, s][:, 128 * t : 128 * t + 128],
-                rhs=y_code[q][:, half(h)].bitcast(FP8X4),
-                rhs_scale=y_sc[q][:, half(h)],
-                start=(q == 0),
-                stop=(q == 1),
+                rhs=y_code[:, part].bitcast(FP8X4),
+                rhs_scale=y_sc[:, part],
+                start=(i is not None),
+                stop=(i is None),
             )
 
-        def cross(h, s, t, i):
-            cross_pass(h, s, t, 0, i)
-            cross_pass(h, s, t, 1)
+        def cross(s, t, lo, hi, i):
+            cross_pass(s, t, lo, hi, 0, i)
+            cross_pass(s, t, lo, hi, 1)
 
-        def lift(h, s, t):
+        def lift(s, t, lo, hi):
             nc.scalar.activation(
-                out=upper[s, t][:, half(h)], in_=cross_ps[h, s, t][:], func=ACT.Identity, scale=of_slot(g_over_t, s, t), bias=of_slot(width, s, t)
+                out=upper[s, t][:, lo:hi], in_=cross_ps[s, t, lo], func=ACT.Identity, scale=of_slot(g_over_t, s, t), bias=of_slot(width, s, t)
             )
 
         def low_rank(s, slots, lo, hi, i):
@@ -279,7 +292,7 @@ def tile_lowrankplussoftthresholdedcrosscovarianc_d2p_kernel(
             )
 
         def laid(s, lo, hi, run):
-            return words(sig_laid[s], lo, hi).rearrange("p (c i t) -> p c t i", i=run, t=4)
+            return sig_words(s, lo, hi).rearrange("p (c i t) -> p c t i", i=run, t=4)
 
         def by_slot(tile, lo, hi, run):
             return tile[:, :, lo:hi].rearrange("p t (c i) -> p c t i", i=run)
@@ -303,14 +316,14 @@ def tile_lowrankplussoftthresholdedcrosscovarianc_d2p_kernel(
                     stop=True,
                 )
 
-        def sig_fetch(s, lo, hi):
-            scalar_copy(
-                out=words(sig_laid[s], lo, hi).bitcast(F32).rearrange("p (c u) -> p c u", u=2),
+        def sig_fetch(s, lo, hi, copy=scalar_copy):
+            copy(
+                out=sig_words(s, lo, hi).bitcast(F32).rearrange("p (c u) -> p c u", u=2),
                 in_=pair_ps[s, lo][:].bitcast(F32).rearrange("p (u c) -> p c u", u=2),
             )
 
-        def sig_quant(s, lo, hi):
-            quantise(sig_code[s], sig_sc[s], sig_laid[s], lo, hi)
+        def sig_quant(s, lo, hi, groups=1):
+            quantise(sig_code, sig_sc, sig_laid, sig_word(s, lo), sig_word(s, lo) + groups * (hi - lo))
 
         def exposure(lo, hi, s, blocks, i=None):
             n = hi - lo
@@ -321,8 +334,8 @@ def tile_lowrankplussoftthresholdedcrosscovarianc_d2p_kernel(
                     out=out_ps[lo, blocks[0]][:, n * k : n * (k + 1)],
                     lhsT=w_code[:, s, 256 * b : 256 * b + 256].bitcast(FP4X4),
                     lhsT_scale=w_sc[:, s, 128 * b : 128 * b + 128],
-                    rhs=sig_code[s][:, lo:hi].bitcast(FP8X4),
-                    rhs_scale=sig_sc[s][:, lo:hi],
+                    rhs=sig_code[:, sig_word(s, lo) : sig_word(s, lo) + n].bitcast(FP8X4),
+                    rhs_scale=sig_sc[:, sig_word(s, lo) : sig_word(s, lo) + n],
                     start=(i is not None and k == 0),
                     stop=(i is None and k == len(blocks) - 1),
                 )
@@ -367,7 +380,7 @@ def tile_lowrankplussoftthresholdedcrosscovarianc_d2p_kernel(
         y_widen(0, 7)
         x_fetch(0, 0, 128, 384, scalar_copy)
         x_fetch(0, 0, 384, 512, scalar_copy)
-        y_quant(0, 0, 512)
+        y_quant(0, 0)
         y_finish(0, 6)
         y_lay(1, range(4))
         y_finish(0, 7)
@@ -375,12 +388,11 @@ def tile_lowrankplussoftthresholdedcrosscovarianc_d2p_kernel(
         x_pair(1, 0, 256, 512, 2)
         turn_l(LOW[0])
         for t in SLOTS:
-            cross_pass(0, 0, t, 0, RING[t])
+            cross_pass(0, t, 0, 512, 0, RING[t])
         x_lay_by_line(1, 0, 0, 256)
         x_fetch(1, 0, 256, 512, scalar_copy)
         factors_of_g()
-        y_quant(1, 0, 512)
-        y_quant(0, 512, J)
+        y_quant(1, 0, halves=2)
         x_quant(1, 0)
         widths()
         fetch_l()
@@ -389,15 +401,15 @@ def tile_lowrankplussoftthresholdedcrosscovarianc_d2p_kernel(
         x_lay(0, 1, 0, 256, vector_copy)
         y_lay(1, (4,))
         LOW = (0, 1, 2, 3)
-        cross_pass(0, 0, 0, 1)
+        cross_pass(0, 0, 0, 512, 1)
         for t in (1, 2, 3):
-            cross_pass(0, 0, t, 1)
+            cross_pass(0, t, 0, 512, 1)
             low_rank(0, (t - 1,), 0, 512, LOW[t - 1])
-        lift(0, 0, 0)
+        lift(0, 0, 0, 512)
         x_pair(1, 1, 352, 512, RING[0])
         low_rank(0, (3,), 0, 512, LOW[3])
         for t in (1, 2, 3):
-            lift(0, 0, t)
+            lift(0, t, 0, 512)
         x_quant(0, 1)
         y_lay(1, (5,))
         x_lay_in_order(1, 1, 0, 352)
@@ -407,29 +419,29 @@ def tile_lowrankplussoftthresholdedcrosscovarianc_d2p_kernel(
         lower(0, (0, 1, 2), 0, 512, scalar_shift)
         lower(0, (3,), 0, 256, scalar_shift)
         for t in (1, 2, 3):
-            cross_pass(0, 1, t, 0, RING[t])
-        cross_pass(0, 1, 0, 0, RING[0])
+            cross_pass(1, t, 0, 512, 0, RING[t])
+        cross_pass(1, 0, 0, 512, 0, RING[0])
         x_quant(1, 1)
         y_lay(1, (6, 7))
         for t in SLOTS:
-            cross_pass(0, 1, t, 1)
+            cross_pass(1, t, 0, 512, 1)
             low_rank(1, (t,), 0, 512, LOW[t])
-            lift(0, 1, t)
+            lift(1, t, 0, 512)
         floor_by_slot(0, 3, 256, 512)
         floor(0, (0, 1, 2), 256, 512)
         floor(0, SLOTS, 0, 256)
-        y_quant(1, 512, J)
+        y_quant(1, 1)
         sig_lay(0, 0, 384, gpsimd_copy)
         for t in SLOTS:
             cap(1, t, 0, 512)
         lower(1, (0, 1, 2), 0, 512, scalar_shift)
         for t in SLOTS:
-            cross(1, 0, t, RING[t])
-            lift(1, 0, t)
+            cross(0, t, 512, J, RING[t])
+            lift(0, t, 512, J)
             low_rank(0, (t,), 512, J, LOW[t])
         for t in SLOTS:
-            cross(1, 1, t, RING[t])
-            lift(1, 1, t)
+            cross(1, t, 512, J, RING[t])
+            lift(1, t, 512, J)
         sig_lay(0, 384, 512, vector_copy)
         floor_by_slot(1, 3, 0, 512)
         floor(1, (0, 1, 2), 0, 512)
@@ -469,21 +481,23 @@ def tile_lowrankplussoftthresholdedcrosscovarianc_d2p_kernel(
         lower(1, (1, 2, 3), 768, J, scalar_shift)
         for b in (2, 3):
             store(0, 512, (b,), scalar_copy)
-        sig_quant(1, 512, 768)
-        sig_quant(0, 512, 768)
+        floor(0, SLOTS, 896, J)
+        sig_pair(0, 896, J, RING[2])
+        sig_quant(0, 512, 768, groups=2)
         for blocks, i in (((0, 1), LOW[0]), ((2, 3), LOW[1])):
             exposure(512, 768, 1, blocks, i)
             exposure(512, 768, 0, blocks)
         floor_and_lay(0, 768, 896)
         floor_and_lay(1, 768, 896)
         sig_quant(0, 768, 896)
-        exposure(768, 896, 0, ROW_BLOCKS, RING[3])
+        sig_fetch(0, 896, J)
         store(512, 768, (0, 1), scalar_copy)
         store(512, 768, (2, 3), scalar_copy)
         sig_quant(1, 768, 896)
-        exposure(768, 896, 1, ROW_BLOCKS)
-        floor_and_lay(0, 896, J)
-        store(768, 896, ROW_BLOCKS, scalar_copy)
+        for blocks, i in (((0, 1), RING[3]), ((2, 3), LOW[3])):
+            exposure(768, 896, 0, blocks, i)
+            exposure(768, 896, 1, blocks)
+            store(768, 896, blocks, scalar_copy)
         floor_and_lay(1, 896, J)
         sig_quant(0, 896, J)
         LAST = (RING[0], RING[1], RING[2], LOW[2])

@@ -396,9 +396,11 @@ def tile_lowrankplussoftthresholdedcrosscovarianc_d2p_kernel(
         x_quant(1, 0)
         widths()
         fetch_l()
-        x_lay_by_line(0, 1, 256, 512)
-        spans()
         x_lay(0, 1, 0, 256, vector_copy)
+        x_lay_by_line(0, 1, 256, 384)
+        x_pair(0, 1, 384, 512, 2)
+        x_fetch(0, 1, 384, 512, scalar_copy)
+        spans()
         y_lay(1, (4,))
         LOW = (0, 1, 2, 3)
         cross_pass(0, 0, 0, 512, 1)

from contextlib import ExitStack

import concourse.mybir as mybir
from concourse.masks import make_identity

F32 = mybir.dt.float32
BF16 = mybir.dt.bfloat16
U8 = mybir.dt.uint8
U32 = mybir.dt.uint32
I32 = mybir.dt.int32
FP8 = mybir.dt.float8_e4m3fn
FP8X4 = mybir.dt.float8_e4m3fn_x4
FP4X4 = mybir.dt.float4_e2m1fn_x4
ALU = mybir.AluOpType
ACT = mybir.ActivationFunctionType

T, N, J, K, P = 1024, 1024, 1024, 128, 512
FLOPS = 2 * T * N * J + 2 * N * K * J + 2 * P * N * J

BANK = 512
BLOCK = 128
SLOTS = range(4)
ROW_BLOCKS = range(4)
CHUNKS = ((0, 512), (512, 768), (768, 896), (896, J))
Y_LOADS = ((0, 0, J), (1, 0, BANK), (1, BANK, J))


def tile_lowrankplussoftthresholdedcrosscovarianc_d2p_kernel(
    tc, x, y_bytes, y_scale, l, m, tau, g, w_words, w_scales, out
):
    nc = tc.nc
    with ExitStack() as ctx:
        keep = ctx.enter_context(tc.tile_pool(name="keep", bufs=1))
        psum = ctx.enter_context(tc.psum_pool(name="psum", bufs=1))
        ctx.enter_context(tc.manual_schedule())

        pairs = [(a, b) for a in range(2) for b in range(2)]

        def tiles(name, shape, dtype, keys):
            return {key: keep.tile(shape, dtype, name=f"{name}_{i}", align_bytes=64) for i, key in enumerate(keys)}

        x_raw = tiles("x_raw", [128, 4, BANK], BF16, pairs)
        y_raw = {(q, lo): keep.tile([128, 4, hi - lo], U8, name=f"y_raw_{q}_{lo}", align_bytes=64) for q, lo, hi in Y_LOADS}
        x_laid, x_code, x_sc = tiles("x_laid", [128, 4 * BANK], BF16, pairs[:3]), tiles("x_code", [128, BANK], U32, pairs), tiles("x_sc", [128, BANK], U8, pairs)
        y_laid = keep.tile([128, 8 * J], BF16, name="y_laid", align_bytes=64)
        y_code = keep.tile([128, 2 * J], U32, name="y_code", align_bytes=64)
        y_sc = keep.tile([128, 2 * J], U8, name="y_sc", align_bytes=64)
        x_laid[1, 1] = x_laid[0, 1]
        upper = {(s, t): keep.tile([128, J], F32, name=f"upper_{s}{t}") for s in range(2) for t in SLOTS}
        capped = tiles("capped", [128, 4, J], BF16, range(2))
        lowered = tiles("lowered", [128, 4, J], BF16, range(2))
        floored = tiles("floored", [128, 4, J], BF16, range(2))
        sig_laid = keep.tile([128, 8 * J], BF16, name="sig_laid", align_bytes=64)
        sig_code = keep.tile([128, 2 * J], U32, name="sig_code", align_bytes=64)
        sig_sc = keep.tile([128, 2 * J], U8, name="sig_sc", align_bytes=64)
        l_sb = keep.tile([128, 2, 4, K], BF16, name="l_sb")
        m_sb = tiles("m_sb", [K, BANK], BF16, range(2))
        l_t = keep.tile([K, 8, 128], BF16, name="l_t")
        ident = keep.tile([128, 128], BF16, name="ident")
        y_row = keep.tile([128, 16], F32, name="y_row")
        y_fac = keep.tile([128, 16], F32, name="y_fac")
        spreader = keep.tile([128, 128], F32, name="spreader")
        g_sb = keep.tile([128, 8], BF16, name="g_sb")
        tau_sb = keep.tile([128, 8], BF16, name="tau_sb")
        g_over_t = keep.tile([128, 8], F32, name="g_over_t")
        g_abs = keep.tile([128, 8], F32, name="g_abs")
        width = keep.tile([128, 8], F32, name="width")
        span_down = keep.tile([128, 8], F32, name="span_down")
        w_code = keep.tile([128, 2, 2 * P], U8, name="w_code", align_bytes=64)
        w_sc = keep.tile([128, 2, P], U8, name="w_sc", align_bytes=64)

        x_v = x.rearrange("(q p j) n -> q p j n", q=2, p=128, j=4)
        y_v = y_bytes.rearrange("(q p j) n -> q p j n", q=2, p=128, j=4)

        def load_y(i):
            q, lo, hi = Y_LOADS[i]
            nc.sync.dma_start(out=y_raw[q, lo][:], in_=y_v[q][:, :, lo:hi])

        def load_x(q, s, rows=slice(0, 4)):
            nc.sync.dma_start(out=x_raw[q, s][:, rows], in_=x_v[q][:, rows, BANK * s : BANK * (s + 1)])

        def load_by_slot(tile, vector, queue):
            queue.dma_start(out=tile[:].rearrange("p (s t) -> p s t", s=2), in_=vector.rearrange("(s p t) -> p s t", s=2, p=128, t=4))

        def load_l():
            nc.sync.dma_start(out=l_sb[:], in_=l.rearrange("(s p t) k -> p s t k", s=2, p=128, t=4))

        def load_m(h):
            nc.sync.dma_start(out=m_sb[h][:], in_=m[:, BANK * h : BANK * (h + 1)])

        def load_w():
            nc.sync.dma_start(out=w_code[:].bitcast(I32), in_=w_words.bitcast(I32).rearrange("s p n -> p s n"))
            nc.vector.memset(w_sc[:].bitcast(I32), 0)
            for i in range(4):
                nc.sync.dma_start(
                    out=w_sc[32 * i : 32 * i + 4].bitcast(I32),
                    in_=w_scales[:, 4 * i : 4 * i + 4, :].bitcast(I32).rearrange("s r n -> r s n"),
                )

        def load_y_scale():
            nc.sync.dma_start(out=y_row[124:128].rearrange("p (q b) -> p q b", q=2), in_=y_scale.rearrange("(q i) b -> i q b", q=2))
            nc.vector.memset(y_row[0:124], 0.0)

        def make_spreader():
            nc.gpsimd.memset(spreader[:], 0.0)
            nc.gpsimd.affine_select(
                out=spreader[:], in_=spreader[:], pattern=[[-1, 4], [0, 32]], compare_op=ALU.not_equal, fill=1.0, base=-124, channel_multiplier=1
            )

        def spread_y_scale(i):
            ps = bank(i, "ps_scale", F32, 16)
            nc.tensor.matmul(ps[:], spreader[:], y_row[:], start=True, stop=True)
            nc.scalar.copy(out=y_fac[:], in_=ps[:])

        def warm_up(i):
            ps = bank(i, "ps_warm", F32, 384)
            nc.tensor.matmul(
                ps[:].rearrange("p (r n) -> p r n", r=3), spreader[:], spreader[:].unsqueeze(1).to_broadcast([128, 3, 128]), start=True, stop=True
            )

        vector_copy = nc.vector.tensor_copy
        scalar_copy = nc.scalar.copy

        def gpsimd_copy(out, in_):
            nc.gpsimd.tensor_scalar(out=out, in0=in_, scalar1=1.0, scalar2=0.0, op0=ALU.mult, op1=ALU.add)

        def scalar_shift(out, in_, term):
            nc.scalar.activation(out=out, in_=in_, func=ACT.Identity, bias=term)

        def gpsimd_shift(out, in_, term):
            nc.gpsimd.tensor_scalar(out=out, in0=in_, scalar1=1.0, scalar2=term, op0=ALU.mult, op1=ALU.add)

        def of_slot(tile, s, t):
            return tile[:, 4 * s + t : 4 * s + t + 1]

        def bank(i, name, dtype=F32, columns=BANK):
            return psum.tile([128, columns], dtype, name=name, tag=f"bank_{i}")

        def words(laid, lo, hi):
            return laid[:, 4 * lo : 4 * hi]

        def y_word(q, column):
            return 2 * BANK * (column // BANK) + BANK * q + column % BANK

        def sig_word(s, column):
            first, end = [chunk for chunk in CHUNKS if chunk[0] <= column][-1]
            return 2 * first + s * (end - first) + column - first

        def sig_words(s, lo, hi):
            return words(sig_laid, sig_word(s, lo), sig_word(s, lo) + hi - lo)

        def quantise(code, scale, laid, lo, hi):
            nc.vector.quantize_mx(out=code[:, lo:hi].bitcast(FP8X4), scales=scale[:, lo:hi], in_=words(laid, lo, hi))

        def y_block(q, b):
            lo = BLOCK * b
            first = max(a for of_pass, a, z in Y_LOADS if of_pass == q and a <= lo)
            return y_raw[q, first][:, :, lo - first : lo - first + BLOCK].bitcast(FP8), words(y_laid, y_word(q, lo), y_word(q, lo) + BLOCK)

        def y_scale_into(out, in0, q, b):
            nc.vector.tensor_scalar(out=out, in0=in0, scalar1=y_fac[:, 8 * q + b : 8 * q + b + 1], scalar2=None, op0=ALU.mult)

        def y_lay(q, blocks):
            for b in blocks:
                codes, laid_words = y_block(q, b)
                y_scale_into(laid_words.rearrange("p (c i j) -> p c j i", i=8, j=4), codes.rearrange("p j (c i) -> p c j i", i=8), q, b)

        def y_widen(q, b):
            codes, laid_words = y_block(q, b)
            scalar_copy(out=laid_words.rearrange("p (c j) -> p c j", j=4), in_=codes.rearrange("p j c -> p c j"))

        def y_finish(q, b):
            laid_words = y_block(q, b)[1]
            y_scale_into(laid_words, laid_words, q, b)

        def y_quant(q, h, halves=1):
            quantise(y_code, y_sc, y_laid, y_word(q, BANK * h), y_word(q, BANK * h) + BANK * halves)

        def x_lay(q, s, lo, hi, copy):
            copy(
                out=x_laid[q, s][:].rearrange("p (t u e j) -> p u j e t", t=4, e=2, j=4)[:, lo // 8 : hi // 8],
                in_=x_raw[q, s][:].rearrange("p j (u e t) -> p u j e t", e=2, t=4)[:, lo // 8 : hi // 8],
            )

        def x_lay_by_line(q, s, lo, hi):
            scalar_copy(
                out=x_laid[q, s][:].rearrange("p (t u e j) -> p t u j e", t=4, e=2, j=4)[:, :, lo // 8 : hi // 8],
                in_=x_raw[q, s][:].rearrange("p j (u e t) -> p t u j e", e=2, t=4)[:, :, lo // 8 : hi // 8],
            )

        def x_lay_in_order(q, s, lo, hi):
            gpsimd_copy(
                out=x_laid[q, s][:].rearrange("p (t r j) -> p r t j", t=4, j=4)[:, lo // 4 : hi // 4],
                in_=x_raw[q, s][:].rearrange("p j (r t) -> p r t j", t=4)[:, lo // 4 : hi // 4],
            )

        pair_ps = {}

        def x_pair_rows(q, s, lo, hi, u, i=None):
            n = hi - lo
            if u == 0:
                pair_ps[q, s, lo] = bank(i, "ps_pair", BF16, 4 * n)
            nc.tensor.matmul(
                pair_ps[q, s, lo][:, 2 * n * u : 2 * n * (u + 1)].rearrange("p (c e) -> p e c", e=2),
                ident[:],
                x_raw[q, s][:, 2 * u : 2 * u + 2, lo:hi],
                start=True,
                stop=True,
            )

        def x_pair(q, s, lo, hi, i):
            x_pair_rows(q, s, lo, hi, 0, i)
            x_pair_rows(q, s, lo, hi, 1)

        def x_fetch(q, s, lo, hi, copy):
            copy(
                out=x_laid[q, s][:].bitcast(F32).rearrange("p (t r u) -> p t r u", t=4, u=2)[:, :, lo // 4 : hi // 4, :],
                in_=pair_ps[q, s, lo][:].bitcast(F32).rearrange("p (u r t) -> p t r u", u=2, t=4),
            )

        def x_quant(q, s):
            quantise(x_code[q, s], x_sc[q, s], x_laid[q, s], 0, BANK)

        turn_ps = {}

        def turn_l(i):
            turn_ps[0] = bank(i, "ps_l", BF16, 2 * BANK)
            for s in range(2):
                for t in SLOTS:
                    nc.tensor.transpose(turn_ps[0][:, 128 * (4 * s + t) : 128 * (4 * s + t + 1)], l_sb[:, s, t, :], ident[:])

        def fetch_l():
            scalar_copy(out=l_t[:].rearrange("p t n -> p (t n)"), in_=turn_ps[0][:])

        def factors_of_g():
            nc.scalar.activation(out=g_over_t[:], in_=g_sb[:], func=ACT.Copy, scale=1.0 / T)
            nc.scalar.activation(out=g_abs[:], in_=g_sb[:], func=ACT.Abs)

        def widths():
            nc.vector.tensor_tensor(out=width[:], in0=g_abs[:], in1=tau_sb[:], op=ALU.mult)

        def spans():
            nc.scalar.activation(out=span_down[:], in_=width[:], func=ACT.Copy, scale=-2.0)

        cross_ps, low_ps, out_ps = {}, {}, {}

        def cross_pass(s, t, lo, hi, q, i=None):
            if i is not None:
                cross_ps[s, t, lo] = bank(i, "ps_cross")[:, : hi - lo]
            part = slice(y_word(q, lo), y_word(q, lo) + hi - lo)
            nc.tensor.matmul_mx(
                out=cross_ps[s, t, lo],
                lhsT=x_code[q, s][:, 128 * t : 128 * t + 128].bitcast(FP8X4),
                lhsT_scale=x_sc[q, s][:, 128 * t : 128 * t + 128],
                rhs=y_code[:, part].bitcast(FP8X4),
                rhs_scale=y_sc[:, part],
                start=(i is not None),
                stop=(i is None),
            )

        def cross(s, t, lo, hi, i):
            cross_pass(s, t, lo, hi, 0, i)
            cross_pass(s, t, lo, hi, 1)

        def lift(s, t, lo, hi):
            nc.scalar.activation(
                out=upper[s, t][:, lo:hi], in_=cross_ps[s, t, lo], func=ACT.Identity, scale=of_slot(g_over_t, s, t), bias=of_slot(width, s, t)
            )

        def low_rank(s, slots, lo, hi, i):
            ps = bank(i, "ps_low")
            for n, t in enumerate(slots):
                low_ps[s, t, lo] = ps[:, (hi - lo) * n : (hi - lo) * (n + 1)]
                nc.tensor.matmul(low_ps[s, t, lo], l_t[:, 4 * s + t, :], m_sb[lo // BANK][:, lo % BANK : lo % BANK + hi - lo], start=True, stop=True)

        def cap(s, t, lo, hi):
            nc.vector.scalar_tensor_tensor(
                out=capped[s][:, t, lo:hi], in0=low_ps[s, t, lo], scalar=of_slot(g_sb, s, t), in1=upper[s, t][:, lo:hi], op0=ALU.mult, op1=ALU.min
            )

        def lower(s, slots, lo, hi, shift):
            for t in slots:
                shift(lowered[s][:, t, lo:hi], upper[s, t][:, lo:hi], of_slot(span_down, s, t))

        def floor(s, slots, lo, hi):
            part = (slice(None), slice(slots[0], slots[-1] + 1), slice(lo, hi))
            nc.vector.tensor_tensor(out=floored[s][part], in0=capped[s][part], in1=lowered[s][part], op=ALU.max)

        def floor_by_slot(s, t, lo, hi):
            nc.vector.scalar_tensor_tensor(
                out=floored[s][:, t, lo:hi], in0=upper[s, t][:, lo:hi], scalar=of_slot(span_down, s, t), in1=capped[s][:, t, lo:hi], op0=ALU.add, op1=ALU.max
            )

        def laid(s, lo, hi, run):
            return sig_words(s, lo, hi).rearrange("p (c i t) -> p c t i", i=run, t=4)

        def by_slot(tile, lo, hi, run):
            return tile[:, :, lo:hi].rearrange("p t (c i) -> p c t i", i=run)

        def floor_and_lay(s, lo, hi):
            nc.vector.tensor_tensor(out=laid(s, lo, hi, 4), in0=by_slot(capped[s], lo, hi, 4), in1=by_slot(lowered[s], lo, hi, 4), op=ALU.max)

        def sig_lay(s, lo, hi, copy):
            run = 1 if copy is gpsimd_copy else 4
            copy(out=laid(s, lo, hi, run), in_=by_slot(floored[s], lo, hi, run))

        def sig_pair(s, lo, hi, i):
            n = hi - lo
            pair_ps[s, lo] = bank(i, "ps_pair", BF16, 4 * n)
            for u in range(2):
                nc.tensor.matmul(
                    pair_ps[s, lo][:, 2 * n * u : 2 * n * (u + 1)].rearrange("p (c e) -> p e c", e=2),
                    ident[:],
                    floored[s][:, 2 * u : 2 * u + 2, lo:hi],
                    start=True,
                    stop=True,
                )

        def sig_fetch(s, lo, hi, copy=scalar_copy):
            copy(
                out=sig_words(s, lo, hi).bitcast(F32).rearrange("p (c u) -> p c u", u=2),
                in_=pair_ps[s, lo][:].bitcast(F32).rearrange("p (u c) -> p c u", u=2),
            )

        def sig_quant(s, lo, hi, groups=1):
            quantise(sig_code, sig_sc, sig_laid, sig_word(s, lo), sig_word(s, lo) + groups * (hi - lo))

        def exposure(lo, hi, s, blocks, i=None):
            n = hi - lo
            if i is not None:
                out_ps[lo, blocks[0]] = bank(i, "ps_out")
            for k, b in enumerate(blocks):
                nc.tensor.matmul_mx(
                    out=out_ps[lo, blocks[0]][:, n * k : n * (k + 1)],
                    lhsT=w_code[:, s, 256 * b : 256 * b + 256].bitcast(FP4X4),
                    lhsT_scale=w_sc[:, s, 128 * b : 128 * b + 128],
                    rhs=sig_code[:, sig_word(s, lo) : sig_word(s, lo) + n].bitcast(FP8X4),
                    rhs_scale=sig_sc[:, sig_word(s, lo) : sig_word(s, lo) + n],
                    start=(i is not None and k == 0),
                    stop=(i is None and k == len(blocks) - 1),
                )

        def store(lo, hi, blocks, copy, queue=nc.sync):
            n = len(blocks) * (hi - lo)
            staged = keep.tile([128, n], F32, name=f"staged_{lo}_{blocks[0]}")
            copy(out=staged[:], in_=out_ps[lo, blocks[0]][:, :n])
            queue.dma_start(
                out=out[128 * blocks[0] : 128 * (blocks[-1] + 1), lo:hi].rearrange("(b p) n -> p b n", p=128),
                in_=staged[:].rearrange("p (b n) -> p b n", b=len(blocks)),
            )

        load_y_scale()
        load_y(0)
        load_x(0, 0)
        load_y(1)
        load_x(1, 0, slice(0, 2))
        load_x(1, 0, slice(2, 4))
        load_l()
        load_by_slot(g_sb, g, nc.sync)
        load_by_slot(tau_sb, tau, nc.sync)
        load_x(0, 1)
        load_y(2)
        load_m(0)
        load_x(1, 1)
        load_m(1)
        load_w()
        make_spreader()
        make_identity(nc, ident[:])
        spread_y_scale(7)
        warm_up(6)

        RING, LOW = (4, 5, 6, 7), (3, 0, 1, 2)
        y_lay(0, range(5))
        y_widen(0, 5)
        y_widen(0, 6)
        y_finish(0, 5)
        x_pair(0, 0, 128, 384, 0)
        x_pair(0, 0, 384, 512, 1)
        x_lay_by_line(0, 0, 0, 128)
        y_widen(0, 7)
        x_fetch(0, 0, 128, 384, scalar_copy)
        x_fetch(0, 0, 384, 512, scalar_copy)
        y_quant(0, 0)
        y_finish(0, 6)
        y_lay(1, range(4))
        y_finish(0, 7)
        x_quant(0, 0)
        x_pair(1, 0, 256, 512, 2)
        turn_l(LOW[0])
        for t in SLOTS:
            cross_pass(0, t, 0, 512, 0, RING[t])
        x_lay_by_line(1, 0, 0, 256)
        x_fetch(1, 0, 256, 512, scalar_copy)
        factors_of_g()
        y_quant(1, 0, halves=2)
        x_quant(1, 0)
        widths()
        fetch_l()
        x_lay(0, 1, 0, 256, vector_copy)
        x_lay_by_line(0, 1, 256, 384)
        x_pair(0, 1, 384, 512, 2)
        x_fetch(0, 1, 384, 512, scalar_copy)
        spans()
        y_lay(1, (4,))
        LOW = (0, 1, 2, 3)
        cross_pass(0, 0, 0, 512, 1)
        for t in (1, 2, 3):
            cross_pass(0, t, 0, 512, 1)
            low_rank(0, (t - 1,), 0, 512, LOW[t - 1])
        lift(0, 0, 0, 512)
        x_pair(1, 1, 352, 512, RING[0])
        low_rank(0, (3,), 0, 512, LOW[3])
        for t in (1, 2, 3):
            lift(0, t, 0, 512)
        x_quant(0, 1)
        y_lay(1, (5,))
        x_lay_in_order(1, 1, 0, 352)
        for t in SLOTS:
            cap(0, t, 0, 512)
        x_fetch(1, 1, 352, 512, scalar_copy)
        lower(0, (0, 1, 2), 0, 512, scalar_shift)
        lower(0, (3,), 0, 256, scalar_shift)
        for t in (1, 2, 3):
            cross_pass(1, t, 0, 512, 0, RING[t])
        cross_pass(1, 0, 0, 512, 0, RING[0])
        x_quant(1, 1)
        y_lay(1, (6, 7))
        for t in SLOTS:
            cross_pass(1, t, 0, 512, 1)
            low_rank(1, (t,), 0, 512, LOW[t])
            lift(1, t, 0, 512)
        floor_by_slot(0, 3, 256, 512)
        floor(0, (0, 1, 2), 256, 512)
        floor(0, SLOTS, 0, 256)
        y_quant(1, 1)
        sig_lay(0, 0, 384, gpsimd_copy)
        for t in SLOTS:
            cap(1, t, 0, 512)
        lower(1, (0, 1, 2), 0, 512, scalar_shift)
        for t in SLOTS:
            cross(0, t, 512, J, RING[t])
            lift(0, t, 512, J)
            low_rank(0, (t,), 512, J, LOW[t])
        for t in SLOTS:
            cross(1, t, 512, J, RING[t])
            lift(1, t, 512, J)
        sig_lay(0, 384, 512, vector_copy)
        floor_by_slot(1, 3, 0, 512)
        floor(1, (0, 1, 2), 0, 512)
        sig_quant(0, 0, 512)
        sig_lay(1, 0, 512, gpsimd_copy)
        lower(0, (0,), 512, 768, gpsimd_shift)
        for t in SLOTS:
            cap(0, t, 512, J)
        low_rank(1, (0, 1), 512, 768, LOW[0])
        low_rank(1, (2, 3), 512, 768, LOW[1])
        low_rank(1, (0, 1), 768, J, LOW[2])
        low_rank(1, (2, 3), 768, J, LOW[3])
        for t in SLOTS:
            cap(1, t, 512, 768)
        for b in (0, 1):
            exposure(0, 512, 0, (b,), RING[b])
        sig_quant(1, 0, 512)
        for b in (0, 1):
            exposure(0, 512, 1, (b,))
        lower(0, (1, 2, 3), 512, 768, scalar_shift)
        lower(1, (0, 1, 2), 512, 768, scalar_shift)
        floor(0, SLOTS, 512, 768)
        sig_pair(0, 512, 768, RING[2])
        floor_by_slot(1, 3, 512, 768)
        floor(1, (0, 1, 2), 512, 768)
        sig_lay(1, 512, 768, gpsimd_copy)
        for t in SLOTS:
            cap(1, t, 768, J)
        for b in (2, 3):
            exposure(0, 512, 0, (b,), LOW[b])
            exposure(0, 512, 1, (b,))
        lower(0, SLOTS, 768, J, scalar_shift)
        store(0, 512, (0,), scalar_copy)
        store(0, 512, (1,), vector_copy)
        lower(1, (0,), 768, J, scalar_shift)
        sig_fetch(0, 512, 768)
        lower(1, (1, 2, 3), 768, J, scalar_shift)
        for b in (2, 3):
            store(0, 512, (b,), scalar_copy)
        floor(0, SLOTS, 896, J)
        sig_pair(0, 896, J, RING[2])
        sig_quant(0, 512, 768, groups=2)
        for blocks, i in (((0, 1), LOW[0]), ((2, 3), LOW[1])):
            exposure(512, 768, 1, blocks, i)
            exposure(512, 768, 0, blocks)
        floor_and_lay(0, 768, 896)
        floor_and_lay(1, 768, 896)
        sig_quant(0, 768, 896)
        sig_fetch(0, 896, J)
        store(512, 768, (0, 1), scalar_copy)
        store(512, 768, (2, 3), scalar_copy)
        sig_quant(1, 768, 896)
        for blocks, i in (((0, 1), RING[3]), ((2, 3), LOW[3])):
            exposure(768, 896, 0, blocks, i)
            exposure(768, 896, 1, blocks)
            store(768, 896, blocks, scalar_copy)
        floor_and_lay(1, 896, J)
        sig_quant(0, 896, J)
        LAST = (RING[0], RING[1], RING[2], LOW[2])
        for b in ROW_BLOCKS:
            exposure(896, J, 0, (b,), LAST[b])
        sig_quant(1, 896, J)
        for b in ROW_BLOCKS:
            exposure(896, J, 1, (b,))
        for b in ROW_BLOCKS:
            store(896, J, (b,), scalar_copy if b % 2 else vector_copy)
